import numpy as np
import ml_dtypes


def mxq(x, axis, fmt="e4m3"):
    dtype, down = {"e4m3": (ml_dtypes.float8_e4m3fn, 7), "e5m2": (ml_dtypes.float8_e5m2, 14)}[fmt]
    v = np.moveaxis(np.asarray(x, np.float32).astype(ml_dtypes.bfloat16).astype(np.float64), axis, -1)
    blocks = v.reshape(v.shape[:-1] + (-1, 32))
    amax = np.abs(blocks).max(-1, keepdims=True)
    byte = np.maximum(np.where(amax > 0, np.frexp(amax)[1] - 1 + 127, 0) - down, 1)
    scale = np.exp2(byte - 127.0)
    codes = (blocks / scale).astype(np.float32).astype(dtype).astype(np.float64)
    return np.moveaxis((codes * scale).reshape(v.shape), -1, axis)


WIDE = False


def mx_kscale(k):
    if not WIDE:
        return np.ones(k)
    levels = np.array([10, -10, 5, -5, 0])
    if k % 512:
        return np.exp2(np.random.permutation(np.resize(levels, k // 32))).repeat(32)
    a = np.empty((k // 512, 16))
    for p in range(k // 512):
        a[p, :8] = np.random.permutation(np.resize(levels, 8))
        for g in range(8):
            far = levels[np.abs(levels - a[p, g]) >= 10]
            a[p, g + 8] = far[np.random.randint(len(far))]
    return np.exp2(a.ravel()).repeat(32)


def f64(x):
    return np.asarray(x).astype(np.float64)


def striped(idx):
    return np.tile(idx.reshape(-1, 16).T, (8, 1)).astype(np.uint16)


def unstriped(offs):
    return offs[:16].T.reshape(-1).astype(np.int64)


E2M1 = np.array([0.0, 0.5, 1.0, 1.5, 2.0, 3.0, 4.0, 6.0, -0.0, -0.5, -1.0, -1.5, -2.0, -3.0, -4.0, -6.0])


def pack_weight(w, fmt):
    k, n = w.shape
    w = f64(np.asarray(w, np.float32).astype(ml_dtypes.bfloat16)).reshape(k // 32, 32, n)
    amax = np.abs(w).max(1)
    if fmt == "e4m3":
        byte = np.frexp(amax)[1] - 1 + 127 - 7
    else:
        mant, ex = np.frexp(amax / 6.0)
        byte = np.where(mant > 0.5, ex, ex - 1) + 127
    byte = np.clip(np.where(amax > 0, byte, 1), 1, 254)
    scaled = (w * np.exp2(127.0 - byte)[:, None, :]).reshape(k, n).astype(np.float32)
    by_word = np.ascontiguousarray(scaled.reshape(k // 512, 128, 4, n).transpose(0, 1, 3, 2))
    if fmt == "e4m3":
        words = by_word.astype(ml_dtypes.float8_e4m3fn).view(np.uint8)
    else:
        c = by_word.astype(ml_dtypes.float4_e2m1fn).view(np.uint8) & 0xF
        words = (c[..., 0::2] | (c[..., 1::2] << 4)).reshape(k // 512, 128, 2 * n)
    return np.ascontiguousarray(words), np.ascontiguousarray(byte.astype(np.uint8).reshape(k // 512, 16, n))


def unpack_weight(words, scales, fmt):
    g, _, n = scales.shape
    words = np.ascontiguousarray(words).reshape(g, 128, n, -1)
    if fmt == "e4m3":
        vals = words.view(ml_dtypes.float8_e4m3fn).astype(np.float64)
    else:
        nib = np.empty((g, 128, n, 4), np.uint8)
        nib[..., 0::2] = words & 0xF
        nib[..., 1::2] = words >> 4
        vals = E2M1[nib]
    vals = vals * np.repeat(np.exp2(scales.astype(np.float64) - 127.0), 8, axis=1)[..., None]
    return vals.transpose(0, 1, 3, 2).reshape(g * 512, n)


def gelu(v):
    return 0.5 * v * (1.0 + np.tanh(np.sqrt(2.0 / np.pi) * (v + 0.044715 * v**3)))


K, T, S, H, T2, P, N = 1024, 4096, 1024, 1024, 2048, 1024, 512


def setup_inputs():
    n = np.random.standard_normal
    s = mx_kscale(K)[:, None]
    u = mx_kscale(H)[:, None]
    tab_words, tab_scales = pack_weight(n((K, T)) * s, "e4m3")
    w2_words, w2_scales = pack_weight(n((H, N)) / np.sqrt(H) / u, "e2m1")
    return {
        "tab_words": tab_words, "tab_scales": tab_scales,
        "offs": striped(np.random.permutation(T)[:S]),
        "w1": (n((K, H)) / np.sqrt(K) / s).astype(np.float32),
        "gain": (2.0 * np.exp(0.3 * n(H)) * u[:, 0]).astype(np.float32),
        "wgs": np.exp(0.3 * n((128, S))).astype(np.float32),
        "offs2": striped(np.random.permutation(T2)[:S]),
        "offs3": striped(np.random.permutation(T2)[:P]),
        "offs4": striped(np.random.permutation(T2)[:P]),
        "ev": (0.7 * n((H, P)) * u).astype(np.float32),
        "w2_words": w2_words, "w2_scales": w2_scales,
        "res": (0.7 * n((N, P))).astype(np.float32),
    }


def reference(tab_words, tab_scales, offs, w1, gain, wgs, offs2, offs3, offs4, ev, w2_words, w2_scales, res):
    v = unpack_weight(tab_words, tab_scales, "e4m3")[:, unstriped(offs)]
    e = mxq(f64(w1), 0, "e4m3").T @ v
    h = f64(gain)[:, None] * (1.0 / (1.0 + np.exp(-e)))
    page = np.zeros((H, T2))
    page[:, unstriped(offs2)] = np.tile(f64(wgs), (H // 128, 1)) * h
    x1 = page[:, unstriped(offs3)]
    x2 = page[:, unstriped(offs4)]
    z = np.minimum(x1, x2) + f64(ev)
    y = unpack_weight(w2_words, w2_scales, "e2m1").T @ mxq(z, 0, "e4m3")
    return y + f64(res)

@@ -1,0 +1,378 @@
+from contextlib import ExitStack
+
+import concourse.mybir as mybir
+from concourse.masks import make_identity
+
+K, T, S, H, T2, M, N = 1024, 4096, 1024, 1024, 2048, 1024, 512
+FLOPS = 2 * K * H * S + 2 * H * N * M
+
+F32 = mybir.dt.float32
+BF16 = mybir.dt.bfloat16
+I32 = mybir.dt.int32
+U32 = mybir.dt.uint32
+U16 = mybir.dt.uint16
+U8 = mybir.dt.uint8
+FP8X4 = mybir.dt.float8_e4m3fn_x4
+FP4X4 = mybir.dt.float4_e2m1fn_x4
+ALU = mybir.AluOpType
+ACT = mybir.ActivationFunctionType
+
+P = 128
+PACK = 4
+K_PASS = P * PACK
+BANK = 512
+CHUNK = 256
+STRIPE = 16
+FIN = {3: (0, 1, 2, 3), 4: (4, 5), 5: (6, 7)}
+XB = 2
+NB = 4
+
+
+def tile_list_cousin_matcher_kernel(
+    tc, tab_words, tab_scales, offs, w1, gain, wgs, offs2, offs3, offs4, ev, w2_words, w2_scales, res, out
+):
+    nc = tc.nc
+
+    with ExitStack() as ctx:
+        lists = ctx.enter_context(tc.tile_pool(name="lists", bufs=1))
+        keep = ctx.enter_context(tc.tile_pool(name="keep", bufs=1))
+        ring = ctx.enter_context(tc.tile_pool(name="ring", bufs=2))
+        psum = ctx.enter_context(tc.psum_pool(name="psum", bufs=2))
+
+        def entries(list_tile, first, count):
+            return list_tile[:, first // STRIPE : (first + count) // STRIPE]
+
+        def add_transposed(bank, first, second):
+            blocks = len(first)
+            for b in range(blocks):
+                nc.tensor.matmul(bank[:, b, :], first[b], ident[:], start=(b == 0), stop=False, is_transpose=True)
+            for b in range(blocks):
+                nc.tensor.matmul(
+                    bank[:, b, :], second[b], ident[:], start=False, stop=(b == blocks - 1), is_transpose=True
+                )
+
+        def blocks_of(ap, first, count):
+            return [ap[:, first + P * b : first + P * (b + 1)] for b in range(count)]
+
+        tab_plane = keep.tile([P, T], U8, name="tab_plane", tag="plane_then_codes", align_bytes=64)
+        nc.vector.memset(tab_plane[:].bitcast(I32), 0)
+        for q in range(4):
+            nc.gpsimd.dma_start(
+                tab_plane[32 * q : 32 * q + 8, :].bitcast(I32), tab_scales[:, 4 * q : 4 * q + 4, :].bitcast(I32)
+            )
+        ident = keep.tile([P, P], F32, name="ident")
+        make_identity(nc, ident[:])
+        gain_rows = keep.tile([P, P], F32, name="gain_rows")
+        nc.vector.memset(gain_rows[:], 0.0)
+        page = keep.tile([P, T2], F32, name="page")
+        nc.vector.memset(page[:], 0.0)
+
+        idx = lists.tile([P, S // STRIPE], U16, name="idx")
+        idx2 = lists.tile([P, S // STRIPE], U16, name="idx2")
+        idx3 = lists.tile([P, M // STRIPE], U16, name="idx3")
+        idx4 = lists.tile([P, M // STRIPE], U16, name="idx4")
+
+        def load_table(a):
+            tab = ring.tile([P, T], I32, name="tab", tag="wide")
+            nc.sync.dma_start(tab[:], tab_words[a].rearrange("p t i -> p (t i)").bitcast(I32))
+            return tab
+
+        def load_w1_plain(pair):
+            raws = []
+            for a in range(2):
+                raw = ring.tile([P, PACK, 2 * P], F32, name="w1_plain", bufs=4)
+                rows = w1[K_PASS * a : K_PASS * (a + 1), 2 * P * pair : 2 * P * (pair + 1)]
+                nc.sync.dma_start(raw[:], rows.rearrange("(p i) c -> p i c", i=PACK))
+                raws.append(raw)
+            return raws
+
+        def load_ev(s):
+            ev_rows = ring.tile([P, M], F32, name="ev_rows", bufs=4)
+            if s < PACK:
+                nc.sync.dma_start(ev_rows[:], ev[P * s : P * (s + 1), :])
+            else:
+                nc.sync.dma_start(ev_rows[:], ev[K_PASS:, :].rearrange("(p t) m -> p t m", t=PACK)[:, s - PACK, :])
+            return ev_rows
+
+        nc.sync.dma_start(idx[:], offs)
+        tabs = [load_table(0)]
+        w1_plain = [load_w1_plain(0)]
+        nc.sync.dma_start(gain_rows[0:PACK, :], gain[0:K_PASS].rearrange("(s p) -> s p", p=P))
+        tabs.append(load_table(1))
+        wgs_plain = keep.tile([P, S], F32, name="wgs_plain")
+        nc.sync.dma_start(wgs_plain[:], wgs)
+        nc.sync.dma_start(idx2[:], offs2)
+        nc.sync.dma_start(idx4[:], offs4)
+        nc.sync.dma_start(idx3[:], offs3)
+        evs = [load_ev(0)]
+        w1_plain.append(load_w1_plain(1))
+        evs.append(load_ev(1))
+        evs.append(load_ev(2))
+        evs.append(load_ev(3))
+
+        w1_woven_raw = []
+        for a in range(2):
+            raw = ring.tile([P, PACK, K_PASS], F32, name="w1_woven_raw", tag="half_wide")
+            rows = w1[K_PASS * a : K_PASS * (a + 1), K_PASS:]
+            nc.sync.dma_start(raw[:], rows.rearrange("(p i) c -> p i c", i=PACK))
+            w1_woven_raw.append(raw)
+        wgs_woven = keep.tile([P, PACK, S], F32, name="wgs_woven")
+        for q in range(4):
+            nc.sync.dma_start(wgs_woven[32 * q : 32 * (q + 1), :, :], wgs.rearrange("(p t) j -> p t j", t=PACK))
+        gain_woven = keep.tile([P, PACK], F32, name="gain_woven")
+        nc.sync.dma_start(gain_woven[:], gain[K_PASS:].rearrange("(p t) -> p t", t=PACK))
+        w2_codes = keep.tile([P, 2, 2 * N], U8, name="w2_codes", align_bytes=64)
+        nc.sync.dma_start(w2_codes[:].bitcast(I32), w2_words.rearrange("a p c -> p a c").bitcast(I32))
+        w2_plane = keep.tile([P, 2, N], U8, name="w2_plane", align_bytes=64)
+        nc.vector.memset(w2_plane[:].rearrange("p a c -> p (a c)").bitcast(I32), 0)
+        for q in range(4):
+            nc.sync.dma_start(
+                w2_plane[32 * q : 32 * q + 4, :, :].bitcast(I32),
+                w2_scales[:, 4 * q : 4 * q + 4, :].rearrange("a r c -> r a c").bitcast(I32),
+            )
+
+        v_plane = keep.tile([P, S], U8, name="v_plane", align_bytes=64)
+        nc.vector.tensor_copy(v_plane[:], tab_plane[:].indirect(idx[:]))
+        v_codes = [
+            keep.tile([P, S], U32, name="v_codes0", align_bytes=64),
+            keep.tile([P, S], U32, name="v_codes1", tag="plane_then_codes", align_bytes=64),
+        ]
+        nc.vector.tensor_copy(v_codes[0][:], tabs[0][:].bitcast(U32).indirect(idx[:]))
+
+        gain_bank = psum.tile([P, BANK], F32, name="gain_bank", tag="work", bufs=NB)
+        nc.tensor.transpose(gain_bank[:, 0:P], gain_rows[:], ident[:])
+        gain_plain = keep.tile([P, PACK], F32, name="gain_plain")
+        nc.scalar.copy(gain_plain[:], gain_bank[:, 0:PACK])
+
+
+        w1_codes = keep.tile([P, H // P, 2 * P], U32, name="w1_codes", align_bytes=64)
+        w1_plane = keep.tile([P, H // P, 2 * P], U8, name="w1_plane", align_bytes=64)
+
+        def quantise_w1(first, rounded):
+            count = rounded.shape[1]
+            nc.vector.quantize_mx(
+                out=w1_codes[:, first : first + count, :].rearrange("p s c -> p (s c)").bitcast(FP8X4),
+                scales=w1_plane[:, first : first + count, :].rearrange("p s c -> p (s c)"),
+                in_=rounded[:].rearrange("p s a c i -> p (s a c i)"),
+            )
+
+        def prepare_plain(pair):
+            rounded = keep.tile([P, 2, 2, P, PACK], BF16, name="w1_rounded", tag="turnstile", align_bytes=64)
+            for a in range(2):
+                nc.scalar.copy(rounded[:, :, a, :, :], w1_plain[pair][a][:].rearrange("p i (s c) -> p s c i", s=2))
+            quantise_w1(2 * pair, rounded)
+
+        def activations(s):
+            codes, plane = w1_codes[:, s, :], w1_plane[:, s, :]
+            if s < PACK:
+                weights, scale = wgs_plain[:], gain_plain[:, s : s + 1]
+            else:
+                weights, scale = wgs_woven[:, s - PACK, :], gain_woven[:, s - PACK : s - PACK + 1]
+            if s == 0:
+                first = keep.tile([P, BANK], F32, name="factor_first", tag="turnstile", align_bytes=64)
+                nc.scalar.activation(first[:], weights[:, 0:BANK], ACT.Copy, scale=scale)
+                second = keep.tile([P, BANK], F32, name="factor", tag="factor0")
+                nc.scalar.activation(second[:], weights[:, BANK:], ACT.Copy, scale=scale)
+                factor = [first[:], second[:]]
+            else:
+                whole = keep.tile([P, S], F32, name="factor", tag="factor%d" % (s % 2))
+                nc.scalar.activation(whole[:], weights, ACT.Copy, scale=scale)
+                factor = [whole[:]]
+            sig = keep.tile([P, S], F32, name="sig", tag="sig%d" % (s % 2), align_bytes=64)
+            for j0 in range(0, S, BANK):
+                cols = slice(j0, j0 + BANK)
+                e_bank = psum.tile([P, BANK], F32, name="e_bank", tag="work", bufs=NB)
+                for a in range(2):
+                    nc.tensor.matmul_mx(
+                        out=e_bank[:],
+                        lhsT=codes[:, P * a : P * (a + 1)].bitcast(FP8X4),
+                        lhsT_scale=plane[:, P * a : P * (a + 1)],
+                        rhs=v_codes[a][:, cols].bitcast(FP8X4),
+                        rhs_scale=v_plane[4 * a :, cols],
+                        start=(a == 0),
+                        stop=(a == 1),
+                    )
+                nc.scalar.activation(sig[:, cols], e_bank[:], ACT.Sigmoid)
+            return sig, factor
+
+        prepare_plain(0)
+        for j0 in range(0, S, BANK):
+            nc.vector.tensor_copy(
+                v_codes[1][:, j0 : j0 + BANK], tabs[1][:].bitcast(U32).indirect(entries(idx, j0, BANK))
+            )
+        ready = [activations(0)]
+
+        excess_t = ring.tile([P, M // P, PACK, P], F32, name="excess_t", tag="wide")
+        base_t = ring.tile([P, M // P, PACK, P], F32, name="base_t", tag="wide")
+        z_rounded = [
+            [ring.tile([P, CHUNK, PACK], BF16, name="z_rounded", bufs=8, align_bytes=64) for c in range(M // CHUNK)]
+            for a in range(2)
+        ]
+
+        def fetch_and_turn(s, m0):
+            if m0 == BANK:
+                neg_x2 = keep.tile([P, BANK], F32, name="neg_x2", tag="factor%d" % (s % 2))
+            elif s == 0:
+                neg_x2 = keep.tile([P, BANK], F32, name="neg_x2", tag="turnstile", align_bytes=64)
+            else:
+                neg_x2 = ring.tile([P, BANK], F32, name="neg_x2", bufs=XB)
+            nc.vector.tensor_scalar(neg_x2[:], page[:].indirect(entries(idx4, m0, BANK)), -1.0, 0.0, ALU.mult, ALU.add)
+            if m0 == BANK:
+                x1 = keep.tile([P, BANK], F32, name="x1", tag="sig%d" % (s % 2), align_bytes=64)
+            elif s in (0, 2):
+                x1 = keep.tile([P, BANK], F32, name="x1", tag="woven", align_bytes=64)
+            else:
+                x1 = ring.tile([P, BANK], F32, name="x1", bufs=XB)
+            nc.vector.tensor_copy(x1[:], page[:].indirect(entries(idx3, m0, BANK)))
+            diff = psum.tile([P, PACK, P], F32, name="diff", tag="work", bufs=NB)
+            add_transposed(diff, blocks_of(neg_x2, 0, PACK), blocks_of(x1, 0, PACK))
+            base = psum.tile([P, PACK, P], F32, name="base", tag="work", bufs=NB)
+            add_transposed(base, blocks_of(evs[s], m0, PACK), blocks_of(x1, 0, PACK))
+            return diff, base
+
+        def combine_plain(s, m0):
+            diff, base = fetch_and_turn(s, m0)
+            where = (slice(None), slice(m0 // P, m0 // P + PACK), slice(None), slice(32 * s, 32 * (s + 1)))
+            pattern = "m b (q t) -> m b t q"
+            nc.scalar.activation(excess_t[where], diff[:].rearrange(pattern, t=PACK), ACT.Relu)
+            nc.scalar.activation(base_t[where], base[:].rearrange(pattern, t=PACK), ACT.Copy, scale=-1.0)
+
+        def finish_plain(mb):
+            neg_z = psum.tile([P, PACK, P], F32, name="neg_z", tag="work", bufs=NB)
+            add_transposed(neg_z, [excess_t[:, mb, t, :] for t in range(PACK)], [base_t[:, mb, t, :] for t in range(PACK)])
+            c, part = divmod(mb, CHUNK // P)
+            nc.scalar.activation(
+                z_rounded[0][c][:, P * part : P * (part + 1), :],
+                neg_z[:].rearrange("p t m -> p m t"),
+                ACT.Copy,
+                scale=-1.0,
+            )
+
+        def combine_woven(s, m0):
+            diff, base = fetch_and_turn(s, m0)
+            excess = ring.tile([P, BANK], F32, name="excess")
+            nc.scalar.activation(excess[:], diff[:].rearrange("m b p -> m (b p)"), ACT.Relu)
+            neg_base = ring.tile([P, BANK], F32, name="neg_base", align_bytes=64)
+            nc.scalar.activation(neg_base[:], base[:].rearrange("m b p -> m (b p)"), ACT.Copy, scale=-1.0)
+            return excess, neg_base
+
+        def finish_woven(s, m0, excess, neg_base):
+            neg_z = psum.tile([P, PACK, P], F32, name="neg_z", tag="work", bufs=NB)
+            add_transposed(neg_z, blocks_of(excess, 0, PACK), blocks_of(neg_base, 0, PACK))
+            flat = neg_z[:].rearrange("p b m -> p (b m)")
+            for c0 in range(0, BANK, CHUNK):
+                nc.scalar.activation(
+                    z_rounded[1][(m0 + c0) // CHUNK][:, :, s - PACK], flat[:, c0 : c0 + CHUNK], ACT.Copy, scale=-1.0
+                )
+
+        def combine_direct(s, c):
+            m0 = CHUNK * c
+            x1 = ring.tile([P, CHUNK], F32, name="x1", bufs=XB)
+            nc.vector.tensor_copy(x1[:], page[:].indirect(entries(idx3, m0, CHUNK)))
+            x2 = ring.tile([P, CHUNK], F32, name="x2", tag="neg_x2", bufs=XB)
+            nc.vector.tensor_copy(x2[:], page[:].indirect(entries(idx4, m0, CHUNK)))
+            least = ring.tile([P, CHUNK], F32, name="least", tag="excess")
+            nc.vector.tensor_tensor(least[:], x1[:], x2[:], ALU.min)
+            z = ring.tile([P, CHUNK], F32, name="z", tag="w1_plain", bufs=4)
+            nc.vector.tensor_tensor(z[:], least[:], evs[s][:, m0 : m0 + CHUNK], ALU.add)
+            nc.scalar.copy(z_rounded[1][c][:, :, s - PACK], z[:])
+
+        z_mx = [[], []]
+
+        def quantise_z(a, c):
+            if a == 0:
+                codes = z_first[c // 2][:, CHUNK * (c % 2) : CHUNK * (c % 2 + 1)]
+            else:
+                codes = ring.tile([P, CHUNK], U32, name="z_codes", bufs=4, align_bytes=64)
+            plane = ring.tile([P, CHUNK], U8, name="z_plane", bufs=8, align_bytes=64)
+            nc.vector.quantize_mx(
+                out=codes[:].bitcast(FP8X4), scales=plane[:], in_=z_rounded[a][c][:].rearrange("p m t -> p (m t)")
+            )
+            z_mx[a].append((codes, plane))
+
+        res_rows = []
+
+        def multiply(y, a, c, pair):
+            codes, plane = z_mx[a][c]
+            steps = [(b, m0) for b in range(2) for m0 in range(0, CHUNK, P)]
+            for b, m0 in steps:
+                n0 = P * (2 * pair + b)
+                nc.tensor.matmul_mx(
+                    out=y[:, b, m0 : m0 + P],
+                    lhsT=w2_codes[:, a, 2 * n0 : 2 * (n0 + P)].bitcast(FP4X4),
+                    lhsT_scale=w2_plane[:, a, n0 : n0 + P],
+                    rhs=codes[:, m0 : m0 + P].bitcast(FP8X4),
+                    rhs_scale=plane[:, m0 : m0 + P],
+                    start=(a == 0 and (b, m0) == steps[0]),
+                    stop=(a == 1 and (b, m0) == steps[-1]),
+                )
+
+        def open_scores(c):
+            banks = []
+            for pair in range(2):
+                y = psum.tile([P, 2, CHUNK], F32, name="y", tag="y", bufs=8 - NB)
+                multiply(y, 0, c, pair)
+                banks.append(y)
+            return banks
+
+        def close_scores(c):
+            cols = slice(CHUNK * c, CHUNK * (c + 1))
+            for pair in range(2):
+                y = score_banks[c][pair]
+                multiply(y, 1, c, pair)
+                result = ring.tile([P, 2, CHUNK], F32, name="result", bufs=4)
+                nc.vector.tensor_tensor(result[:], y[:], res_rows[pair][:, :, cols], ALU.add)
+                rows = out[2 * P * pair : 2 * P * (pair + 1), cols]
+                nc.sync.dma_start(rows.rearrange("(b p) m -> p b m", p=P), result[:])
+
+        slices = H // P
+        for s in range(slices):
+            sig, factor = ready[s]
+            piece = BANK if s == 0 else S
+            for j0 in range(0, S, piece):
+                cols = slice(j0, j0 + piece)
+                nc.vector.tensor_tensor(
+                    page[:].indirect(entries(idx2, j0, piece)), sig[:, cols], factor[j0 // piece], ALU.mult
+                )
+            if s == 0:
+                ready.append(activations(1))
+                prepare_plain(1)
+            if s < slices - 1:
+                turned = [(combine_plain if s < PACK else combine_woven)(s, m0) for m0 in range(0, M, BANK)]
+                if s + 2 < slices:
+                    ready.append(activations(s + 2))
+                if s >= PACK:
+                    for half in range(2):
+                        finish_woven(s, BANK * half, *turned[half])
+                for mb in FIN.get(s, ()):
+                    finish_plain(mb)
+                if s + PACK < slices:
+                    evs.append(load_ev(s + PACK))
+            if s == 0:
+                w1_woven = keep.tile([P, PACK, 2, P, PACK], BF16, name="w1_woven", tag="woven", align_bytes=64)
+                for a in range(2):
+                    nc.scalar.copy(
+                        w1_woven[:, :, a, :, :].rearrange("p t c i -> p c i t"),
+                        w1_woven_raw[a][:].rearrange("p i (c t) -> p c i t", t=PACK),
+                    )
+                quantise_w1(PACK, w1_woven)
+                for pair in range(2):
+                    rows = ring.tile([P, 2, M], F32, name="res_rows", tag="half_wide")
+                    source = res[2 * P * pair : 2 * P * (pair + 1), :]
+                    nc.sync.dma_start(rows[:], source.rearrange("(b p) m -> p b m", p=P))
+                    res_rows.append(rows)
+
+        chunks = M // CHUNK
+        z_first = [ring.tile([P, BANK], U32, name="z_first", tag="neg_base", align_bytes=64) for half in range(2)]
+        for c in range(chunks):
+            quantise_z(0, c)
+        score_banks = [open_scores(0)]
+        for step in range(chunks + 2):
+            if step < chunks:
+                combine_direct(slices - 1, step)
+            if step + 1 < chunks:
+                score_banks.append(open_scores(step + 1))
+            if 1 <= step <= chunks:
+                quantise_z(1, step - 1)
+            if step >= 2:
+                close_scores(step - 2)

@@ -23,9 +23,9 @@ K_PASS = P * PACK
 BANK = 512
 CHUNK = 256
 STRIPE = 16
-FIN = {3: (0, 1, 2, 3), 4: (4, 5), 5: (6, 7)}
+FIN = {3: (0, 1), 4: (2, 3), 5: (4, 5), 6: (6, 7)}
 XB = 2
-NB = 4
+NB = 6
 
 
 def tile_list_cousin_matcher_kernel(
@@ -57,11 +57,13 @@ def tile_list_cousin_matcher_kernel(
         tab_plane = keep.tile([P, T], U8, name="tab_plane", tag="plane_then_codes", align_bytes=64)
         nc.vector.memset(tab_plane[:].bitcast(I32), 0)
         for q in range(4):
-            nc.gpsimd.dma_start(
+            nc.sync.dma_start(
                 tab_plane[32 * q : 32 * q + 8, :].bitcast(I32), tab_scales[:, 4 * q : 4 * q + 4, :].bitcast(I32)
             )
         ident = keep.tile([P, P], F32, name="ident")
         make_identity(nc, ident[:])
+        ident_bf16 = keep.tile([P, P], BF16, name="ident_bf16")
+        make_identity(nc, ident_bf16[:])
         gain_rows = keep.tile([P, P], F32, name="gain_rows")
         nc.vector.memset(gain_rows[:], 0.0)
         page = keep.tile([P, T2], F32, name="page")
@@ -168,17 +170,16 @@ def tile_list_cousin_matcher_kernel(
                 weights, scale = wgs_plain[:], gain_plain[:, s : s + 1]
             else:
                 weights, scale = wgs_woven[:, s - PACK, :], gain_woven[:, s - PACK : s - PACK + 1]
+            both = keep.tile([P, 2, S], F32, name="both", tag="held%d" % (s % 2))
+            sig = both[:, 0, :]
             if s == 0:
                 first = keep.tile([P, BANK], F32, name="factor_first", tag="turnstile", align_bytes=64)
                 nc.scalar.activation(first[:], weights[:, 0:BANK], ACT.Copy, scale=scale)
-                second = keep.tile([P, BANK], F32, name="factor", tag="factor0")
-                nc.scalar.activation(second[:], weights[:, BANK:], ACT.Copy, scale=scale)
-                factor = [first[:], second[:]]
+                nc.scalar.activation(both[:, 1, BANK:], weights[:, BANK:], ACT.Copy, scale=scale)
+                factor = [first[:], both[:, 1, BANK:]]
             else:
-                whole = keep.tile([P, S], F32, name="factor", tag="factor%d" % (s % 2))
-                nc.scalar.activation(whole[:], weights, ACT.Copy, scale=scale)
-                factor = [whole[:]]
-            sig = keep.tile([P, S], F32, name="sig", tag="sig%d" % (s % 2), align_bytes=64)
+                nc.scalar.activation(both[:, 1, :], weights, ACT.Copy, scale=scale)
+                factor = [both[:, 1, :]]
             for j0 in range(0, S, BANK):
                 cols = slice(j0, j0 + BANK)
                 e_bank = psum.tile([P, BANK], F32, name="e_bank", tag="work", bufs=NB)
@@ -204,21 +205,22 @@ def tile_list_cousin_matcher_kernel(
 
         excess_t = ring.tile([P, M // P, PACK, P], F32, name="excess_t", tag="wide")
         base_t = ring.tile([P, M // P, PACK, P], F32, name="base_t", tag="wide")
-        z_rounded = [
-            [ring.tile([P, CHUNK, PACK], BF16, name="z_rounded", bufs=8, align_bytes=64) for c in range(M // CHUNK)]
-            for a in range(2)
-        ]
+        z_plain = [keep.tile([P, BANK, PACK], BF16, name="z_plain%d" % half, align_bytes=64) for half in range(2)]
+        z_woven = [ring.tile([P, CHUNK, PACK], BF16, name="z_woven", bufs=4, align_bytes=64) for c in range(M // CHUNK)]
+
+        z_rows = [keep.tile([P, PACK, BANK], BF16, name="z_rows%d" % half) for half in range(2)]
 
         def fetch_and_turn(s, m0):
             if m0 == BANK:
-                neg_x2 = keep.tile([P, BANK], F32, name="neg_x2", tag="factor%d" % (s % 2))
+                both = keep.tile([P, 2, BANK], F32, name="both", tag="held%d" % (s % 2))
+                neg_x2 = both[:, 0, :]
             elif s == 0:
                 neg_x2 = keep.tile([P, BANK], F32, name="neg_x2", tag="turnstile", align_bytes=64)
             else:
                 neg_x2 = ring.tile([P, BANK], F32, name="neg_x2", bufs=XB)
             nc.vector.tensor_scalar(neg_x2[:], page[:].indirect(entries(idx4, m0, BANK)), -1.0, 0.0, ALU.mult, ALU.add)
             if m0 == BANK:
-                x1 = keep.tile([P, BANK], F32, name="x1", tag="sig%d" % (s % 2), align_bytes=64)
+                x1 = both[:, 1, :]
             elif s in (0, 2):
                 x1 = keep.tile([P, BANK], F32, name="x1", tag="woven", align_bytes=64)
             else:
@@ -240,55 +242,68 @@ def tile_list_cousin_matcher_kernel(
         def finish_plain(mb):
             neg_z = psum.tile([P, PACK, P], F32, name="neg_z", tag="work", bufs=NB)
             add_transposed(neg_z, [excess_t[:, mb, t, :] for t in range(PACK)], [base_t[:, mb, t, :] for t in range(PACK)])
-            c, part = divmod(mb, CHUNK // P)
+            half, part = divmod(mb, PACK)
             nc.scalar.activation(
-                z_rounded[0][c][:, P * part : P * (part + 1), :],
+                z_plain[half][:, P * part : P * (part + 1), :],
                 neg_z[:].rearrange("p t m -> p m t"),
                 ACT.Copy,
                 scale=-1.0,
             )
 
         def combine_woven(s, m0):
-            diff, base = fetch_and_turn(s, m0)
-            excess = ring.tile([P, BANK], F32, name="excess")
-            nc.scalar.activation(excess[:], diff[:].rearrange("m b p -> m (b p)"), ACT.Relu)
-            neg_base = ring.tile([P, BANK], F32, name="neg_base", align_bytes=64)
-            nc.scalar.activation(neg_base[:], base[:].rearrange("m b p -> m (b p)"), ACT.Copy, scale=-1.0)
-            return excess, neg_base
+            if m0 == BANK:
+                both = keep.tile([P, 2, BANK], F32, name="both", tag="held%d" % (s % 2))
+                x2, x1 = both[:, 0, :], both[:, 1, :]
+            else:
+                x2 = ring.tile([P, BANK], F32, name="neg_x2", bufs=XB)
+                x1 = ring.tile([P, BANK], F32, name="x1", bufs=XB)
+            nc.vector.tensor_copy(x2[:], page[:].indirect(entries(idx4, m0, BANK)))
+            nc.vector.tensor_copy(x1[:], page[:].indirect(entries(idx3, m0, BANK)))
+            nc.vector.tensor_tensor(x1[:], x1[:], x2[:], ALU.min)
+            z_t = psum.tile([P, PACK, P], F32, name="z_t", tag="work", bufs=NB)
+            add_transposed(z_t, blocks_of(evs[s], m0, PACK), blocks_of(x1, 0, PACK))
+            turned = ring.tile([P, BANK], BF16, name="turned", align_bytes=64)
+            nc.scalar.copy(turned[:], z_t[:].rearrange("m b p -> m (b p)"))
+            return turned
 
-        def finish_woven(s, m0, excess, neg_base):
-            neg_z = psum.tile([P, PACK, P], F32, name="neg_z", tag="work", bufs=NB)
-            add_transposed(neg_z, blocks_of(excess, 0, PACK), blocks_of(neg_base, 0, PACK))
-            flat = neg_z[:].rearrange("p b m -> p (b m)")
-            for c0 in range(0, BANK, CHUNK):
-                nc.scalar.activation(
-                    z_rounded[1][(m0 + c0) // CHUNK][:, :, s - PACK], flat[:, c0 : c0 + CHUNK], ACT.Copy, scale=-1.0
-                )
+        def finish_woven(s, m0, turned):
+            z_bank = psum.tile([P, BANK], BF16, name="z_bank", tag="y" if s == 6 else "work", bufs=8 - NB if s == 6 else NB)
+            for b in range(PACK):
+                nc.tensor.transpose(z_bank[:, P * b : P * (b + 1)], turned[:, P * b : P * (b + 1)], ident_bf16[:])
+            nc.scalar.copy(z_rows[m0 // BANK][:, s - PACK, :], z_bank[:])
 
         def combine_direct(s, c):
             m0 = CHUNK * c
-            x1 = ring.tile([P, CHUNK], F32, name="x1", bufs=XB)
+            if c == 0:
+                x1 = keep.tile([P, CHUNK], F32, name="x1", tag="z_plain1", align_bytes=64)
+            else:
+                x1 = ring.tile([P, CHUNK], F32, name="x1", bufs=XB)
             nc.vector.tensor_copy(x1[:], page[:].indirect(entries(idx3, m0, CHUNK)))
-            x2 = ring.tile([P, CHUNK], F32, name="x2", tag="neg_x2", bufs=XB)
+            if c == 0:
+                x2 = keep.tile([P, CHUNK], F32, name="x2", tag="z_plain0", align_bytes=64)
+            else:
+                x2 = ring.tile([P, CHUNK], F32, name="x2", tag="neg_x2", bufs=XB)
             nc.vector.tensor_copy(x2[:], page[:].indirect(entries(idx4, m0, CHUNK)))
-            least = ring.tile([P, CHUNK], F32, name="least", tag="excess")
+            least = ring.tile([P, CHUNK], F32, name="least")
             nc.vector.tensor_tensor(least[:], x1[:], x2[:], ALU.min)
-            z = ring.tile([P, CHUNK], F32, name="z", tag="w1_plain", bufs=4)
-            nc.vector.tensor_tensor(z[:], least[:], evs[s][:, m0 : m0 + CHUNK], ALU.add)
-            nc.scalar.copy(z_rounded[1][c][:, :, s - PACK], z[:])
+            rows = z_rows[m0 // BANK][:, :, m0 % BANK : m0 % BANK + CHUNK]
+            nc.vector.tensor_tensor(rows[:, s - PACK, :], least[:], evs[s][:, m0 : m0 + CHUNK], ALU.add)
+            weave = nc.vector.tensor_copy if c == M // CHUNK - 1 else nc.scalar.copy
+            weave(
+                z_woven[c][:].rearrange("p (m i) t -> p m t i", i=PACK),
+                rows.rearrange("p t (m i) -> p m t i", i=PACK),
+            )
 
         z_mx = [[], []]
 
-        def quantise_z(a, c):
-            if a == 0:
-                codes = z_first[c // 2][:, CHUNK * (c % 2) : CHUNK * (c % 2 + 1)]
-            else:
-                codes = ring.tile([P, CHUNK], U32, name="z_codes", bufs=4, align_bytes=64)
-            plane = ring.tile([P, CHUNK], U8, name="z_plane", bufs=8, align_bytes=64)
+        def quantise_z(a, rounded):
+            width = rounded.shape[1]
+            codes = ring.tile([P, width], U32, name="z_codes%d" % a, bufs=M // width, align_bytes=64)
+            plane = ring.tile([P, width], U8, name="z_plane%d" % a, bufs=M // width, align_bytes=64)
             nc.vector.quantize_mx(
-                out=codes[:].bitcast(FP8X4), scales=plane[:], in_=z_rounded[a][c][:].rearrange("p m t -> p (m t)")
+                out=codes[:].bitcast(FP8X4), scales=plane[:], in_=rounded[:].rearrange("p m t -> p (m t)")
             )
-            z_mx[a].append((codes, plane))
+            z_mx[a].extend((codes[:, c0 : c0 + CHUNK], plane[:, c0 : c0 + CHUNK]) for c0 in range(0, width, CHUNK))
 
         res_rows = []
 
@@ -310,7 +325,7 @@ def tile_list_cousin_matcher_kernel(
         def open_scores(c):
             banks = []
             for pair in range(2):
-                y = psum.tile([P, 2, CHUNK], F32, name="y", tag="y", bufs=8 - NB)
+                y = psum.tile([P, 2, CHUNK], F32, name="y", tag="y" if c == 0 else "work", bufs=8 - NB if c == 0 else NB)
                 multiply(y, 0, c, pair)
                 banks.append(y)
             return banks
@@ -343,7 +358,7 @@ def tile_list_cousin_matcher_kernel(
                     ready.append(activations(s + 2))
                 if s >= PACK:
                     for half in range(2):
-                        finish_woven(s, BANK * half, *turned[half])
+                        finish_woven(s, BANK * half, turned[half])
                 for mb in FIN.get(s, ()):
                     finish_plain(mb)
                 if s + PACK < slices:
@@ -352,8 +367,8 @@ def tile_list_cousin_matcher_kernel(
                 w1_woven = keep.tile([P, PACK, 2, P, PACK], BF16, name="w1_woven", tag="woven", align_bytes=64)
                 for a in range(2):
                     nc.scalar.copy(
-                        w1_woven[:, :, a, :, :].rearrange("p t c i -> p c i t"),
-                        w1_woven_raw[a][:].rearrange("p i (c t) -> p c i t", t=PACK),
+                        w1_woven[:, :, a, :, :].rearrange("p t c i -> p c t i"),
+                        w1_woven_raw[a][:].rearrange("p i (c t) -> p c t i", t=PACK),
                     )
                 quantise_w1(PACK, w1_woven)
                 for pair in range(2):
@@ -363,9 +378,8 @@ def tile_list_cousin_matcher_kernel(
                     res_rows.append(rows)
 
         chunks = M // CHUNK
-        z_first = [ring.tile([P, BANK], U32, name="z_first", tag="neg_base", align_bytes=64) for half in range(2)]
-        for c in range(chunks):
-            quantise_z(0, c)
+        for half in range(2):
+            quantise_z(0, z_plain[half])
         score_banks = [open_scores(0)]
         for step in range(chunks + 2):
             if step < chunks:
@@ -373,6 +387,6 @@ def tile_list_cousin_matcher_kernel(
             if step + 1 < chunks:
                 score_banks.append(open_scores(step + 1))
             if 1 <= step <= chunks:
-                quantise_z(1, step - 1)
+                quantise_z(1, z_woven[step - 1])
             if step >= 2:
                 close_scores(step - 2)

@@ -23,8 +23,10 @@ K_PASS = P * PACK
 BANK = 512
 CHUNK = 256
 STRIPE = 16
-FIN = {3: (0, 1), 4: (2, 3), 5: (4, 5), 6: (6, 7)}
+FIN = {3: (4, 5), 4: (6,), 5: (7,)}
+FIN2 = {2: (0, 1, 2, 3)}
 XB = 2
+AFTER = {(0, 0): 0, (0, 512): 1, (1, 0): 3}
 NB = 6
 
 
@@ -62,12 +64,11 @@ def tile_list_cousin_matcher_kernel(
             )
         ident = keep.tile([P, P], F32, name="ident")
         make_identity(nc, ident[:])
-        ident_bf16 = keep.tile([P, P], BF16, name="ident_bf16")
-        make_identity(nc, ident_bf16[:])
         gain_rows = keep.tile([P, P], F32, name="gain_rows")
         nc.vector.memset(gain_rows[:], 0.0)
-        page = keep.tile([P, T2], F32, name="page")
-        nc.vector.memset(page[:], 0.0)
+        pages = [keep.tile([P, T2], F32, name="page%d" % n) for n in range(2)]
+        for page in pages:
+            nc.vector.memset(page[:], 0.0)
 
         idx = lists.tile([P, S // STRIPE], U16, name="idx")
         idx2 = lists.tile([P, S // STRIPE], U16, name="idx2")
@@ -102,15 +103,13 @@ def tile_list_cousin_matcher_kernel(
         nc.sync.dma_start(gain_rows[0:PACK, :], gain[0:K_PASS].rearrange("(s p) -> s p", p=P))
         tabs.append(load_table(1))
         wgs_plain = keep.tile([P, S], F32, name="wgs_plain")
-        nc.sync.dma_start(wgs_plain[:], wgs)
+        nc.sync.dma_start(wgs_plain[:, 0:BANK], wgs[:, 0:BANK])
         nc.sync.dma_start(idx2[:], offs2)
         nc.sync.dma_start(idx4[:], offs4)
         nc.sync.dma_start(idx3[:], offs3)
         evs = [load_ev(0)]
+        nc.sync.dma_start(wgs_plain[:, BANK:], wgs[:, BANK:])
         w1_plain.append(load_w1_plain(1))
-        evs.append(load_ev(1))
-        evs.append(load_ev(2))
-        evs.append(load_ev(3))
 
         w1_woven_raw = []
         for a in range(2):
@@ -118,11 +117,19 @@ def tile_list_cousin_matcher_kernel(
             rows = w1[K_PASS * a : K_PASS * (a + 1), K_PASS:]
             nc.sync.dma_start(raw[:], rows.rearrange("(p i) c -> p i c", i=PACK))
             w1_woven_raw.append(raw)
-        wgs_woven = keep.tile([P, PACK, S], F32, name="wgs_woven")
-        for q in range(4):
-            nc.sync.dma_start(wgs_woven[32 * q : 32 * (q + 1), :, :], wgs.rearrange("(p t) j -> p t j", t=PACK))
         gain_woven = keep.tile([P, PACK], F32, name="gain_woven")
         nc.sync.dma_start(gain_woven[:], gain[K_PASS:].rearrange("(p t) -> p t", t=PACK))
+
+        def load_wgs_woven(pair):
+            rows = keep.tile([P, 2, S], F32, name="wgs_woven%d" % pair)
+            source = wgs.rearrange("(p t) j -> p t j", t=PACK)[:, 2 * pair : 2 * pair + 2, :]
+            for q in range(4):
+                nc.sync.dma_start(rows[32 * q : 32 * (q + 1), :, :], source)
+            return [rows[:, 0, :], rows[:, 1, :]]
+
+        wgs_woven = load_wgs_woven(0)
+        evs.extend(load_ev(s) for s in range(1, PACK))
+        wgs_woven.extend(load_wgs_woven(1))
         w2_codes = keep.tile([P, 2, 2 * N], U8, name="w2_codes", align_bytes=64)
         nc.sync.dma_start(w2_codes[:].bitcast(I32), w2_words.rearrange("a p c -> p a c").bitcast(I32))
         w2_plane = keep.tile([P, 2, N], U8, name="w2_plane", align_bytes=64)
@@ -169,17 +176,13 @@ def tile_list_cousin_matcher_kernel(
             if s < PACK:
                 weights, scale = wgs_plain[:], gain_plain[:, s : s + 1]
             else:
-                weights, scale = wgs_woven[:, s - PACK, :], gain_woven[:, s - PACK : s - PACK + 1]
-            both = keep.tile([P, 2, S], F32, name="both", tag="held%d" % (s % 2))
+                weights, scale = wgs_woven[s - PACK], gain_woven[:, s - PACK : s - PACK + 1]
+            both = ring.tile([P, 2, S], F32, name="both")
             sig = both[:, 0, :]
             if s == 0:
                 first = keep.tile([P, BANK], F32, name="factor_first", tag="turnstile", align_bytes=64)
                 nc.scalar.activation(first[:], weights[:, 0:BANK], ACT.Copy, scale=scale)
-                nc.scalar.activation(both[:, 1, BANK:], weights[:, BANK:], ACT.Copy, scale=scale)
                 factor = [first[:], both[:, 1, BANK:]]
-            else:
-                nc.scalar.activation(both[:, 1, :], weights, ACT.Copy, scale=scale)
-                factor = [both[:, 1, :]]
             for j0 in range(0, S, BANK):
                 cols = slice(j0, j0 + BANK)
                 e_bank = psum.tile([P, BANK], F32, name="e_bank", tag="work", bufs=NB)
@@ -194,6 +197,13 @@ def tile_list_cousin_matcher_kernel(
                         stop=(a == 1),
                     )
                 nc.scalar.activation(sig[:, cols], e_bank[:], ACT.Sigmoid)
+            if s == 0:
+                nc.scalar.activation(both[:, 1, BANK:], weights[:, BANK:], ACT.Copy, scale=scale)
+            else:
+                column = keep.tile([P, 1], F32, name="column", tag="held%d" % ((s + 1) % 2))
+                nc.scalar.copy(column[:], scale)
+                nc.scalar.activation(both[:, 1, :], weights, ACT.Copy, scale=column[:])
+                factor = [both[:, 1, :]]
             return sig, factor
 
         prepare_plain(0)
@@ -203,29 +213,30 @@ def tile_list_cousin_matcher_kernel(
             )
         ready = [activations(0)]
 
-        excess_t = ring.tile([P, M // P, PACK, P], F32, name="excess_t", tag="wide")
-        base_t = ring.tile([P, M // P, PACK, P], F32, name="base_t", tag="wide")
+        turned_plain = [ring.tile([P, 2, PACK, PACK, P], F32, name="turned_plain", tag="wide") for half in range(2)]
         z_plain = [keep.tile([P, BANK, PACK], BF16, name="z_plain%d" % half, align_bytes=64) for half in range(2)]
         z_woven = [ring.tile([P, CHUNK, PACK], BF16, name="z_woven", bufs=4, align_bytes=64) for c in range(M // CHUNK)]
 
         z_rows = [keep.tile([P, PACK, BANK], BF16, name="z_rows%d" % half) for half in range(2)]
 
         def fetch_and_turn(s, m0):
-            if m0 == BANK:
+            if (s, m0) in AFTER:
+                neg_x2 = after[:, AFTER[(s, m0)], :]
+            elif m0 == BANK:
                 both = keep.tile([P, 2, BANK], F32, name="both", tag="held%d" % (s % 2))
                 neg_x2 = both[:, 0, :]
-            elif s == 0:
-                neg_x2 = keep.tile([P, BANK], F32, name="neg_x2", tag="turnstile", align_bytes=64)
             else:
                 neg_x2 = ring.tile([P, BANK], F32, name="neg_x2", bufs=XB)
-            nc.vector.tensor_scalar(neg_x2[:], page[:].indirect(entries(idx4, m0, BANK)), -1.0, 0.0, ALU.mult, ALU.add)
-            if m0 == BANK:
+            nc.vector.tensor_scalar(neg_x2[:], pages[s % 2][:].indirect(entries(idx4, m0, BANK)), -1.0, 0.0, ALU.mult, ALU.add)
+            if (s, m0) in AFTER and (s, m0) != (0, 0):
+                x1 = after[:, AFTER[(s, m0)] + 1, :]
+            elif m0 == BANK:
                 x1 = both[:, 1, :]
             elif s in (0, 2):
                 x1 = keep.tile([P, BANK], F32, name="x1", tag="woven", align_bytes=64)
             else:
                 x1 = ring.tile([P, BANK], F32, name="x1", bufs=XB)
-            nc.vector.tensor_copy(x1[:], page[:].indirect(entries(idx3, m0, BANK)))
+            nc.vector.tensor_copy(x1[:], pages[s % 2][:].indirect(entries(idx3, m0, BANK)))
             diff = psum.tile([P, PACK, P], F32, name="diff", tag="work", bufs=NB)
             add_transposed(diff, blocks_of(neg_x2, 0, PACK), blocks_of(x1, 0, PACK))
             base = psum.tile([P, PACK, P], F32, name="base", tag="work", bufs=NB)
@@ -234,15 +245,15 @@ def tile_list_cousin_matcher_kernel(
 
         def combine_plain(s, m0):
             diff, base = fetch_and_turn(s, m0)
-            where = (slice(None), slice(m0 // P, m0 // P + PACK), slice(None), slice(32 * s, 32 * (s + 1)))
+            target = turned_plain[m0 // BANK][:, :, :, :, 32 * s : 32 * (s + 1)]
             pattern = "m b (q t) -> m b t q"
-            nc.scalar.activation(excess_t[where], diff[:].rearrange(pattern, t=PACK), ACT.Relu)
-            nc.scalar.activation(base_t[where], base[:].rearrange(pattern, t=PACK), ACT.Copy, scale=-1.0)
+            nc.scalar.activation(target[:, 0], diff[:].rearrange(pattern, t=PACK), ACT.Relu)
+            nc.scalar.activation(target[:, 1], base[:].rearrange(pattern, t=PACK), ACT.Copy, scale=-1.0)
 
         def finish_plain(mb):
             neg_z = psum.tile([P, PACK, P], F32, name="neg_z", tag="work", bufs=NB)
-            add_transposed(neg_z, [excess_t[:, mb, t, :] for t in range(PACK)], [base_t[:, mb, t, :] for t in range(PACK)])
             half, part = divmod(mb, PACK)
+            add_transposed(neg_z, *[[turned_plain[half][:, k, part, t, :] for t in range(PACK)] for k in range(2)])
             nc.scalar.activation(
                 z_plain[half][:, P * part : P * (part + 1), :],
                 neg_z[:].rearrange("p t m -> p m t"),
@@ -251,26 +262,18 @@ def tile_list_cousin_matcher_kernel(
             )
 
         def combine_woven(s, m0):
-            if m0 == BANK:
-                both = keep.tile([P, 2, BANK], F32, name="both", tag="held%d" % (s % 2))
-                x2, x1 = both[:, 0, :], both[:, 1, :]
-            else:
-                x2 = ring.tile([P, BANK], F32, name="neg_x2", bufs=XB)
-                x1 = ring.tile([P, BANK], F32, name="x1", bufs=XB)
-            nc.vector.tensor_copy(x2[:], page[:].indirect(entries(idx4, m0, BANK)))
-            nc.vector.tensor_copy(x1[:], page[:].indirect(entries(idx3, m0, BANK)))
-            nc.vector.tensor_tensor(x1[:], x1[:], x2[:], ALU.min)
-            z_t = psum.tile([P, PACK, P], F32, name="z_t", tag="work", bufs=NB)
-            add_transposed(z_t, blocks_of(evs[s], m0, PACK), blocks_of(x1, 0, PACK))
-            turned = ring.tile([P, BANK], BF16, name="turned", align_bytes=64)
-            nc.scalar.copy(turned[:], z_t[:].rearrange("m b p -> m (b p)"))
-            return turned
+            diff, base = fetch_and_turn(s, m0)
+            excess = ring.tile([P, BANK], F32, name="excess")
+            nc.scalar.activation(excess[:], diff[:].rearrange("m b p -> m (b p)"), ACT.Relu)
+            neg_base = ring.tile([P, BANK], F32, name="neg_base")
+            nc.scalar.activation(neg_base[:], base[:].rearrange("m b p -> m (b p)"), ACT.Copy, scale=-1.0)
+            return excess, neg_base
 
         def finish_woven(s, m0, turned):
-            z_bank = psum.tile([P, BANK], BF16, name="z_bank", tag="y" if s == 6 else "work", bufs=8 - NB if s == 6 else NB)
-            for b in range(PACK):
-                nc.tensor.transpose(z_bank[:, P * b : P * (b + 1)], turned[:, P * b : P * (b + 1)], ident_bf16[:])
-            nc.scalar.copy(z_rows[m0 // BANK][:, s - PACK, :], z_bank[:])
+            neg_z = psum.tile([P, PACK, P], F32, name="neg_z", tag="y" if s == 6 else "work", bufs=8 - NB if s == 6 else NB)
+            add_transposed(neg_z, blocks_of(turned[0], 0, PACK), blocks_of(turned[1], 0, PACK))
+            flat = neg_z[:].rearrange("p b m -> p (b m)")
+            nc.scalar.activation(z_rows[m0 // BANK][:, s - PACK, :], flat, ACT.Copy, scale=-1.0)
 
         def combine_direct(s, c):
             m0 = CHUNK * c
@@ -278,12 +281,12 @@ def tile_list_cousin_matcher_kernel(
                 x1 = keep.tile([P, CHUNK], F32, name="x1", tag="z_plain1", align_bytes=64)
             else:
                 x1 = ring.tile([P, CHUNK], F32, name="x1", bufs=XB)
-            nc.vector.tensor_copy(x1[:], page[:].indirect(entries(idx3, m0, CHUNK)))
+            nc.vector.tensor_copy(x1[:], pages[s % 2][:].indirect(entries(idx3, m0, CHUNK)))
             if c == 0:
                 x2 = keep.tile([P, CHUNK], F32, name="x2", tag="z_plain0", align_bytes=64)
             else:
                 x2 = ring.tile([P, CHUNK], F32, name="x2", tag="neg_x2", bufs=XB)
-            nc.vector.tensor_copy(x2[:], page[:].indirect(entries(idx4, m0, CHUNK)))
+            nc.vector.tensor_copy(x2[:], pages[s % 2][:].indirect(entries(idx4, m0, CHUNK)))
             least = ring.tile([P, CHUNK], F32, name="least")
             nc.vector.tensor_tensor(least[:], x1[:], x2[:], ALU.min)
             rows = z_rows[m0 // BANK][:, :, m0 % BANK : m0 % BANK + CHUNK]
@@ -335,36 +338,37 @@ def tile_list_cousin_matcher_kernel(
             for pair in range(2):
                 y = score_banks[c][pair]
                 multiply(y, 1, c, pair)
-                result = ring.tile([P, 2, CHUNK], F32, name="result", bufs=4)
+                result = ring.tile([P, 2, CHUNK], F32, name="result", tag="w1_plain", bufs=4)
                 nc.vector.tensor_tensor(result[:], y[:], res_rows[pair][:, :, cols], ALU.add)
                 rows = out[2 * P * pair : 2 * P * (pair + 1), cols]
                 nc.sync.dma_start(rows.rearrange("(b p) m -> p b m", p=P), result[:])
 
-        slices = H // P
-        for s in range(slices):
+        def scatter(s):
             sig, factor = ready[s]
-            piece = BANK if s == 0 else S
+            piece = S // len(factor)
             for j0 in range(0, S, piece):
-                cols = slice(j0, j0 + piece)
                 nc.vector.tensor_tensor(
-                    page[:].indirect(entries(idx2, j0, piece)), sig[:, cols], factor[j0 // piece], ALU.mult
+                    pages[s % 2][:].indirect(entries(idx2, j0, piece)),
+                    sig[:, j0 : j0 + piece],
+                    factor[j0 // piece],
+                    ALU.mult,
                 )
+
+        def combine(s, m0):
+            return (combine_plain if s < PACK else combine_woven)(s, m0)
+
+        slices = H // P
+        scatter(0)
+        ready.append(activations(1))
+        prepare_plain(1)
+        ready.append(activations(2))
+        after = keep.tile([P, 5, BANK], F32, name="after", tag="turnstile", align_bytes=64)
+        early = combine(0, 0)
+        w1_woven = keep.tile([P, PACK, 2, P, PACK], BF16, name="w1_woven", tag="woven", align_bytes=64)
+        for s in range(slices - 1):
+            scatter(s + 1)
+            late = combine(s, BANK)
             if s == 0:
-                ready.append(activations(1))
-                prepare_plain(1)
-            if s < slices - 1:
-                turned = [(combine_plain if s < PACK else combine_woven)(s, m0) for m0 in range(0, M, BANK)]
-                if s + 2 < slices:
-                    ready.append(activations(s + 2))
-                if s >= PACK:
-                    for half in range(2):
-                        finish_woven(s, BANK * half, turned[half])
-                for mb in FIN.get(s, ()):
-                    finish_plain(mb)
-                if s + PACK < slices:
-                    evs.append(load_ev(s + PACK))
-            if s == 0:
-                w1_woven = keep.tile([P, PACK, 2, P, PACK], BF16, name="w1_woven", tag="woven", align_bytes=64)
                 for a in range(2):
                     nc.scalar.copy(
                         w1_woven[:, :, a, :, :].rearrange("p t c i -> p c t i"),
@@ -376,6 +380,19 @@ def tile_list_cousin_matcher_kernel(
                     source = res[2 * P * pair : 2 * P * (pair + 1), :]
                     nc.sync.dma_start(rows[:], source.rearrange("(b p) m -> p b m", p=P))
                     res_rows.append(rows)
+            if s + 3 < slices:
+                ready.append(activations(s + 3))
+            if s >= PACK:
+                finish_woven(s, 0, early)
+                finish_woven(s, BANK, late)
+            for mb in FIN.get(s, ()):
+                finish_plain(mb)
+            if s + PACK < slices:
+                evs.append(load_ev(s + PACK))
+            if s + 2 < slices:
+                early = combine(s + 1, 0)
+            for mb in FIN2.get(s, ()):
+                finish_plain(mb)
 
         chunks = M // CHUNK
         for half in range(2):

@@ -18,16 +18,18 @@ ALU = mybir.AluOpType
 ACT = mybir.ActivationFunctionType
 
 P = 128
+QUADRANT = 32
 PACK = 4
 K_PASS = P * PACK
-BANK = 512
+HALF = 512
 CHUNK = 256
 STRIPE = 16
-FIN = {3: (4, 5), 4: (6,), 5: (7,)}
-FIN2 = {2: (0, 1, 2, 3)}
-XB = 2
-AFTER = {(0, 0): 0, (0, 512): 1, (1, 0): 3}
-NB = 6
+SLICES = H // P
+CHUNKS = M // CHUNK
+LAST = SLICES - 1
+WORK_BANKS = 6
+END_BANKS = 2
+LATE_BLOCKS = {3: (4, 5), 4: (6,), 5: (7,)}
 
 
 def tile_list_cousin_matcher_kernel(
@@ -39,29 +41,32 @@ def tile_list_cousin_matcher_kernel(
         lists = ctx.enter_context(tc.tile_pool(name="lists", bufs=1))
         keep = ctx.enter_context(tc.tile_pool(name="keep", bufs=1))
         ring = ctx.enter_context(tc.tile_pool(name="ring", bufs=2))
-        psum = ctx.enter_context(tc.psum_pool(name="psum", bufs=2))
+        psum = ctx.enter_context(tc.psum_pool(name="psum", bufs=WORK_BANKS))
 
         def entries(list_tile, first, count):
             return list_tile[:, first // STRIPE : (first + count) // STRIPE]
 
-        def add_transposed(bank, first, second):
-            blocks = len(first)
-            for b in range(blocks):
-                nc.tensor.matmul(bank[:, b, :], first[b], ident[:], start=(b == 0), stop=False, is_transpose=True)
-            for b in range(blocks):
+        def bank(shape, at_end=False):
+            if at_end:
+                return psum.tile(shape, F32, name="end_bank", bufs=END_BANKS)
+            return psum.tile(shape, F32, name="work_bank")
+
+        def blocks_of(ap, first):
+            return [ap[:, first + P * b : first + P * (b + 1)] for b in range(PACK)]
+
+        def add_transposed(target, left, right):
+            for b in range(PACK):
+                nc.tensor.matmul(target[:, b, :], left[b], ident[:], start=(b == 0), stop=False, is_transpose=True)
+            for b in range(PACK):
                 nc.tensor.matmul(
-                    bank[:, b, :], second[b], ident[:], start=False, stop=(b == blocks - 1), is_transpose=True
+                    target[:, b, :], right[b], ident[:], start=False, stop=(b == PACK - 1), is_transpose=True
                 )
 
-        def blocks_of(ap, first, count):
-            return [ap[:, first + P * b : first + P * (b + 1)] for b in range(count)]
-
-        tab_plane = keep.tile([P, T], U8, name="tab_plane", tag="plane_then_codes", align_bytes=64)
+        tab_plane = keep.tile([P, T], U8, name="tab_plane", tag="plane_then_words", align_bytes=64)
         nc.vector.memset(tab_plane[:].bitcast(I32), 0)
-        for q in range(4):
-            nc.sync.dma_start(
-                tab_plane[32 * q : 32 * q + 8, :].bitcast(I32), tab_scales[:, 4 * q : 4 * q + 4, :].bitcast(I32)
-            )
+        for q in range(P // QUADRANT):
+            rows = tab_plane[QUADRANT * q : QUADRANT * q + 2 * PACK, :]
+            nc.sync.dma_start(rows.bitcast(I32), tab_scales[:, PACK * q : PACK * (q + 1), :].bitcast(I32))
         ident = keep.tile([P, P], F32, name="ident")
         make_identity(nc, ident[:])
         gain_rows = keep.tile([P, P], F32, name="gain_rows")
@@ -76,9 +81,9 @@ def tile_list_cousin_matcher_kernel(
         idx4 = lists.tile([P, M // STRIPE], U16, name="idx4")
 
         def load_table(a):
-            tab = ring.tile([P, T], I32, name="tab", tag="wide")
-            nc.sync.dma_start(tab[:], tab_words[a].rearrange("p t i -> p (t i)").bitcast(I32))
-            return tab
+            words = ring.tile([P, T], I32, name="tab", tag="wide")
+            nc.sync.dma_start(words[:], tab_words[a].rearrange("p t i -> p (t i)").bitcast(I32))
+            return words
 
         def load_w1_plain(pair):
             raws = []
@@ -90,12 +95,19 @@ def tile_list_cousin_matcher_kernel(
             return raws
 
         def load_ev(s):
-            ev_rows = ring.tile([P, M], F32, name="ev_rows", bufs=4)
+            rows = ring.tile([P, M], F32, name="ev_rows", bufs=4)
             if s < PACK:
-                nc.sync.dma_start(ev_rows[:], ev[P * s : P * (s + 1), :])
+                nc.sync.dma_start(rows[:], ev[P * s : P * (s + 1), :])
             else:
-                nc.sync.dma_start(ev_rows[:], ev[K_PASS:, :].rearrange("(p t) m -> p t m", t=PACK)[:, s - PACK, :])
-            return ev_rows
+                nc.sync.dma_start(rows[:], ev[K_PASS:, :].rearrange("(p t) m -> p t m", t=PACK)[:, s - PACK, :])
+            return rows
+
+        def load_wgs_woven(pair):
+            rows = keep.tile([P, 2, S], F32, name="wgs_woven%d" % pair)
+            source = wgs.rearrange("(p t) j -> p t j", t=PACK)[:, 2 * pair : 2 * pair + 2, :]
+            for q in range(P // QUADRANT):
+                nc.sync.dma_start(rows[QUADRANT * q : QUADRANT * (q + 1), :, :], source)
+            return [rows[:, 0, :], rows[:, 1, :]]
 
         nc.sync.dma_start(idx[:], offs)
         tabs = [load_table(0)]
@@ -103,12 +115,12 @@ def tile_list_cousin_matcher_kernel(
         nc.sync.dma_start(gain_rows[0:PACK, :], gain[0:K_PASS].rearrange("(s p) -> s p", p=P))
         tabs.append(load_table(1))
         wgs_plain = keep.tile([P, S], F32, name="wgs_plain")
-        nc.sync.dma_start(wgs_plain[:, 0:BANK], wgs[:, 0:BANK])
+        nc.sync.dma_start(wgs_plain[:, 0:HALF], wgs[:, 0:HALF])
         nc.sync.dma_start(idx2[:], offs2)
         nc.sync.dma_start(idx4[:], offs4)
         nc.sync.dma_start(idx3[:], offs3)
         evs = [load_ev(0)]
-        nc.sync.dma_start(wgs_plain[:, BANK:], wgs[:, BANK:])
+        nc.sync.dma_start(wgs_plain[:, HALF:], wgs[:, HALF:])
         w1_plain.append(load_w1_plain(1))
 
         w1_woven_raw = []
@@ -119,14 +131,6 @@ def tile_list_cousin_matcher_kernel(
             w1_woven_raw.append(raw)
         gain_woven = keep.tile([P, PACK], F32, name="gain_woven")
         nc.sync.dma_start(gain_woven[:], gain[K_PASS:].rearrange("(p t) -> p t", t=PACK))
-
-        def load_wgs_woven(pair):
-            rows = keep.tile([P, 2, S], F32, name="wgs_woven%d" % pair)
-            source = wgs.rearrange("(p t) j -> p t j", t=PACK)[:, 2 * pair : 2 * pair + 2, :]
-            for q in range(4):
-                nc.sync.dma_start(rows[32 * q : 32 * (q + 1), :, :], source)
-            return [rows[:, 0, :], rows[:, 1, :]]
-
         wgs_woven = load_wgs_woven(0)
         evs.extend(load_ev(s) for s in range(1, PACK))
         wgs_woven.extend(load_wgs_woven(1))
@@ -134,28 +138,27 @@ def tile_list_cousin_matcher_kernel(
         nc.sync.dma_start(w2_codes[:].bitcast(I32), w2_words.rearrange("a p c -> p a c").bitcast(I32))
         w2_plane = keep.tile([P, 2, N], U8, name="w2_plane", align_bytes=64)
         nc.vector.memset(w2_plane[:].rearrange("p a c -> p (a c)").bitcast(I32), 0)
-        for q in range(4):
+        for q in range(P // QUADRANT):
             nc.sync.dma_start(
-                w2_plane[32 * q : 32 * q + 4, :, :].bitcast(I32),
-                w2_scales[:, 4 * q : 4 * q + 4, :].rearrange("a r c -> r a c").bitcast(I32),
+                w2_plane[QUADRANT * q : QUADRANT * q + PACK, :, :].bitcast(I32),
+                w2_scales[:, PACK * q : PACK * (q + 1), :].rearrange("a r c -> r a c").bitcast(I32),
             )
 
         v_plane = keep.tile([P, S], U8, name="v_plane", align_bytes=64)
         nc.vector.tensor_copy(v_plane[:], tab_plane[:].indirect(idx[:]))
         v_codes = [
             keep.tile([P, S], U32, name="v_codes0", align_bytes=64),
-            keep.tile([P, S], U32, name="v_codes1", tag="plane_then_codes", align_bytes=64),
+            keep.tile([P, S], U32, name="v_codes1", tag="plane_then_words", align_bytes=64),
         ]
         nc.vector.tensor_copy(v_codes[0][:], tabs[0][:].bitcast(U32).indirect(idx[:]))
 
-        gain_bank = psum.tile([P, BANK], F32, name="gain_bank", tag="work", bufs=NB)
+        gain_bank = bank([P, HALF])
         nc.tensor.transpose(gain_bank[:, 0:P], gain_rows[:], ident[:])
         gain_plain = keep.tile([P, PACK], F32, name="gain_plain")
         nc.scalar.copy(gain_plain[:], gain_bank[:, 0:PACK])
 
-
-        w1_codes = keep.tile([P, H // P, 2 * P], U32, name="w1_codes", align_bytes=64)
-        w1_plane = keep.tile([P, H // P, 2 * P], U8, name="w1_plane", align_bytes=64)
+        w1_codes = keep.tile([P, SLICES, 2 * P], U32, name="w1_codes", align_bytes=64)
+        w1_plane = keep.tile([P, SLICES, 2 * P], U8, name="w1_plane", align_bytes=64)
 
         def quantise_w1(first, rounded):
             count = rounded.shape[1]
@@ -166,132 +169,140 @@ def tile_list_cousin_matcher_kernel(
             )
 
         def prepare_plain(pair):
-            rounded = keep.tile([P, 2, 2, P, PACK], BF16, name="w1_rounded", tag="turnstile", align_bytes=64)
+            rounded = keep.tile([P, 2, 2, P, PACK], BF16, name="w1_rounded", tag="opening", align_bytes=64)
             for a in range(2):
                 nc.scalar.copy(rounded[:, :, a, :, :], w1_plain[pair][a][:].rearrange("p i (s c) -> p s c i", s=2))
             quantise_w1(2 * pair, rounded)
 
         def activations(s):
-            codes, plane = w1_codes[:, s, :], w1_plane[:, s, :]
             if s < PACK:
                 weights, scale = wgs_plain[:], gain_plain[:, s : s + 1]
             else:
                 weights, scale = wgs_woven[s - PACK], gain_woven[:, s - PACK : s - PACK + 1]
-            both = ring.tile([P, 2, S], F32, name="both")
-            sig = both[:, 0, :]
+            placed = ring.tile([P, 2, S], F32, name="placed")
+            sigmoid = placed[:, 0, :]
             if s == 0:
-                first = keep.tile([P, BANK], F32, name="factor_first", tag="turnstile", align_bytes=64)
-                nc.scalar.activation(first[:], weights[:, 0:BANK], ACT.Copy, scale=scale)
-                factor = [first[:], both[:, 1, BANK:]]
-            for j0 in range(0, S, BANK):
-                cols = slice(j0, j0 + BANK)
-                e_bank = psum.tile([P, BANK], F32, name="e_bank", tag="work", bufs=NB)
+                first = keep.tile([P, HALF], F32, name="factor_first", tag="opening", align_bytes=64)
+                nc.scalar.activation(first[:], weights[:, 0:HALF], ACT.Copy, scale=scale)
+            for j0 in range(0, S, HALF):
+                cols = slice(j0, j0 + HALF)
+                e_bank = bank([P, HALF])
                 for a in range(2):
                     nc.tensor.matmul_mx(
                         out=e_bank[:],
-                        lhsT=codes[:, P * a : P * (a + 1)].bitcast(FP8X4),
-                        lhsT_scale=plane[:, P * a : P * (a + 1)],
+                        lhsT=w1_codes[:, s, P * a : P * (a + 1)].bitcast(FP8X4),
+                        lhsT_scale=w1_plane[:, s, P * a : P * (a + 1)],
                         rhs=v_codes[a][:, cols].bitcast(FP8X4),
-                        rhs_scale=v_plane[4 * a :, cols],
+                        rhs_scale=v_plane[PACK * a :, cols],
                         start=(a == 0),
                         stop=(a == 1),
                     )
-                nc.scalar.activation(sig[:, cols], e_bank[:], ACT.Sigmoid)
+                nc.scalar.activation(sigmoid[:, cols], e_bank[:], ACT.Sigmoid)
             if s == 0:
-                nc.scalar.activation(both[:, 1, BANK:], weights[:, BANK:], ACT.Copy, scale=scale)
-            else:
-                column = keep.tile([P, 1], F32, name="column", tag="held%d" % ((s + 1) % 2))
-                nc.scalar.copy(column[:], scale)
-                nc.scalar.activation(both[:, 1, :], weights, ACT.Copy, scale=column[:])
-                factor = [both[:, 1, :]]
-            return sig, factor
+                nc.scalar.activation(placed[:, 1, HALF:], weights[:, HALF:], ACT.Copy, scale=scale)
+                return sigmoid, [first[:], placed[:, 1, HALF:]]
+            column = keep.tile([P, 1], F32, name="gain_column", tag="late%d" % ((s + 1) % 2))
+            nc.scalar.copy(column[:], scale)
+            nc.scalar.activation(placed[:, 1, :], weights, ACT.Copy, scale=column[:])
+            return sigmoid, [placed[:, 1, :]]
 
         prepare_plain(0)
-        for j0 in range(0, S, BANK):
+        for j0 in range(0, S, HALF):
             nc.vector.tensor_copy(
-                v_codes[1][:, j0 : j0 + BANK], tabs[1][:].bitcast(U32).indirect(entries(idx, j0, BANK))
+                v_codes[1][:, j0 : j0 + HALF], tabs[1][:].bitcast(U32).indirect(entries(idx, j0, HALF))
             )
         ready = [activations(0)]
 
         turned_plain = [ring.tile([P, 2, PACK, PACK, P], F32, name="turned_plain", tag="wide") for half in range(2)]
-        z_plain = [keep.tile([P, BANK, PACK], BF16, name="z_plain%d" % half, align_bytes=64) for half in range(2)]
-        z_woven = [ring.tile([P, CHUNK, PACK], BF16, name="z_woven", bufs=4, align_bytes=64) for c in range(M // CHUNK)]
+        z_plain = [keep.tile([P, HALF, PACK], BF16, name="z_plain%d" % half, align_bytes=64) for half in range(2)]
+        z_woven = [keep.tile([P, CHUNK, PACK], BF16, name="z_woven%d" % c, align_bytes=64) for c in range(CHUNKS)]
+        z_rows = [keep.tile([P, PACK, HALF], BF16, name="z_rows%d" % half) for half in range(2)]
 
-        z_rows = [keep.tile([P, PACK, BANK], BF16, name="z_rows%d" % half) for half in range(2)]
+        def scatter(s):
+            sigmoid, factor = ready[s]
+            piece = S // len(factor)
+            for j0 in range(0, S, piece):
+                nc.vector.tensor_tensor(
+                    pages[s % 2][:].indirect(entries(idx2, j0, piece)),
+                    sigmoid[:, j0 : j0 + piece],
+                    factor[j0 // piece],
+                    ALU.mult,
+                )
+
+        def first_x1(s):
+            if s in (0, 2):
+                return keep.tile([P, HALF], F32, name="x1_held", tag="woven", align_bytes=64)
+            return ring.tile([P, HALF], F32, name="x1")
 
         def fetch_and_turn(s, m0):
-            if (s, m0) in AFTER:
-                neg_x2 = after[:, AFTER[(s, m0)], :]
-            elif m0 == BANK:
-                both = keep.tile([P, 2, BANK], F32, name="both", tag="held%d" % (s % 2))
-                neg_x2 = both[:, 0, :]
+            page = pages[s % 2]
+            if (s, m0) == (0, 0):
+                neg_x2 = opening[:, 0, :]
+            elif (s, m0) == (0, HALF):
+                neg_x2, x1 = opening[:, 1, :], opening[:, 2, :]
+            elif (s, m0) == (1, 0):
+                neg_x2, x1 = opening[:, 3, :], opening[:, 4, :]
+            elif m0 == HALF:
+                late_pair = keep.tile([P, 2, HALF], F32, name="late_pair", tag="late%d" % (s % 2))
+                neg_x2, x1 = late_pair[:, 0, :], late_pair[:, 1, :]
             else:
-                neg_x2 = ring.tile([P, BANK], F32, name="neg_x2", bufs=XB)
-            nc.vector.tensor_scalar(neg_x2[:], pages[s % 2][:].indirect(entries(idx4, m0, BANK)), -1.0, 0.0, ALU.mult, ALU.add)
-            if (s, m0) in AFTER and (s, m0) != (0, 0):
-                x1 = after[:, AFTER[(s, m0)] + 1, :]
-            elif m0 == BANK:
-                x1 = both[:, 1, :]
-            elif s in (0, 2):
-                x1 = keep.tile([P, BANK], F32, name="x1", tag="woven", align_bytes=64)
+                neg_x2 = ring.tile([P, HALF], F32, name="x2")
+            nc.vector.tensor_scalar(neg_x2[:], page[:].indirect(entries(idx4, m0, HALF)), -1.0, 0.0, ALU.mult, ALU.add)
+            if m0 == 0 and s != 1:
+                x1 = first_x1(s)
+            nc.vector.tensor_copy(x1[:], page[:].indirect(entries(idx3, m0, HALF)))
+            difference = bank([P, PACK, P])
+            add_transposed(difference, blocks_of(neg_x2, 0), blocks_of(x1, 0))
+            base = bank([P, PACK, P])
+            add_transposed(base, blocks_of(evs[s], m0), blocks_of(x1, 0))
+            return difference, base
+
+        def combine(s, m0):
+            difference, base = fetch_and_turn(s, m0)
+            if s < PACK:
+                target = turned_plain[m0 // HALF][:, :, :, :, QUADRANT * s : QUADRANT * (s + 1)]
+                excess, neg_base, pattern = target[:, 0], target[:, 1], "m b (q t) -> m b t q"
+                nc.scalar.activation(excess, difference[:].rearrange(pattern, t=PACK), ACT.Relu)
+                nc.scalar.activation(neg_base, base[:].rearrange(pattern, t=PACK), ACT.Copy, scale=-1.0)
             else:
-                x1 = ring.tile([P, BANK], F32, name="x1", bufs=XB)
-            nc.vector.tensor_copy(x1[:], pages[s % 2][:].indirect(entries(idx3, m0, BANK)))
-            diff = psum.tile([P, PACK, P], F32, name="diff", tag="work", bufs=NB)
-            add_transposed(diff, blocks_of(neg_x2, 0, PACK), blocks_of(x1, 0, PACK))
-            base = psum.tile([P, PACK, P], F32, name="base", tag="work", bufs=NB)
-            add_transposed(base, blocks_of(evs[s], m0, PACK), blocks_of(x1, 0, PACK))
-            return diff, base
-
-        def combine_plain(s, m0):
-            diff, base = fetch_and_turn(s, m0)
-            target = turned_plain[m0 // BANK][:, :, :, :, 32 * s : 32 * (s + 1)]
-            pattern = "m b (q t) -> m b t q"
-            nc.scalar.activation(target[:, 0], diff[:].rearrange(pattern, t=PACK), ACT.Relu)
-            nc.scalar.activation(target[:, 1], base[:].rearrange(pattern, t=PACK), ACT.Copy, scale=-1.0)
-
-        def finish_plain(mb):
-            neg_z = psum.tile([P, PACK, P], F32, name="neg_z", tag="work", bufs=NB)
-            half, part = divmod(mb, PACK)
-            add_transposed(neg_z, *[[turned_plain[half][:, k, part, t, :] for t in range(PACK)] for k in range(2)])
-            nc.scalar.activation(
-                z_plain[half][:, P * part : P * (part + 1), :],
-                neg_z[:].rearrange("p t m -> p m t"),
-                ACT.Copy,
-                scale=-1.0,
-            )
-
-        def combine_woven(s, m0):
-            diff, base = fetch_and_turn(s, m0)
-            excess = ring.tile([P, BANK], F32, name="excess")
-            nc.scalar.activation(excess[:], diff[:].rearrange("m b p -> m (b p)"), ACT.Relu)
-            neg_base = ring.tile([P, BANK], F32, name="neg_base")
-            nc.scalar.activation(neg_base[:], base[:].rearrange("m b p -> m (b p)"), ACT.Copy, scale=-1.0)
+                excess = ring.tile([P, HALF], F32, name="excess")
+                nc.scalar.activation(excess[:], difference[:].rearrange("m b p -> m (b p)"), ACT.Relu)
+                neg_base = ring.tile([P, HALF], F32, name="neg_base")
+                nc.scalar.activation(neg_base[:], base[:].rearrange("m b p -> m (b p)"), ACT.Copy, scale=-1.0)
             return excess, neg_base
 
-        def finish_woven(s, m0, turned):
-            neg_z = psum.tile([P, PACK, P], F32, name="neg_z", tag="y" if s == 6 else "work", bufs=8 - NB if s == 6 else NB)
-            add_transposed(neg_z, blocks_of(turned[0], 0, PACK), blocks_of(turned[1], 0, PACK))
-            flat = neg_z[:].rearrange("p b m -> p (b m)")
-            nc.scalar.activation(z_rows[m0 // BANK][:, s - PACK, :], flat, ACT.Copy, scale=-1.0)
+        def finish_plain(block):
+            neg_z = bank([P, PACK, P])
+            half, b = divmod(block, PACK)
+            add_transposed(neg_z, *[[turned_plain[half][:, k, b, t, :] for t in range(PACK)] for k in range(2)])
+            nc.scalar.activation(
+                z_plain[half][:, P * b : P * (b + 1), :], neg_z[:].rearrange("p t m -> p m t"), ACT.Copy, scale=-1.0
+            )
 
-        def combine_direct(s, c):
+        def finish_woven(s, m0, excess, neg_base):
+            neg_z = bank([P, PACK, P], at_end=(s == LAST - 1))
+            add_transposed(neg_z, blocks_of(excess, 0), blocks_of(neg_base, 0))
+            flat = neg_z[:].rearrange("p b m -> p (b m)")
+            nc.scalar.activation(z_rows[m0 // HALF][:, s - PACK, :], flat, ACT.Copy, scale=-1.0)
+
+        def combine_last(c):
             m0 = CHUNK * c
+            page = pages[LAST % 2]
             if c == 0:
-                x1 = keep.tile([P, CHUNK], F32, name="x1", tag="z_plain1", align_bytes=64)
+                x1 = keep.tile([P, CHUNK], F32, name="x1_first", tag="z_plain1", align_bytes=64)
             else:
-                x1 = ring.tile([P, CHUNK], F32, name="x1", bufs=XB)
-            nc.vector.tensor_copy(x1[:], pages[s % 2][:].indirect(entries(idx3, m0, CHUNK)))
+                x1 = ring.tile([P, CHUNK], F32, name="x1")
+            nc.vector.tensor_copy(x1[:], page[:].indirect(entries(idx3, m0, CHUNK)))
             if c == 0:
-                x2 = keep.tile([P, CHUNK], F32, name="x2", tag="z_plain0", align_bytes=64)
+                x2 = keep.tile([P, CHUNK], F32, name="x2_first", tag="z_plain0", align_bytes=64)
             else:
-                x2 = ring.tile([P, CHUNK], F32, name="x2", tag="neg_x2", bufs=XB)
-            nc.vector.tensor_copy(x2[:], pages[s % 2][:].indirect(entries(idx4, m0, CHUNK)))
+                x2 = ring.tile([P, CHUNK], F32, name="x2")
+            nc.vector.tensor_copy(x2[:], page[:].indirect(entries(idx4, m0, CHUNK)))
             least = ring.tile([P, CHUNK], F32, name="least")
             nc.vector.tensor_tensor(least[:], x1[:], x2[:], ALU.min)
-            rows = z_rows[m0 // BANK][:, :, m0 % BANK : m0 % BANK + CHUNK]
-            nc.vector.tensor_tensor(rows[:, s - PACK, :], least[:], evs[s][:, m0 : m0 + CHUNK], ALU.add)
-            weave = nc.vector.tensor_copy if c == M // CHUNK - 1 else nc.scalar.copy
+            rows = z_rows[m0 // HALF][:, :, m0 % HALF : m0 % HALF + CHUNK]
+            nc.vector.tensor_tensor(rows[:, LAST - PACK, :], least[:], evs[LAST][:, m0 : m0 + CHUNK], ALU.add)
+            weave = nc.vector.tensor_copy if c == CHUNKS - 1 else nc.scalar.copy
             weave(
                 z_woven[c][:].rearrange("p (m i) t -> p m t i", i=PACK),
                 rows.rearrange("p t (m i) -> p m t i", i=PACK),
@@ -312,8 +323,8 @@ def tile_list_cousin_matcher_kernel(
 
         def multiply(y, a, c, pair):
             codes, plane = z_mx[a][c]
-            steps = [(b, m0) for b in range(2) for m0 in range(0, CHUNK, P)]
-            for b, m0 in steps:
+            parts = [(b, m0) for b in range(2) for m0 in range(0, CHUNK, P)]
+            for b, m0 in parts:
                 n0 = P * (2 * pair + b)
                 nc.tensor.matmul_mx(
                     out=y[:, b, m0 : m0 + P],
@@ -321,14 +332,14 @@ def tile_list_cousin_matcher_kernel(
                     lhsT_scale=w2_plane[:, a, n0 : n0 + P],
                     rhs=codes[:, m0 : m0 + P].bitcast(FP8X4),
                     rhs_scale=plane[:, m0 : m0 + P],
-                    start=(a == 0 and (b, m0) == steps[0]),
-                    stop=(a == 1 and (b, m0) == steps[-1]),
+                    start=(a == 0 and (b, m0) == parts[0]),
+                    stop=(a == 1 and (b, m0) == parts[-1]),
                 )
 
         def open_scores(c):
             banks = []
             for pair in range(2):
-                y = psum.tile([P, 2, CHUNK], F32, name="y", tag="y" if c == 0 else "work", bufs=8 - NB if c == 0 else NB)
+                y = bank([P, 2, CHUNK], at_end=(c == 0))
                 multiply(y, 0, c, pair)
                 banks.append(y)
             return banks
@@ -338,36 +349,21 @@ def tile_list_cousin_matcher_kernel(
             for pair in range(2):
                 y = score_banks[c][pair]
                 multiply(y, 1, c, pair)
-                result = ring.tile([P, 2, CHUNK], F32, name="result", tag="w1_plain", bufs=4)
-                nc.vector.tensor_tensor(result[:], y[:], res_rows[pair][:, :, cols], ALU.add)
+                result = results[c // 2][:, 2 * (c % 2) + pair, :, :]
+                nc.vector.tensor_tensor(result, y[:], res_rows[pair][:, :, cols], ALU.add)
                 rows = out[2 * P * pair : 2 * P * (pair + 1), cols]
-                nc.sync.dma_start(rows.rearrange("(b p) m -> p b m", p=P), result[:])
+                nc.sync.dma_start(rows.rearrange("(b p) m -> p b m", p=P), result)
 
-        def scatter(s):
-            sig, factor = ready[s]
-            piece = S // len(factor)
-            for j0 in range(0, S, piece):
-                nc.vector.tensor_tensor(
-                    pages[s % 2][:].indirect(entries(idx2, j0, piece)),
-                    sig[:, j0 : j0 + piece],
-                    factor[j0 // piece],
-                    ALU.mult,
-                )
-
-        def combine(s, m0):
-            return (combine_plain if s < PACK else combine_woven)(s, m0)
-
-        slices = H // P
         scatter(0)
         ready.append(activations(1))
         prepare_plain(1)
         ready.append(activations(2))
-        after = keep.tile([P, 5, BANK], F32, name="after", tag="turnstile", align_bytes=64)
+        opening = keep.tile([P, 5, HALF], F32, name="opening", tag="opening", align_bytes=64)
         early = combine(0, 0)
         w1_woven = keep.tile([P, PACK, 2, P, PACK], BF16, name="w1_woven", tag="woven", align_bytes=64)
-        for s in range(slices - 1):
+        for s in range(LAST):
             scatter(s + 1)
-            late = combine(s, BANK)
+            late = combine(s, HALF)
             if s == 0:
                 for a in range(2):
                     nc.scalar.copy(
@@ -380,30 +376,31 @@ def tile_list_cousin_matcher_kernel(
                     source = res[2 * P * pair : 2 * P * (pair + 1), :]
                     nc.sync.dma_start(rows[:], source.rearrange("(b p) m -> p b m", p=P))
                     res_rows.append(rows)
-            if s + 3 < slices:
+            if s + 3 < SLICES:
                 ready.append(activations(s + 3))
             if s >= PACK:
-                finish_woven(s, 0, early)
-                finish_woven(s, BANK, late)
-            for mb in FIN.get(s, ()):
-                finish_plain(mb)
-            if s + PACK < slices:
+                finish_woven(s, 0, *early)
+                finish_woven(s, HALF, *late)
+            for block in LATE_BLOCKS.get(s, ()):
+                finish_plain(block)
+            if s + PACK < SLICES:
                 evs.append(load_ev(s + PACK))
-            if s + 2 < slices:
+            if s + 1 < LAST:
                 early = combine(s + 1, 0)
-            for mb in FIN2.get(s, ()):
-                finish_plain(mb)
+            if s + 1 == PACK - 1:
+                for block in range(PACK):
+                    finish_plain(block)
 
-        chunks = M // CHUNK
         for half in range(2):
             quantise_z(0, z_plain[half])
+        results = [ring.tile([P, PACK, 2, CHUNK], F32, name="results", tag="placed") for half in range(2)]
         score_banks = [open_scores(0)]
-        for step in range(chunks + 2):
-            if step < chunks:
-                combine_direct(slices - 1, step)
-            if step + 1 < chunks:
+        for step in range(CHUNKS + 2):
+            if step < CHUNKS:
+                combine_last(step)
+            if step + 1 < CHUNKS:
                 score_banks.append(open_scores(step + 1))
-            if 1 <= step <= chunks:
+            if 1 <= step <= CHUNKS:
                 quantise_z(1, z_woven[step - 1])
             if step >= 2:
                 close_scores(step - 2)

@@ -27,9 +27,10 @@ STRIPE = 16
 SLICES = H // P
 CHUNKS = M // CHUNK
 LAST = SLICES - 1
-WORK_BANKS = 6
-END_BANKS = 2
-LATE_BLOCKS = {3: (4, 5), 4: (6,), 5: (7,)}
+PAGES = 3
+W1_GROUPS = ((0, 1), (1, 2), (2, 4), (4, 8))
+VECTOR_PAGES = 1
+BANKS = 8
 
 
 def tile_list_cousin_matcher_kernel(
@@ -40,40 +41,33 @@ def tile_list_cousin_matcher_kernel(
     with ExitStack() as ctx:
         lists = ctx.enter_context(tc.tile_pool(name="lists", bufs=1))
         keep = ctx.enter_context(tc.tile_pool(name="keep", bufs=1))
-        ring = ctx.enter_context(tc.tile_pool(name="ring", bufs=2))
-        psum = ctx.enter_context(tc.psum_pool(name="psum", bufs=WORK_BANKS))
+        psum = ctx.enter_context(tc.psum_pool(name="psum", bufs=1))
 
         def entries(list_tile, first, count):
             return list_tile[:, first // STRIPE : (first + count) // STRIPE]
 
-        def bank(shape, at_end=False):
-            if at_end:
-                return psum.tile(shape, F32, name="end_bank", bufs=END_BANKS)
-            return psum.tile(shape, F32, name="work_bank")
+        def work_bank(shape, dtype=F32):
+            return psum.tile(shape, dtype, name="work_bank", bufs=BANKS)
 
-        def blocks_of(ap, first):
-            return [ap[:, first + P * b : first + P * (b + 1)] for b in range(PACK)]
-
-        def add_transposed(target, left, right):
-            for b in range(PACK):
-                nc.tensor.matmul(target[:, b, :], left[b], ident[:], start=(b == 0), stop=False, is_transpose=True)
-            for b in range(PACK):
-                nc.tensor.matmul(
-                    target[:, b, :], right[b], ident[:], start=False, stop=(b == PACK - 1), is_transpose=True
-                )
-
-        tab_plane = keep.tile([P, T], U8, name="tab_plane", tag="plane_then_words", align_bytes=64)
+        tab_plane = keep.tile([P, T], U8, name="tab_plane", align_bytes=64)
         nc.vector.memset(tab_plane[:].bitcast(I32), 0)
-        for q in range(P // QUADRANT):
-            rows = tab_plane[QUADRANT * q : QUADRANT * q + 2 * PACK, :]
-            nc.sync.dma_start(rows.bitcast(I32), tab_scales[:, PACK * q : PACK * (q + 1), :].bitcast(I32))
-        ident = keep.tile([P, P], F32, name="ident")
-        make_identity(nc, ident[:])
         gain_rows = keep.tile([P, P], F32, name="gain_rows")
         nc.vector.memset(gain_rows[:], 0.0)
-        pages = [keep.tile([P, T2], F32, name="page%d" % n) for n in range(2)]
-        for page in pages:
-            nc.vector.memset(page[:], 0.0)
+        w2_plane = keep.tile([P, 2, N], U8, name="w2_plane", align_bytes=64)
+        nc.vector.memset(w2_plane[:].rearrange("p a c -> p (a c)").bitcast(I32), 0)
+        minus_one = keep.tile([P, HALF], F32, name="minus_one")
+        nc.vector.memset(minus_one[:], -1.0)
+        ident = keep.tile([P, P], F32, name="ident")
+        make_identity(nc, ident[:])
+        ident_bf16 = keep.tile([P, P], BF16, name="ident_bf16")
+        make_identity(nc, ident_bf16[:])
+        pages = [keep.tile([P, T2], F32, name="page%d" % s) for s in range(PAGES)]
+        for s, page in enumerate(pages):
+            if s < VECTOR_PAGES:
+                nc.vector.memset(page[:], 0.0)
+            else:
+                for c0 in range(0, T2, HALF):
+                    nc.gpsimd.memset(page[:, c0 : c0 + HALF], 0.0)
 
         idx = lists.tile([P, S // STRIPE], U16, name="idx")
         idx2 = lists.tile([P, S // STRIPE], U16, name="idx2")
@@ -81,21 +75,39 @@ def tile_list_cousin_matcher_kernel(
         idx4 = lists.tile([P, M // STRIPE], U16, name="idx4")
 
         def load_table(a):
-            words = ring.tile([P, T], I32, name="tab", tag="wide")
+            words = keep.tile([P, T], I32, name="tab", tag="tab%d" % a)
             nc.sync.dma_start(words[:], tab_words[a].rearrange("p t i -> p (t i)").bitcast(I32))
             return words
 
-        def load_w1_plain(pair):
+        def load_w1(g):
+            first, last = W1_GROUPS[g]
             raws = []
             for a in range(2):
-                raw = ring.tile([P, PACK, 2 * P], F32, name="w1_plain", bufs=4)
-                rows = w1[K_PASS * a : K_PASS * (a + 1), 2 * P * pair : 2 * P * (pair + 1)]
+                raw = keep.tile([P, PACK, P * (last - first)], F32, name="w1_raw", tag="raw%d_%d" % (g, a))
+                rows = w1[K_PASS * a : K_PASS * (a + 1), P * first : P * last]
                 nc.sync.dma_start(raw[:], rows.rearrange("(p i) c -> p i c", i=PACK))
                 raws.append(raw)
             return raws
 
+        tabs = [load_table(0)]
+        nc.sync.dma_start(idx[:], offs)
+        for q in range(P // QUADRANT):
+            rows = tab_plane[QUADRANT * q : QUADRANT * q + 2 * PACK, :]
+            nc.sync.dma_start(rows.bitcast(I32), tab_scales[:, PACK * q : PACK * (q + 1), :].bitcast(I32))
+        w1_raw = [load_w1(0)]
+        nc.sync.dma_start(gain_rows[0:PACK, :], gain[0:K_PASS].rearrange("(s p) -> s p", p=P))
+        tabs.append(load_table(1))
+        wgs_rows = keep.tile([P, S], F32, name="wgs_rows")
+        nc.sync.dma_start(wgs_rows[:, 0:HALF], wgs[:, 0:HALF])
+        nc.sync.dma_start(idx2[:], offs2)
+        w1_raw.append(load_w1(1))
+        nc.sync.dma_start(wgs_rows[:, HALF:], wgs[:, HALF:])
+        w1_raw.append(load_w1(2))
+        nc.sync.dma_start(idx3[:], offs3)
+        nc.sync.dma_start(idx4[:], offs4)
+
         def load_ev(s):
-            rows = ring.tile([P, M], F32, name="ev_rows", bufs=4)
+            rows = keep.tile([P, M], F32, name="ev_rows", bufs=PACK)
             if s < PACK:
                 nc.sync.dma_start(rows[:], ev[P * s : P * (s + 1), :])
             else:
@@ -109,50 +121,30 @@ def tile_list_cousin_matcher_kernel(
                 nc.sync.dma_start(rows[QUADRANT * q : QUADRANT * (q + 1), :, :], source)
             return [rows[:, 0, :], rows[:, 1, :]]
 
-        nc.sync.dma_start(idx[:], offs)
-        tabs = [load_table(0)]
-        w1_plain = [load_w1_plain(0)]
-        nc.sync.dma_start(gain_rows[0:PACK, :], gain[0:K_PASS].rearrange("(s p) -> s p", p=P))
-        tabs.append(load_table(1))
-        wgs_plain = keep.tile([P, S], F32, name="wgs_plain")
-        nc.sync.dma_start(wgs_plain[:, 0:HALF], wgs[:, 0:HALF])
-        nc.sync.dma_start(idx2[:], offs2)
-        nc.sync.dma_start(idx4[:], offs4)
-        nc.sync.dma_start(idx3[:], offs3)
         evs = [load_ev(0)]
-        nc.sync.dma_start(wgs_plain[:, HALF:], wgs[:, HALF:])
-        w1_plain.append(load_w1_plain(1))
-
-        w1_woven_raw = []
-        for a in range(2):
-            raw = ring.tile([P, PACK, K_PASS], F32, name="w1_woven_raw", tag="half_wide")
-            rows = w1[K_PASS * a : K_PASS * (a + 1), K_PASS:]
-            nc.sync.dma_start(raw[:], rows.rearrange("(p i) c -> p i c", i=PACK))
-            w1_woven_raw.append(raw)
+        w1_raw.append(load_w1(3))
         gain_woven = keep.tile([P, PACK], F32, name="gain_woven")
         nc.sync.dma_start(gain_woven[:], gain[K_PASS:].rearrange("(p t) -> p t", t=PACK))
+        evs.append(load_ev(1))
         wgs_woven = load_wgs_woven(0)
-        evs.extend(load_ev(s) for s in range(1, PACK))
+        evs.extend(load_ev(s) for s in range(2, PACK))
         wgs_woven.extend(load_wgs_woven(1))
         w2_codes = keep.tile([P, 2, 2 * N], U8, name="w2_codes", align_bytes=64)
         nc.sync.dma_start(w2_codes[:].bitcast(I32), w2_words.rearrange("a p c -> p a c").bitcast(I32))
-        w2_plane = keep.tile([P, 2, N], U8, name="w2_plane", align_bytes=64)
-        nc.vector.memset(w2_plane[:].rearrange("p a c -> p (a c)").bitcast(I32), 0)
         for q in range(P // QUADRANT):
             nc.sync.dma_start(
                 w2_plane[QUADRANT * q : QUADRANT * q + PACK, :, :].bitcast(I32),
                 w2_scales[:, PACK * q : PACK * (q + 1), :].rearrange("a r c -> r a c").bitcast(I32),
             )
 
+        v_codes = [keep.tile([P, S], U32, name="v_codes%d" % a, align_bytes=64) for a in range(2)]
+        nc.vector.tensor_copy(v_codes[0][:], tabs[0][:].bitcast(U32).indirect(idx[:]))
         v_plane = keep.tile([P, S], U8, name="v_plane", align_bytes=64)
         nc.vector.tensor_copy(v_plane[:], tab_plane[:].indirect(idx[:]))
-        v_codes = [
-            keep.tile([P, S], U32, name="v_codes0", align_bytes=64),
-            keep.tile([P, S], U32, name="v_codes1", tag="plane_then_words", align_bytes=64),
-        ]
-        nc.vector.tensor_copy(v_codes[0][:], tabs[0][:].bitcast(U32).indirect(idx[:]))
+        res_rows = keep.tile([P, N // P, M], F32, name="res_rows", tag="tab0")
+        nc.sync.dma_start(res_rows[:], res.rearrange("(b p) m -> p b m", p=P))
 
-        gain_bank = bank([P, HALF])
+        gain_bank = work_bank([P, HALF])
         nc.tensor.transpose(gain_bank[:, 0:P], gain_rows[:], ident[:])
         gain_plain = keep.tile([P, PACK], F32, name="gain_plain")
         nc.scalar.copy(gain_plain[:], gain_bank[:, 0:PACK])
@@ -160,33 +152,36 @@ def tile_list_cousin_matcher_kernel(
         w1_codes = keep.tile([P, SLICES, 2 * P], U32, name="w1_codes", align_bytes=64)
         w1_plane = keep.tile([P, SLICES, 2 * P], U8, name="w1_plane", align_bytes=64)
 
-        def quantise_w1(first, rounded):
-            count = rounded.shape[1]
+        def prepare_w1(g):
+            first, last = W1_GROUPS[g]
+            rounded = keep.tile(
+                [P, last - first, 2, P, PACK], BF16, name="w1_rounded", tag="rounded%d" % (g % 2), align_bytes=64
+            )
+            for a in range(2):
+                if first < PACK:
+                    nc.scalar.copy(
+                        rounded[:, :, a, :, :].rearrange("p s (c j) i -> p s c i j", j=PACK),
+                        w1_raw[g][a][:].rearrange("p i (s c j) -> p s c i j", s=last - first, j=PACK),
+                    )
+                else:
+                    nc.scalar.copy(
+                        rounded[:, :, a, :, :].rearrange("p t c i -> p c t i"),
+                        w1_raw[g][a][:].rearrange("p i (c t) -> p c t i", t=PACK),
+                    )
             nc.vector.quantize_mx(
-                out=w1_codes[:, first : first + count, :].rearrange("p s c -> p (s c)").bitcast(FP8X4),
-                scales=w1_plane[:, first : first + count, :].rearrange("p s c -> p (s c)"),
+                out=w1_codes[:, first:last, :].rearrange("p s c -> p (s c)").bitcast(FP8X4),
+                scales=w1_plane[:, first:last, :].rearrange("p s c -> p (s c)"),
                 in_=rounded[:].rearrange("p s a c i -> p (s a c i)"),
             )
 
-        def prepare_plain(pair):
-            rounded = keep.tile([P, 2, 2, P, PACK], BF16, name="w1_rounded", tag="opening", align_bytes=64)
-            for a in range(2):
-                nc.scalar.copy(rounded[:, :, a, :, :], w1_plain[pair][a][:].rearrange("p i (s c) -> p s c i", s=2))
-            quantise_w1(2 * pair, rounded)
-
-        def activations(s):
-            if s < PACK:
-                weights, scale = wgs_plain[:], gain_plain[:, s : s + 1]
+        def sigmoid_of(s):
+            if s in (1, 3):
+                sigmoid = keep.tile([P, S], F32, name="sigmoid_held", tag="raw%d_1" % (2 + s // 2))
             else:
-                weights, scale = wgs_woven[s - PACK], gain_woven[:, s - PACK : s - PACK + 1]
-            placed = ring.tile([P, 2, S], F32, name="placed")
-            sigmoid = placed[:, 0, :]
-            if s == 0:
-                first = keep.tile([P, HALF], F32, name="factor_first", tag="opening", align_bytes=64)
-                nc.scalar.activation(first[:], weights[:, 0:HALF], ACT.Copy, scale=scale)
+                sigmoid = keep.tile([P, S], F32, name="sigmoid", bufs=2)
             for j0 in range(0, S, HALF):
                 cols = slice(j0, j0 + HALF)
-                e_bank = bank([P, HALF])
+                e_bank = work_bank([P, HALF])
                 for a in range(2):
                     nc.tensor.matmul_mx(
                         out=e_bank[:],
@@ -198,128 +193,114 @@ def tile_list_cousin_matcher_kernel(
                         stop=(a == 1),
                     )
                 nc.scalar.activation(sigmoid[:, cols], e_bank[:], ACT.Sigmoid)
-            if s == 0:
-                nc.scalar.activation(placed[:, 1, HALF:], weights[:, HALF:], ACT.Copy, scale=scale)
-                return sigmoid, [first[:], placed[:, 1, HALF:]]
-            column = keep.tile([P, 1], F32, name="gain_column", tag="late%d" % ((s + 1) % 2))
-            nc.scalar.copy(column[:], scale)
-            nc.scalar.activation(placed[:, 1, :], weights, ACT.Copy, scale=column[:])
-            return sigmoid, [placed[:, 1, :]]
+            return sigmoid
 
-        prepare_plain(0)
+        def factor_of(s, j0, count, factor):
+            if s < PACK:
+                weights, scale = wgs_rows[:], gain_plain[:, s : s + 1]
+            else:
+                weights, scale = wgs_woven[s - PACK], gain_woven[:, s - PACK : s - PACK + 1]
+            nc.scalar.activation(factor[:], weights[:, j0 : j0 + count], ACT.Copy, scale=scale)
+            return factor
+
+        def activations(s):
+            sigmoid = sigmoid_of(s)
+            return sigmoid, factor_of(s, 0, S, keep.tile([P, S], F32, name="factor", bufs=2))
+
+        def scatter(s, j0, sigmoid, factor):
+            count = factor.shape[1]
+            nc.vector.tensor_tensor(
+                pages[s % PAGES][:].indirect(entries(idx2, j0, count)), sigmoid[:, j0 : j0 + count], factor[:], ALU.mult
+            )
+
+        def negate_ev(s):
+            nc.scalar.activation(evs[s][:], evs[s][:], ACT.Copy, scale=-1.0)
+
+        prepare_w1(0)
         for j0 in range(0, S, HALF):
             nc.vector.tensor_copy(
                 v_codes[1][:, j0 : j0 + HALF], tabs[1][:].bitcast(U32).indirect(entries(idx, j0, HALF))
             )
-        ready = [activations(0)]
+        results = keep.tile([P, CHUNKS, N // P, CHUNK], F32, name="results", tag="tab1")
+        sigmoid = sigmoid_of(0)
+        scatter(0, 0, sigmoid, factor_of(0, 0, HALF, keep.tile([P, HALF], F32, name="factor", bufs=2)))
+        prepare_w1(1)
+        scatter(0, HALF, sigmoid, factor_of(0, HALF, HALF, keep.tile([P, HALF], F32, name="factor_held", tag="raw1_1")))
+        prepare_w1(2)
+        ready = {1: activations(1)}
 
-        turned_plain = [ring.tile([P, 2, PACK, PACK, P], F32, name="turned_plain", tag="wide") for half in range(2)]
-        z_plain = [keep.tile([P, HALF, PACK], BF16, name="z_plain%d" % half, align_bytes=64) for half in range(2)]
-        z_woven = [keep.tile([P, CHUNK, PACK], BF16, name="z_woven%d" % c, align_bytes=64) for c in range(CHUNKS)]
+        z_turned = [keep.tile([P, PACK, K_PASS], BF16, name="z_turned%d" % half) for half in range(2)]
         z_rows = [keep.tile([P, PACK, HALF], BF16, name="z_rows%d" % half) for half in range(2)]
-
-        def scatter(s):
-            sigmoid, factor = ready[s]
-            piece = S // len(factor)
-            for j0 in range(0, S, piece):
-                nc.vector.tensor_tensor(
-                    pages[s % 2][:].indirect(entries(idx2, j0, piece)),
-                    sigmoid[:, j0 : j0 + piece],
-                    factor[j0 // piece],
-                    ALU.mult,
-                )
-
-        def first_x1(s):
-            if s in (0, 2):
-                return keep.tile([P, HALF], F32, name="x1_held", tag="woven", align_bytes=64)
-            return ring.tile([P, HALF], F32, name="x1")
-
-        def fetch_and_turn(s, m0):
-            page = pages[s % 2]
-            if (s, m0) == (0, 0):
-                neg_x2 = opening[:, 0, :]
-            elif (s, m0) == (0, HALF):
-                neg_x2, x1 = opening[:, 1, :], opening[:, 2, :]
-            elif (s, m0) == (1, 0):
-                neg_x2, x1 = opening[:, 3, :], opening[:, 4, :]
-            elif m0 == HALF:
-                late_pair = keep.tile([P, 2, HALF], F32, name="late_pair", tag="late%d" % (s % 2))
-                neg_x2, x1 = late_pair[:, 0, :], late_pair[:, 1, :]
-            else:
-                neg_x2 = ring.tile([P, HALF], F32, name="x2")
-            nc.vector.tensor_scalar(neg_x2[:], page[:].indirect(entries(idx4, m0, HALF)), -1.0, 0.0, ALU.mult, ALU.add)
-            if m0 == 0 and s != 1:
-                x1 = first_x1(s)
-            nc.vector.tensor_copy(x1[:], page[:].indirect(entries(idx3, m0, HALF)))
-            difference = bank([P, PACK, P])
-            add_transposed(difference, blocks_of(neg_x2, 0), blocks_of(x1, 0))
-            base = bank([P, PACK, P])
-            add_transposed(base, blocks_of(evs[s], m0), blocks_of(x1, 0))
-            return difference, base
-
-        def combine(s, m0):
-            difference, base = fetch_and_turn(s, m0)
-            if s < PACK:
-                target = turned_plain[m0 // HALF][:, :, :, :, QUADRANT * s : QUADRANT * (s + 1)]
-                excess, neg_base, pattern = target[:, 0], target[:, 1], "m b (q t) -> m b t q"
-                nc.scalar.activation(excess, difference[:].rearrange(pattern, t=PACK), ACT.Relu)
-                nc.scalar.activation(neg_base, base[:].rearrange(pattern, t=PACK), ACT.Copy, scale=-1.0)
-            else:
-                excess = ring.tile([P, HALF], F32, name="excess")
-                nc.scalar.activation(excess[:], difference[:].rearrange("m b p -> m (b p)"), ACT.Relu)
-                neg_base = ring.tile([P, HALF], F32, name="neg_base")
-                nc.scalar.activation(neg_base[:], base[:].rearrange("m b p -> m (b p)"), ACT.Copy, scale=-1.0)
-            return excess, neg_base
-
-        def finish_plain(block):
-            neg_z = bank([P, PACK, P])
-            half, b = divmod(block, PACK)
-            add_transposed(neg_z, *[[turned_plain[half][:, k, b, t, :] for t in range(PACK)] for k in range(2)])
-            nc.scalar.activation(
-                z_plain[half][:, P * b : P * (b + 1), :], neg_z[:].rearrange("p t m -> p m t"), ACT.Copy, scale=-1.0
-            )
-
-        def finish_woven(s, m0, excess, neg_base):
-            neg_z = bank([P, PACK, P], at_end=(s == LAST - 1))
-            add_transposed(neg_z, blocks_of(excess, 0), blocks_of(neg_base, 0))
-            flat = neg_z[:].rearrange("p b m -> p (b m)")
-            nc.scalar.activation(z_rows[m0 // HALF][:, s - PACK, :], flat, ACT.Copy, scale=-1.0)
-
-        def combine_last(c):
-            m0 = CHUNK * c
-            page = pages[LAST % 2]
-            if c == 0:
-                x1 = keep.tile([P, CHUNK], F32, name="x1_first", tag="z_plain1", align_bytes=64)
-            else:
-                x1 = ring.tile([P, CHUNK], F32, name="x1")
-            nc.vector.tensor_copy(x1[:], page[:].indirect(entries(idx3, m0, CHUNK)))
-            if c == 0:
-                x2 = keep.tile([P, CHUNK], F32, name="x2_first", tag="z_plain0", align_bytes=64)
-            else:
-                x2 = ring.tile([P, CHUNK], F32, name="x2")
-            nc.vector.tensor_copy(x2[:], page[:].indirect(entries(idx4, m0, CHUNK)))
-            least = ring.tile([P, CHUNK], F32, name="least")
-            nc.vector.tensor_tensor(least[:], x1[:], x2[:], ALU.min)
-            rows = z_rows[m0 // HALF][:, :, m0 % HALF : m0 % HALF + CHUNK]
-            nc.vector.tensor_tensor(rows[:, LAST - PACK, :], least[:], evs[LAST][:, m0 : m0 + CHUNK], ALU.add)
-            weave = nc.vector.tensor_copy if c == CHUNKS - 1 else nc.scalar.copy
-            weave(
-                z_woven[c][:].rearrange("p (m i) t -> p m t i", i=PACK),
-                rows.rearrange("p t (m i) -> p m t i", i=PACK),
-            )
-
         z_mx = [[], []]
 
         def quantise_z(a, rounded):
             width = rounded.shape[1]
-            codes = ring.tile([P, width], U32, name="z_codes%d" % a, bufs=M // width, align_bytes=64)
-            plane = ring.tile([P, width], U8, name="z_plane%d" % a, bufs=M // width, align_bytes=64)
+            codes = keep.tile([P, width], U32, name="z_codes%d" % a, bufs=M // width, align_bytes=64)
+            plane = keep.tile([P, width], U8, name="z_plane%d" % a, bufs=M // width, align_bytes=64)
             nc.vector.quantize_mx(
                 out=codes[:].bitcast(FP8X4), scales=plane[:], in_=rounded[:].rearrange("p m t -> p (m t)")
             )
             z_mx[a].extend((codes[:, c0 : c0 + CHUNK], plane[:, c0 : c0 + CHUNK]) for c0 in range(0, width, CHUNK))
 
-        res_rows = []
+        def add_turned(target, term, first, start, stop):
+            for b in range(PACK):
+                nc.tensor.matmul(
+                    target[:, b, :], term[:, first + P * b : first + P * (b + 1)], ident[:],
+                    start=(start and b == 0), stop=(stop and b == PACK - 1), is_transpose=True,
+                )
+
+        def fetch(s):
+            page = pages[s % PAGES]
+            neg_x1, excess = [], []
+            for m0 in range(0, M, HALF):
+                x = keep.tile([P, HALF], F32, name="neg_x1", bufs=4)
+                nc.vector.tensor_tensor(x[:], page[:].indirect(entries(idx3, m0, HALF)), minus_one[:], ALU.mult)
+                neg_x1.append(x)
+            for half in range(2):
+                d = keep.tile([P, HALF], F32, name="difference", bufs=2)
+                nc.vector.tensor_tensor(
+                    d[:], page[:].indirect(entries(idx4, HALF * half, HALF)), neg_x1[half][:], ALU.add
+                )
+                r = keep.tile([P, HALF], F32, name="excess", bufs=2)
+                nc.scalar.activation(r[:], d[:], ACT.Relu, scale=-1.0)
+                neg_z = work_bank([P, PACK, P])
+                add_turned(neg_z, evs[s], HALF * half, True, False)
+                add_turned(neg_z, neg_x1[half], 0, False, False)
+                add_turned(neg_z, r, 0, False, True)
+                if s < PACK:
+                    nc.scalar.activation(z_turned[half][:, :, P * s : P * (s + 1)], neg_z[:], ACT.Copy, scale=-1.0)
+                else:
+                    rounded = keep.tile([P, PACK, P], BF16, name="z_half", bufs=2)
+                    nc.scalar.activation(rounded[:], neg_z[:], ACT.Copy, scale=-1.0)
+                    back = work_bank([P, PACK, P], BF16)
+                    for b in range(PACK):
+                        nc.tensor.transpose(back[:, b, :], rounded[:, b, :], ident_bf16[:])
+                    nc.scalar.copy(z_rows[half][:, s - PACK, :], back[:].rearrange("p b m -> p (b m)"))
+
+        def finish_plain(half):
+            z_plain = keep.tile([P, HALF, PACK], BF16, name="z_plain", tag="rounded%d" % half, align_bytes=64)
+            words = z_turned[half][:].bitcast(F32)
+            for pair in range(2):
+                back = work_bank([P, 2, 2, P])
+                for b in range(2):
+                    for h in range(2):
+                        nc.tensor.transpose(back[:, b, h, :], words[:, 2 * pair + b, h : 2 * P : 2], ident[:])
+                target = z_plain[:, CHUNK * pair : CHUNK * (pair + 1), :].bitcast(F32)
+                nc.scalar.copy(target.rearrange("p (b m) h -> p b m h", b=2), back[:].rearrange("p b h m -> p b m h"))
+            quantise_z(0, z_plain)
+
+        for s in range(LAST):
+            negate_ev(s)
+            if s == 1:
+                prepare_w1(3)
+            if s + 2 < SLICES:
+                ready[s + 2] = activations(s + 2)
+            scatter(s + 1, 0, *ready[s + 1])
+            fetch(s)
+            if s + PACK < SLICES:
+                evs.append(load_ev(s + PACK))
+            if s in (PACK, PACK + 1):
+                finish_plain(s - PACK)
 
         def multiply(y, a, c, pair):
             codes, plane = z_mx[a][c]
@@ -337,11 +318,9 @@ def tile_list_cousin_matcher_kernel(
                 )
 
         def open_scores(c):
-            banks = []
+            banks = [work_bank([P, 2, CHUNK]) for pair in range(2)]
             for pair in range(2):
-                y = bank([P, 2, CHUNK], at_end=(c == 0))
-                multiply(y, 0, c, pair)
-                banks.append(y)
+                multiply(banks[pair], 0, c, pair)
             return banks
 
         def close_scores(c):
@@ -349,58 +328,34 @@ def tile_list_cousin_matcher_kernel(
             for pair in range(2):
                 y = score_banks[c][pair]
                 multiply(y, 1, c, pair)
-                result = results[c // 2][:, 2 * (c % 2) + pair, :, :]
-                nc.vector.tensor_tensor(result, y[:], res_rows[pair][:, :, cols], ALU.add)
+                result = results[:, c, 2 * pair : 2 * pair + 2, :]
+                nc.vector.tensor_tensor(result, y[:], res_rows[:, 2 * pair : 2 * pair + 2, cols], ALU.add)
                 rows = out[2 * P * pair : 2 * P * (pair + 1), cols]
                 nc.sync.dma_start(rows.rearrange("(b p) m -> p b m", p=P), result)
 
-        scatter(0)
-        ready.append(activations(1))
-        prepare_plain(1)
-        ready.append(activations(2))
-        opening = keep.tile([P, 5, HALF], F32, name="opening", tag="opening", align_bytes=64)
-        early = combine(0, 0)
-        w1_woven = keep.tile([P, PACK, 2, P, PACK], BF16, name="w1_woven", tag="woven", align_bytes=64)
-        for s in range(LAST):
-            scatter(s + 1)
-            late = combine(s, HALF)
-            if s == 0:
-                for a in range(2):
-                    nc.scalar.copy(
-                        w1_woven[:, :, a, :, :].rearrange("p t c i -> p c t i"),
-                        w1_woven_raw[a][:].rearrange("p i (c t) -> p c t i", t=PACK),
-                    )
-                quantise_w1(PACK, w1_woven)
-                for pair in range(2):
-                    rows = ring.tile([P, 2, M], F32, name="res_rows", tag="half_wide")
-                    source = res[2 * P * pair : 2 * P * (pair + 1), :]
-                    nc.sync.dma_start(rows[:], source.rearrange("(b p) m -> p b m", p=P))
-                    res_rows.append(rows)
-            if s + 3 < SLICES:
-                ready.append(activations(s + 3))
-            if s >= PACK:
-                finish_woven(s, 0, *early)
-                finish_woven(s, HALF, *late)
-            for block in LATE_BLOCKS.get(s, ()):
-                finish_plain(block)
-            if s + PACK < SLICES:
-                evs.append(load_ev(s + PACK))
-            if s + 1 < LAST:
-                early = combine(s + 1, 0)
-            if s + 1 == PACK - 1:
-                for block in range(PACK):
-                    finish_plain(block)
+        def fetch_last(list_tile, c):
+            m0 = CHUNK * c
+            x = keep.tile([P, CHUNK], F32, name="x_last", bufs=4)
+            window = pages[LAST % PAGES][:].indirect(entries(list_tile, m0, CHUNK))
+            nc.vector.tensor_tensor(x[:], window, evs[LAST][:, m0 : m0 + CHUNK], ALU.add)
+            return x
 
-        for half in range(2):
-            quantise_z(0, z_plain[half])
-        results = [ring.tile([P, PACK, 2, CHUNK], F32, name="results", tag="placed") for half in range(2)]
-        score_banks = [open_scores(0)]
-        for step in range(CHUNKS + 2):
-            if step < CHUNKS:
-                combine_last(step)
-            if step + 1 < CHUNKS:
-                score_banks.append(open_scores(step + 1))
-            if 1 <= step <= CHUNKS:
-                quantise_z(1, z_woven[step - 1])
-            if step >= 2:
-                close_scores(step - 2)
+        def finish_last(c, x1, x2):
+            m0 = CHUNK * c
+            rows = z_rows[m0 // HALF][:, :, m0 % HALF : m0 % HALF + CHUNK]
+            nc.vector.tensor_tensor(rows[:, LAST - PACK, :], x1[:], x2[:], ALU.min)
+            z_woven = keep.tile([P, CHUNK, PACK], BF16, name="z_woven", bufs=CHUNKS, align_bytes=64)
+            weave = nc.vector.tensor_copy if c == CHUNKS - 1 else nc.scalar.copy
+            weave(
+                z_woven[:].rearrange("p (m i) t -> p m t i", i=PACK), rows.rearrange("p t (m i) -> p m t i", i=PACK)
+            )
+            return z_woven
+
+        score_banks = [open_scores(c) for c in range(CHUNKS)]
+        x1 = fetch_last(idx3, 0)
+        for c in range(CHUNKS):
+            x2 = fetch_last(idx4, c)
+            x1_next = fetch_last(idx3, c + 1) if c + 1 < CHUNKS else None
+            quantise_z(1, finish_last(c, x1, x2))
+            close_scores(c)
+            x1 = x1_next

@@ -31,6 +31,7 @@ PAGES = 3
 W1_GROUPS = ((0, 1), (1, 2), (2, 4), (4, 8))
 VECTOR_PAGES = 1
 BANKS = 8
+FIRST_PIECES = ((0, HALF), (HALF, HALF))
 
 
 def tile_list_cousin_matcher_kernel(
@@ -51,6 +52,9 @@ def tile_list_cousin_matcher_kernel(
 
         tab_plane = keep.tile([P, T], U8, name="tab_plane", align_bytes=64)
         nc.vector.memset(tab_plane[:].bitcast(I32), 0)
+        for q in range(P // QUADRANT):
+            rows = tab_plane[QUADRANT * q : QUADRANT * q + 2 * PACK, :]
+            nc.gpsimd.dma_start(rows.bitcast(I32), tab_scales[:, PACK * q : PACK * (q + 1), :].bitcast(I32))
         gain_rows = keep.tile([P, P], F32, name="gain_rows")
         nc.vector.memset(gain_rows[:], 0.0)
         w2_plane = keep.tile([P, 2, N], U8, name="w2_plane", align_bytes=64)
@@ -91,9 +95,6 @@ def tile_list_cousin_matcher_kernel(
 
         tabs = [load_table(0)]
         nc.sync.dma_start(idx[:], offs)
-        for q in range(P // QUADRANT):
-            rows = tab_plane[QUADRANT * q : QUADRANT * q + 2 * PACK, :]
-            nc.sync.dma_start(rows.bitcast(I32), tab_scales[:, PACK * q : PACK * (q + 1), :].bitcast(I32))
         w1_raw = [load_w1(0)]
         nc.sync.dma_start(gain_rows[0:PACK, :], gain[0:K_PASS].rearrange("(s p) -> s p", p=P))
         tabs.append(load_table(1))
@@ -179,9 +180,9 @@ def tile_list_cousin_matcher_kernel(
                 sigmoid = keep.tile([P, S], F32, name="sigmoid_held", tag="raw%d_1" % (2 + s // 2))
             else:
                 sigmoid = keep.tile([P, S], F32, name="sigmoid", bufs=2)
-            for j0 in range(0, S, HALF):
-                cols = slice(j0, j0 + HALF)
-                e_bank = work_bank([P, HALF])
+            for j0, count in FIRST_PIECES if s == 0 else ((0, HALF), (HALF, HALF)):
+                cols = slice(j0, j0 + count)
+                e_bank = work_bank([P, count])
                 for a in range(2):
                     nc.tensor.matmul_mx(
                         out=e_bank[:],
@@ -217,10 +218,9 @@ def tile_list_cousin_matcher_kernel(
             nc.scalar.activation(evs[s][:], evs[s][:], ACT.Copy, scale=-1.0)
 
         prepare_w1(0)
-        for j0 in range(0, S, HALF):
-            nc.vector.tensor_copy(
-                v_codes[1][:, j0 : j0 + HALF], tabs[1][:].bitcast(U32).indirect(entries(idx, j0, HALF))
-            )
+        for j0, count in FIRST_PIECES:
+            window = tabs[1][:].bitcast(U32).indirect(entries(idx, j0, count))
+            nc.vector.tensor_copy(v_codes[1][:, j0 : j0 + count], window)
         results = keep.tile([P, CHUNKS, N // P, CHUNK], F32, name="results", tag="tab1")
         sigmoid = sigmoid_of(0)
         scatter(0, 0, sigmoid, factor_of(0, 0, HALF, keep.tile([P, HALF], F32, name="factor", bufs=2)))

@@ -29,9 +29,7 @@ CHUNKS = M // CHUNK
 LAST = SLICES - 1
 PAGES = 3
 W1_GROUPS = ((0, 1), (1, 2), (2, 4), (4, 8))
-VECTOR_PAGES = 1
 BANKS = 8
-FIRST_PIECES = ((0, HALF), (HALF, HALF))
 
 
 def tile_list_cousin_matcher_kernel(
@@ -42,6 +40,7 @@ def tile_list_cousin_matcher_kernel(
     with ExitStack() as ctx:
         lists = ctx.enter_context(tc.tile_pool(name="lists", bufs=1))
         keep = ctx.enter_context(tc.tile_pool(name="keep", bufs=1))
+        shared = ctx.enter_context(tc.tile_pool(name="shared", bufs=1))
         psum = ctx.enter_context(tc.psum_pool(name="psum", bufs=1))
 
         def entries(list_tile, first, count):
@@ -50,7 +49,7 @@ def tile_list_cousin_matcher_kernel(
         def work_bank(shape, dtype=F32):
             return psum.tile(shape, dtype, name="work_bank", bufs=BANKS)
 
-        tab_plane = keep.tile([P, T], U8, name="tab_plane", align_bytes=64)
+        tab_plane = keep.tile([P, T], U8, name="tab_plane", tag="plane_then_words", align_bytes=64)
         nc.vector.memset(tab_plane[:].bitcast(I32), 0)
         for q in range(P // QUADRANT):
             rows = tab_plane[QUADRANT * q : QUADRANT * q + 2 * PACK, :]
@@ -65,13 +64,8 @@ def tile_list_cousin_matcher_kernel(
         make_identity(nc, ident[:])
         ident_bf16 = keep.tile([P, P], BF16, name="ident_bf16")
         make_identity(nc, ident_bf16[:])
-        pages = [keep.tile([P, T2], F32, name="page%d" % s) for s in range(PAGES)]
-        for s, page in enumerate(pages):
-            if s < VECTOR_PAGES:
-                nc.vector.memset(page[:], 0.0)
-            else:
-                for c0 in range(0, T2, HALF):
-                    nc.gpsimd.memset(page[:, c0 : c0 + HALF], 0.0)
+        pages = [keep.tile([P, T2], F32, name="page0")]
+        nc.vector.memset(pages[0][:], 0.0)
 
         idx = lists.tile([P, S // STRIPE], U16, name="idx")
         idx2 = lists.tile([P, S // STRIPE], U16, name="idx2")
@@ -79,7 +73,10 @@ def tile_list_cousin_matcher_kernel(
         idx4 = lists.tile([P, M // STRIPE], U16, name="idx4")
 
         def load_table(a):
-            words = keep.tile([P, T], I32, name="tab", tag="tab%d" % a)
+            if a == 0:
+                words = keep.tile([P, T], I32, name="tab", tag="tab0")
+            else:
+                words = shared.tile([P, T], I32, name="tab1", offset=0)
             nc.sync.dma_start(words[:], tab_words[a].rearrange("p t i -> p (t i)").bitcast(I32))
             return words
 
@@ -138,10 +135,11 @@ def tile_list_cousin_matcher_kernel(
                 w2_scales[:, PACK * q : PACK * (q + 1), :].rearrange("a r c -> r a c").bitcast(I32),
             )
 
-        v_codes = [keep.tile([P, S], U32, name="v_codes%d" % a, align_bytes=64) for a in range(2)]
+        v_codes = [keep.tile([P, S], U32, name="v_codes0", align_bytes=64)]
         nc.vector.tensor_copy(v_codes[0][:], tabs[0][:].bitcast(U32).indirect(idx[:]))
         v_plane = keep.tile([P, S], U8, name="v_plane", align_bytes=64)
         nc.vector.tensor_copy(v_plane[:], tab_plane[:].indirect(idx[:]))
+        v_codes.append(keep.tile([P, S], U32, name="v_codes1", tag="plane_then_words", align_bytes=64))
         res_rows = keep.tile([P, N // P, M], F32, name="res_rows", tag="tab0")
         nc.sync.dma_start(res_rows[:], res.rearrange("(b p) m -> p b m", p=P))
 
@@ -180,9 +178,9 @@ def tile_list_cousin_matcher_kernel(
                 sigmoid = keep.tile([P, S], F32, name="sigmoid_held", tag="raw%d_1" % (2 + s // 2))
             else:
                 sigmoid = keep.tile([P, S], F32, name="sigmoid", bufs=2)
-            for j0, count in FIRST_PIECES if s == 0 else ((0, HALF), (HALF, HALF)):
-                cols = slice(j0, j0 + count)
-                e_bank = work_bank([P, count])
+            for j0 in range(0, S, HALF):
+                cols = slice(j0, j0 + HALF)
+                e_bank = work_bank([P, HALF])
                 for a in range(2):
                     nc.tensor.matmul_mx(
                         out=e_bank[:],
@@ -218,10 +216,14 @@ def tile_list_cousin_matcher_kernel(
             nc.scalar.activation(evs[s][:], evs[s][:], ACT.Copy, scale=-1.0)
 
         prepare_w1(0)
-        for j0, count in FIRST_PIECES:
-            window = tabs[1][:].bitcast(U32).indirect(entries(idx, j0, count))
-            nc.vector.tensor_copy(v_codes[1][:, j0 : j0 + count], window)
-        results = keep.tile([P, CHUNKS, N // P, CHUNK], F32, name="results", tag="tab1")
+        for j0 in range(0, S, HALF):
+            window = tabs[1][:].bitcast(U32).indirect(entries(idx, j0, HALF))
+            nc.vector.tensor_copy(v_codes[1][:, j0 : j0 + HALF], window)
+        for n in range(1, PAGES):
+            pages.append(shared.tile([P, T2], F32, name="page%d" % n, offset=4 * T2 * (n - 1)))
+            for c0 in range(0, T2, HALF):
+                nc.gpsimd.memset(pages[n][:, c0 : c0 + HALF], 0.0)
+        results = keep.tile([P, CHUNKS, N // P, CHUNK], F32, name="results")
         sigmoid = sigmoid_of(0)
         scatter(0, 0, sigmoid, factor_of(0, 0, HALF, keep.tile([P, HALF], F32, name="factor", bufs=2)))
         prepare_w1(1)

@@ -41,6 +41,7 @@ def tile_list_cousin_matcher_kernel(
         lists = ctx.enter_context(tc.tile_pool(name="lists", bufs=1))
         keep = ctx.enter_context(tc.tile_pool(name="keep", bufs=1))
         shared = ctx.enter_context(tc.tile_pool(name="shared", bufs=1))
+        late = ctx.enter_context(tc.tile_pool(name="late", bufs=1))
         psum = ctx.enter_context(tc.psum_pool(name="psum", bufs=1))
 
         def entries(list_tile, first, count):
@@ -51,14 +52,11 @@ def tile_list_cousin_matcher_kernel(
 
         tab_plane = keep.tile([P, T], U8, name="tab_plane", tag="plane_then_words", align_bytes=64)
         nc.vector.memset(tab_plane[:].bitcast(I32), 0)
-        for q in range(P // QUADRANT):
-            rows = tab_plane[QUADRANT * q : QUADRANT * q + 2 * PACK, :]
-            nc.gpsimd.dma_start(rows.bitcast(I32), tab_scales[:, PACK * q : PACK * (q + 1), :].bitcast(I32))
         gain_rows = keep.tile([P, P], F32, name="gain_rows")
         nc.vector.memset(gain_rows[:], 0.0)
         w2_plane = keep.tile([P, 2, N], U8, name="w2_plane", align_bytes=64)
         nc.vector.memset(w2_plane[:].rearrange("p a c -> p (a c)").bitcast(I32), 0)
-        minus_one = keep.tile([P, HALF], F32, name="minus_one")
+        minus_one = keep.tile([P, M], F32, name="minus_one")
         nc.vector.memset(minus_one[:], -1.0)
         ident = keep.tile([P, P], F32, name="ident")
         make_identity(nc, ident[:])
@@ -84,7 +82,11 @@ def tile_list_cousin_matcher_kernel(
             first, last = W1_GROUPS[g]
             raws = []
             for a in range(2):
-                raw = keep.tile([P, PACK, P * (last - first)], F32, name="w1_raw", tag="raw%d_%d" % (g, a))
+                shape = [P, PACK, P * (last - first)]
+                if (g, a) == (2, 1):
+                    raw = shared.tile(shape, F32, name="w1_raw_held", offset=4 * T + 2 * S)
+                else:
+                    raw = keep.tile(shape, F32, name="w1_raw", tag="raw%d_%d" % (g, a))
                 rows = w1[K_PASS * a : K_PASS * (a + 1), P * first : P * last]
                 nc.sync.dma_start(raw[:], rows.rearrange("(p i) c -> p i c", i=PACK))
                 raws.append(raw)
@@ -92,6 +94,9 @@ def tile_list_cousin_matcher_kernel(
 
         tabs = [load_table(0)]
         nc.sync.dma_start(idx[:], offs)
+        for q in range(P // QUADRANT):
+            rows = tab_plane[QUADRANT * q : QUADRANT * q + 2 * PACK, :]
+            nc.sync.dma_start(rows.bitcast(I32), tab_scales[:, PACK * q : PACK * (q + 1), :].bitcast(I32))
         w1_raw = [load_w1(0)]
         nc.sync.dma_start(gain_rows[0:PACK, :], gain[0:K_PASS].rearrange("(s p) -> s p", p=P))
         tabs.append(load_table(1))
@@ -119,8 +124,8 @@ def tile_list_cousin_matcher_kernel(
                 nc.sync.dma_start(rows[QUADRANT * q : QUADRANT * (q + 1), :, :], source)
             return [rows[:, 0, :], rows[:, 1, :]]
 
-        evs = [load_ev(0)]
         w1_raw.append(load_w1(3))
+        evs = [load_ev(0)]
         gain_woven = keep.tile([P, PACK], F32, name="gain_woven")
         nc.sync.dma_start(gain_woven[:], gain[K_PASS:].rearrange("(p t) -> p t", t=PACK))
         evs.append(load_ev(1))
@@ -174,8 +179,10 @@ def tile_list_cousin_matcher_kernel(
             )
 
         def sigmoid_of(s):
-            if s in (1, 3):
-                sigmoid = keep.tile([P, S], F32, name="sigmoid_held", tag="raw%d_1" % (2 + s // 2))
+            if s == 1:
+                sigmoid = shared.tile([P, S], F32, name="sigmoid_first", offset=4 * T)
+            elif s == 3:
+                sigmoid = keep.tile([P, S], F32, name="sigmoid_held", tag="raw3_1")
             else:
                 sigmoid = keep.tile([P, S], F32, name="sigmoid", bufs=2)
             for j0 in range(0, S, HALF):
@@ -194,23 +201,28 @@ def tile_list_cousin_matcher_kernel(
                 nc.scalar.activation(sigmoid[:, cols], e_bank[:], ACT.Sigmoid)
             return sigmoid
 
-        def factor_of(s, j0, count, factor):
-            if s < PACK:
-                weights, scale = wgs_rows[:], gain_plain[:, s : s + 1]
-            else:
-                weights, scale = wgs_woven[s - PACK], gain_woven[:, s - PACK : s - PACK + 1]
-            nc.scalar.activation(factor[:], weights[:, j0 : j0 + count], ACT.Copy, scale=scale)
-            return factor
-
         def activations(s):
-            sigmoid = sigmoid_of(s)
-            return sigmoid, factor_of(s, 0, S, keep.tile([P, S], F32, name="factor", bufs=2))
+            edge = 4 * M * (1 + (s - 1) % 2)
+            column = late.tile([P, 16], F32, name="gain_column%d" % s, offset=edge - 32)[:, 0:1]
+            if s < PACK:
+                weights = wgs_rows[:]
+                nc.scalar.copy(column, gain_plain[:, s : s + 1])
+            else:
+                weights = wgs_woven[s - PACK]
+                nc.scalar.copy(column, gain_woven[:, s - PACK : s - PACK + 1])
+            h = sigmoid_of(s)
+            for j0 in range(0, S, HALF):
+                nc.scalar.activation(h[:, j0 : j0 + HALF], h[:, j0 : j0 + HALF], ACT.Copy, scale=column)
+            return h[:], weights
 
-        def scatter(s, j0, sigmoid, factor):
-            count = factor.shape[1]
-            nc.vector.tensor_tensor(
-                pages[s % PAGES][:].indirect(entries(idx2, j0, count)), sigmoid[:, j0 : j0 + count], factor[:], ALU.mult
-            )
+        def scatter(s, j0, left, right):
+            window = pages[s % PAGES][:].indirect(entries(idx2, j0, left.shape[1]))
+            nc.vector.tensor_tensor(window, left, right, ALU.mult)
+
+        def first_factor(j0, tag):
+            factor = keep.tile([P, HALF], F32, name="factor", tag=tag)
+            nc.scalar.activation(factor[:], wgs_rows[:, j0 : j0 + HALF], ACT.Copy, scale=gain_plain[:, 0:1])
+            return factor[:]
 
         def negate_ev(s):
             nc.scalar.activation(evs[s][:], evs[s][:], ACT.Copy, scale=-1.0)
@@ -223,13 +235,12 @@ def tile_list_cousin_matcher_kernel(
             pages.append(shared.tile([P, T2], F32, name="page%d" % n, offset=4 * T2 * (n - 1)))
             for c0 in range(0, T2, HALF):
                 nc.gpsimd.memset(pages[n][:, c0 : c0 + HALF], 0.0)
-        results = keep.tile([P, CHUNKS, N // P, CHUNK], F32, name="results")
         sigmoid = sigmoid_of(0)
-        scatter(0, 0, sigmoid, factor_of(0, 0, HALF, keep.tile([P, HALF], F32, name="factor", bufs=2)))
+        scatter(0, 0, sigmoid[:, 0:HALF], first_factor(0, "factor"))
         prepare_w1(1)
-        scatter(0, HALF, sigmoid, factor_of(0, HALF, HALF, keep.tile([P, HALF], F32, name="factor_held", tag="raw1_1")))
+        scatter(0, HALF, sigmoid[:, HALF:], first_factor(HALF, "raw1_0"))
         prepare_w1(2)
-        ready = {1: activations(1)}
+        ready = {s: activations(s) for s in (1, 2)}
 
         z_turned = [keep.tile([P, PACK, K_PASS], BF16, name="z_turned%d" % half) for half in range(2)]
         z_rows = [keep.tile([P, PACK, HALF], BF16, name="z_rows%d" % half) for half in range(2)]
@@ -251,24 +262,29 @@ def tile_list_cousin_matcher_kernel(
                     start=(start and b == 0), stop=(stop and b == PACK - 1), is_transpose=True,
                 )
 
-        def fetch(s):
+        def fetch_first(s):
+            if s == 0:
+                neg_x1 = shared.tile([P, M], F32, name="neg_x1_first", offset=4 * T + 4 * S)
+            else:
+                neg_x1 = keep.tile([P, M], F32, name="neg_x1", bufs=2)
+            nc.vector.tensor_tensor(neg_x1[:], pages[s % PAGES][:].indirect(idx3[:]), minus_one[:], ALU.mult)
+            return neg_x1
+
+        def fetch_second(s, neg_x1):
             page = pages[s % PAGES]
-            neg_x1, excess = [], []
-            for m0 in range(0, M, HALF):
-                x = keep.tile([P, HALF], F32, name="neg_x1", bufs=4)
-                nc.vector.tensor_tensor(x[:], page[:].indirect(entries(idx3, m0, HALF)), minus_one[:], ALU.mult)
-                neg_x1.append(x)
+            d = late.tile([P, M], F32, name="difference%d" % s, offset=8 * M * (s % 2))
+            r = late.tile([P, M], F32, name="excess%d" % s, offset=4 * M)
+            piece = HALF if s == LAST - 1 else M
+            for m0 in range(0, M, piece):
+                cols = slice(m0, m0 + piece)
+                nc.vector.tensor_tensor(d[:, cols], page[:].indirect(entries(idx4, m0, piece)), neg_x1[:, cols], ALU.add)
             for half in range(2):
-                d = keep.tile([P, HALF], F32, name="difference", bufs=2)
-                nc.vector.tensor_tensor(
-                    d[:], page[:].indirect(entries(idx4, HALF * half, HALF)), neg_x1[half][:], ALU.add
-                )
-                r = keep.tile([P, HALF], F32, name="excess", bufs=2)
-                nc.scalar.activation(r[:], d[:], ACT.Relu, scale=-1.0)
+                cols = slice(HALF * half, HALF * (half + 1))
+                nc.scalar.activation(r[:, cols], d[:, cols], ACT.Relu, scale=-1.0)
                 neg_z = work_bank([P, PACK, P])
                 add_turned(neg_z, evs[s], HALF * half, True, False)
-                add_turned(neg_z, neg_x1[half], 0, False, False)
-                add_turned(neg_z, r, 0, False, True)
+                add_turned(neg_z, neg_x1, HALF * half, False, False)
+                add_turned(neg_z, r, HALF * half, False, True)
                 if s < PACK:
                     nc.scalar.activation(z_turned[half][:, :, P * s : P * (s + 1)], neg_z[:], ACT.Copy, scale=-1.0)
                 else:
@@ -291,18 +307,21 @@ def tile_list_cousin_matcher_kernel(
                 nc.scalar.copy(target.rearrange("p (b m) h -> p b m h", b=2), back[:].rearrange("p b h m -> p b m h"))
             quantise_z(0, z_plain)
 
+        negate_ev(0)
         for s in range(LAST):
-            negate_ev(s)
-            if s == 1:
-                prepare_w1(3)
-            if s + 2 < SLICES:
-                ready[s + 2] = activations(s + 2)
+            neg_x1 = fetch_first(s)
             scatter(s + 1, 0, *ready[s + 1])
-            fetch(s)
+            fetch_second(s, neg_x1)
             if s + PACK < SLICES:
                 evs.append(load_ev(s + PACK))
-            if s in (PACK, PACK + 1):
-                finish_plain(s - PACK)
+            if s == 0:
+                prepare_w1(3)
+            if s in (PACK - 1, PACK):
+                finish_plain(s - PACK + 1)
+            if s + 1 < LAST:
+                negate_ev(s + 1)
+            if s + 3 < SLICES:
+                ready[s + 3] = activations(s + 3)
 
         def multiply(y, a, c, pair):
             codes, plane = z_mx[a][c]
@@ -330,7 +349,7 @@ def tile_list_cousin_matcher_kernel(
             for pair in range(2):
                 y = score_banks[c][pair]
                 multiply(y, 1, c, pair)
-                result = results[:, c, 2 * pair : 2 * pair + 2, :]
+                result = results[c // 2][:, c % 2, 2 * pair : 2 * pair + 2, :]
                 nc.vector.tensor_tensor(result, y[:], res_rows[:, 2 * pair : 2 * pair + 2, cols], ALU.add)
                 rows = out[2 * P * pair : 2 * P * (pair + 1), cols]
                 nc.sync.dma_start(rows.rearrange("(b p) m -> p b m", p=P), result)
@@ -353,6 +372,7 @@ def tile_list_cousin_matcher_kernel(
             )
             return z_woven
 
+        results = [keep.tile([P, 2, N // P, CHUNK], F32, name="results", tag="raw3_%d" % n) for n in range(2)]
         score_banks = [open_scores(c) for c in range(CHUNKS)]
         x1 = fetch_last(idx3, 0)
         for c in range(CHUNKS):

@@ -52,6 +52,8 @@ def tile_list_cousin_matcher_kernel(
 
         tab_plane = keep.tile([P, T], U8, name="tab_plane", tag="plane_then_words", align_bytes=64)
         nc.vector.memset(tab_plane[:].bitcast(I32), 0)
+        v_plane = keep.tile([P, S], U8, name="v_plane", align_bytes=64)
+        nc.vector.memset(v_plane[:].bitcast(I32), 0)
         gain_rows = keep.tile([P, P], F32, name="gain_rows")
         nc.vector.memset(gain_rows[:], 0.0)
         w2_plane = keep.tile([P, 2, N], U8, name="w2_plane", align_bytes=64)
@@ -94,9 +96,9 @@ def tile_list_cousin_matcher_kernel(
 
         tabs = [load_table(0)]
         nc.sync.dma_start(idx[:], offs)
-        for q in range(P // QUADRANT):
-            rows = tab_plane[QUADRANT * q : QUADRANT * q + 2 * PACK, :]
-            nc.sync.dma_start(rows.bitcast(I32), tab_scales[:, PACK * q : PACK * (q + 1), :].bitcast(I32))
+        for a in range(2):
+            rows = tab_plane[P // 2 * a : P // 2 * (a + 1) : PACK, :]
+            nc.sync.dma_start(rows.bitcast(I32), tab_scales[a].rearrange("(q r) t -> r q t", r=PACK).bitcast(I32))
         w1_raw = [load_w1(0)]
         nc.sync.dma_start(gain_rows[0:PACK, :], gain[0:K_PASS].rearrange("(s p) -> s p", p=P))
         tabs.append(load_table(1))
@@ -142,8 +144,13 @@ def tile_list_cousin_matcher_kernel(
 
         v_codes = [keep.tile([P, S], U32, name="v_codes0", align_bytes=64)]
         nc.vector.tensor_copy(v_codes[0][:], tabs[0][:].bitcast(U32).indirect(idx[:]))
-        v_plane = keep.tile([P, S], U8, name="v_plane", align_bytes=64)
-        nc.vector.tensor_copy(v_plane[:], tab_plane[:].indirect(idx[:]))
+        v_spread = keep.tile([P, S], U8, name="v_spread", align_bytes=64)
+        nc.vector.tensor_copy(v_spread[:], tab_plane[:].indirect(idx[:]))
+        for q in range(P // QUADRANT):
+            nc.scalar.dma_start(
+                v_plane[QUADRANT * q : QUADRANT * q + 2 * PACK, :].bitcast(I32),
+                v_spread[PACK * q : P : PACK * PACK, :].bitcast(I32),
+            )
         v_codes.append(keep.tile([P, S], U32, name="v_codes1", tag="plane_then_words", align_bytes=64))
         res_rows = keep.tile([P, N // P, M], F32, name="res_rows", tag="tab0")
         nc.sync.dma_start(res_rows[:], res.rearrange("(b p) m -> p b m", p=P))

@@ -30,6 +30,7 @@ LAST = SLICES - 1
 PAGES = 3
 W1_GROUPS = ((0, 1), (1, 2), (2, 4), (4, 8))
 BANKS = 8
+FIRST_PIECES = ((0, CHUNK), (CHUNK, CHUNK), (HALF, HALF))
 
 
 def tile_list_cousin_matcher_kernel(
@@ -142,8 +143,6 @@ def tile_list_cousin_matcher_kernel(
                 w2_scales[:, PACK * q : PACK * (q + 1), :].rearrange("a r c -> r a c").bitcast(I32),
             )
 
-        v_codes = [keep.tile([P, S], U32, name="v_codes0", align_bytes=64)]
-        nc.vector.tensor_copy(v_codes[0][:], tabs[0][:].bitcast(U32).indirect(idx[:]))
         v_spread = keep.tile([P, S], U8, name="v_spread", align_bytes=64)
         nc.vector.tensor_copy(v_spread[:], tab_plane[:].indirect(idx[:]))
         for q in range(P // QUADRANT):
@@ -151,7 +150,11 @@ def tile_list_cousin_matcher_kernel(
                 v_plane[QUADRANT * q : QUADRANT * q + 2 * PACK, :].bitcast(I32),
                 v_spread[PACK * q : P : PACK * PACK, :].bitcast(I32),
             )
-        v_codes.append(keep.tile([P, S], U32, name="v_codes1", tag="plane_then_words", align_bytes=64))
+        v_codes = [
+            keep.tile([P, S], U32, name="v_codes0", tag="plane_then_words", align_bytes=64),
+            keep.tile([P, S], U32, name="v_codes1", align_bytes=64),
+        ]
+        nc.vector.tensor_copy(v_codes[0][:], tabs[0][:].bitcast(U32).indirect(idx[:]))
         res_rows = keep.tile([P, N // P, M], F32, name="res_rows", tag="tab0")
         nc.sync.dma_start(res_rows[:], res.rearrange("(b p) m -> p b m", p=P))
 
@@ -192,9 +195,9 @@ def tile_list_cousin_matcher_kernel(
                 sigmoid = keep.tile([P, S], F32, name="sigmoid_held", tag="raw3_1")
             else:
                 sigmoid = keep.tile([P, S], F32, name="sigmoid", bufs=2)
-            for j0 in range(0, S, HALF):
-                cols = slice(j0, j0 + HALF)
-                e_bank = work_bank([P, HALF])
+            for j0, count in FIRST_PIECES if s == 0 else ((0, HALF), (HALF, HALF)):
+                cols = slice(j0, j0 + count)
+                e_bank = work_bank([P, count])
                 for a in range(2):
                     nc.tensor.matmul_mx(
                         out=e_bank[:],
@@ -250,12 +253,12 @@ def tile_list_cousin_matcher_kernel(
         ready = {s: activations(s) for s in (1, 2)}
 
         z_turned = [keep.tile([P, PACK, K_PASS], BF16, name="z_turned%d" % half) for half in range(2)]
-        z_rows = [keep.tile([P, PACK, HALF], BF16, name="z_rows%d" % half) for half in range(2)]
+        z_rows = [keep.tile([P, PACK, CHUNK], BF16, name="z_rows%d" % c) for c in range(CHUNKS)]
         z_mx = [[], []]
 
         def quantise_z(a, rounded):
             width = rounded.shape[1]
-            codes = keep.tile([P, width], U32, name="z_codes%d" % a, bufs=M // width, align_bytes=64)
+            codes = keep.tile([P, width], U32, name="z_codes%d" % a, bufs=2, align_bytes=64)
             plane = keep.tile([P, width], U8, name="z_plane%d" % a, bufs=M // width, align_bytes=64)
             nc.vector.quantize_mx(
                 out=codes[:].bitcast(FP8X4), scales=plane[:], in_=rounded[:].rearrange("p m t -> p (m t)")
@@ -274,17 +277,22 @@ def tile_list_cousin_matcher_kernel(
                 neg_x1 = shared.tile([P, M], F32, name="neg_x1_first", offset=4 * T + 4 * S)
             else:
                 neg_x1 = keep.tile([P, M], F32, name="neg_x1", bufs=2)
-            nc.vector.tensor_tensor(neg_x1[:], pages[s % PAGES][:].indirect(idx3[:]), minus_one[:], ALU.mult)
+            piece = HALF if s == LAST - 1 else M
+            for m0 in range(0, M, piece):
+                window = pages[s % PAGES][:].indirect(entries(idx3, m0, piece))
+                nc.vector.tensor_tensor(neg_x1[:, m0 : m0 + piece], window, minus_one[:, 0:piece], ALU.mult)
             return neg_x1
 
         def fetch_second(s, neg_x1):
-            page = pages[s % PAGES]
-            d = late.tile([P, M], F32, name="difference%d" % s, offset=8 * M * (s % 2))
+            if s < LAST - 1:
+                d = late.tile([P, M], F32, name="difference%d" % s, offset=8 * M * (s % 2))
+            else:
+                d = keep.tile([P, M], F32, name="difference_early")
             r = late.tile([P, M], F32, name="excess%d" % s, offset=4 * M)
             piece = HALF if s == LAST - 1 else M
             for m0 in range(0, M, piece):
-                cols = slice(m0, m0 + piece)
-                nc.vector.tensor_tensor(d[:, cols], page[:].indirect(entries(idx4, m0, piece)), neg_x1[:, cols], ALU.add)
+                window = pages[s % PAGES][:].indirect(entries(idx4, m0, piece))
+                nc.vector.tensor_tensor(d[:, m0 : m0 + piece], window, neg_x1[:, m0 : m0 + piece], ALU.add)
             for half in range(2):
                 cols = slice(HALF * half, HALF * (half + 1))
                 nc.scalar.activation(r[:, cols], d[:, cols], ACT.Relu, scale=-1.0)
@@ -295,12 +303,17 @@ def tile_list_cousin_matcher_kernel(
                 if s < PACK:
                     nc.scalar.activation(z_turned[half][:, :, P * s : P * (s + 1)], neg_z[:], ACT.Copy, scale=-1.0)
                 else:
-                    rounded = keep.tile([P, PACK, P], BF16, name="z_half", bufs=2)
+                    if (s, half) == (LAST - 1, 1):
+                        rounded = keep.tile([P, PACK, P], BF16, name="z_half_last", align_bytes=64)
+                    else:
+                        rounded = keep.tile([P, PACK, P], BF16, name="z_half", bufs=2)
                     nc.scalar.activation(rounded[:], neg_z[:], ACT.Copy, scale=-1.0)
                     back = work_bank([P, PACK, P], BF16)
                     for b in range(PACK):
                         nc.tensor.transpose(back[:, b, :], rounded[:, b, :], ident_bf16[:])
-                    nc.scalar.copy(z_rows[half][:, s - PACK, :], back[:].rearrange("p b m -> p (b m)"))
+                    for pair in range(2):
+                        source = back[:, 2 * pair : 2 * pair + 2, :].rearrange("p b m -> p (b m)")
+                        nc.scalar.copy(z_rows[2 * half + pair][:, s - PACK, :], source)
 
         def finish_plain(half):
             z_plain = keep.tile([P, HALF, PACK], BF16, name="z_plain", tag="rounded%d" % half, align_bytes=64)
@@ -317,8 +330,11 @@ def tile_list_cousin_matcher_kernel(
         negate_ev(0)
         for s in range(LAST):
             neg_x1 = fetch_first(s)
+            if s == LAST - 1:
+                fetch_second(s, neg_x1)
             scatter(s + 1, 0, *ready[s + 1])
-            fetch_second(s, neg_x1)
+            if s < LAST - 1:
+                fetch_second(s, neg_x1)
             if s + PACK < SLICES:
                 evs.append(load_ev(s + PACK))
             if s == 0:
@@ -361,30 +377,38 @@ def tile_list_cousin_matcher_kernel(
                 rows = out[2 * P * pair : 2 * P * (pair + 1), cols]
                 nc.sync.dma_start(rows.rearrange("(b p) m -> p b m", p=P), result)
 
-        def fetch_last(list_tile, c):
+        def fetch_last(list_tile, c, held=False):
             m0 = CHUNK * c
-            x = keep.tile([P, CHUNK], F32, name="x_last", bufs=4)
+            if held:
+                x = keep.tile([P, CHUNK], F32, name="x_held", tag="z_rows%d" % (c - 2))
+            else:
+                x = keep.tile([P, CHUNK], F32, name="x_last", bufs=4)
             window = pages[LAST % PAGES][:].indirect(entries(list_tile, m0, CHUNK))
             nc.vector.tensor_tensor(x[:], window, evs[LAST][:, m0 : m0 + CHUNK], ALU.add)
             return x
 
         def finish_last(c, x1, x2):
-            m0 = CHUNK * c
-            rows = z_rows[m0 // HALF][:, :, m0 % HALF : m0 % HALF + CHUNK]
+            rows = z_rows[c][:]
             nc.vector.tensor_tensor(rows[:, LAST - PACK, :], x1[:], x2[:], ALU.min)
-            z_woven = keep.tile([P, CHUNK, PACK], BF16, name="z_woven", bufs=CHUNKS, align_bytes=64)
-            weave = nc.vector.tensor_copy if c == CHUNKS - 1 else nc.scalar.copy
-            weave(
-                z_woven[:].rearrange("p (m i) t -> p m t i", i=PACK), rows.rearrange("p t (m i) -> p m t i", i=PACK)
+            z_woven = woven[c // 2][:, CHUNK * (c % 2) : CHUNK * (c % 2 + 1), :]
+            nc.scalar.copy(
+                z_woven.rearrange("p (m i) t -> p m t i", i=PACK), rows.rearrange("p t (m i) -> p m t i", i=PACK)
             )
             return z_woven
 
         results = [keep.tile([P, 2, N // P, CHUNK], F32, name="results", tag="raw3_%d" % n) for n in range(2)]
         score_banks = [open_scores(c) for c in range(CHUNKS)]
+        woven = [
+            keep.tile([P, HALF, PACK], BF16, name="z_woven", tag=tag, align_bytes=64) for tag in ("z_half_last", "rounded1")
+        ]
         x1 = fetch_last(idx3, 0)
         for c in range(CHUNKS):
-            x2 = fetch_last(idx4, c)
+            x2 = fetch_last(idx4, c, held=(c >= 2))
             x1_next = fetch_last(idx3, c + 1) if c + 1 < CHUNKS else None
-            quantise_z(1, finish_last(c, x1, x2))
-            close_scores(c)
+            z_woven = finish_last(c, x1, x2)
+            if c >= 2:
+                close_scores(c - 2)
+            quantise_z(1, z_woven)
             x1 = x1_next
+        for c in range(2, CHUNKS):
+            close_scores(c)

@@ -27,7 +27,7 @@ STRIPE = 16
 SLICES = H // P
 CHUNKS = M // CHUNK
 LAST = SLICES - 1
-PAGES = 3
+PAGES = 2
 W1_GROUPS = ((0, 1), (1, 2), (2, 4), (4, 8))
 BANKS = 8
 FIRST_PIECES = ((0, CHUNK), (CHUNK, CHUNK), (HALF, HALF))
@@ -65,8 +65,9 @@ def tile_list_cousin_matcher_kernel(
         make_identity(nc, ident[:])
         ident_bf16 = keep.tile([P, P], BF16, name="ident_bf16")
         make_identity(nc, ident_bf16[:])
-        pages = [keep.tile([P, T2], F32, name="page0")]
-        nc.vector.memset(pages[0][:], 0.0)
+        pages = [keep.tile([P, T2], F32, name="page%d" % n) for n in range(PAGES)]
+        for page in pages:
+            nc.vector.memset(page[:], 0.0)
 
         idx = lists.tile([P, S // STRIPE], U16, name="idx")
         idx2 = lists.tile([P, S // STRIPE], U16, name="idx2")
@@ -74,10 +75,7 @@ def tile_list_cousin_matcher_kernel(
         idx4 = lists.tile([P, M // STRIPE], U16, name="idx4")
 
         def load_table(a):
-            if a == 0:
-                words = keep.tile([P, T], I32, name="tab", tag="tab0")
-            else:
-                words = shared.tile([P, T], I32, name="tab1", offset=0)
+            words = keep.tile([P, T], I32, name="tab", tag="tab%d" % a)
             nc.sync.dma_start(words[:], tab_words[a].rearrange("p t i -> p (t i)").bitcast(I32))
             return words
 
@@ -87,7 +85,7 @@ def tile_list_cousin_matcher_kernel(
             for a in range(2):
                 shape = [P, PACK, P * (last - first)]
                 if (g, a) == (2, 1):
-                    raw = shared.tile(shape, F32, name="w1_raw_held", offset=4 * T + 2 * S)
+                    raw = shared.tile(shape, F32, name="w1_raw_held", offset=2 * S)
                 else:
                     raw = keep.tile(shape, F32, name="w1_raw", tag="raw%d_%d" % (g, a))
                 rows = w1[K_PASS * a : K_PASS * (a + 1), P * first : P * last]
@@ -190,7 +188,7 @@ def tile_list_cousin_matcher_kernel(
 
         def sigmoid_of(s):
             if s == 1:
-                sigmoid = shared.tile([P, S], F32, name="sigmoid_first", offset=4 * T)
+                sigmoid = shared.tile([P, S], F32, name="sigmoid_first", offset=0)
             elif s == 3:
                 sigmoid = keep.tile([P, S], F32, name="sigmoid_held", tag="raw3_1")
             else:
@@ -241,10 +239,6 @@ def tile_list_cousin_matcher_kernel(
         for j0 in range(0, S, HALF):
             window = tabs[1][:].bitcast(U32).indirect(entries(idx, j0, HALF))
             nc.vector.tensor_copy(v_codes[1][:, j0 : j0 + HALF], window)
-        for n in range(1, PAGES):
-            pages.append(shared.tile([P, T2], F32, name="page%d" % n, offset=4 * T2 * (n - 1)))
-            for c0 in range(0, T2, HALF):
-                nc.gpsimd.memset(pages[n][:, c0 : c0 + HALF], 0.0)
         sigmoid = sigmoid_of(0)
         scatter(0, 0, sigmoid[:, 0:HALF], first_factor(0, "factor"))
         prepare_w1(1)
@@ -274,7 +268,7 @@ def tile_list_cousin_matcher_kernel(
 
         def fetch_first(s):
             if s == 0:
-                neg_x1 = shared.tile([P, M], F32, name="neg_x1_first", offset=4 * T + 4 * S)
+                neg_x1 = shared.tile([P, M], F32, name="neg_x1_first", offset=4 * S)
             else:
                 neg_x1 = keep.tile([P, M], F32, name="neg_x1", bufs=2)
             piece = HALF if s == LAST - 1 else M
@@ -377,19 +371,9 @@ def tile_list_cousin_matcher_kernel(
                 rows = out[2 * P * pair : 2 * P * (pair + 1), cols]
                 nc.sync.dma_start(rows.rearrange("(b p) m -> p b m", p=P), result)
 
-        def fetch_last(list_tile, c, held=False):
-            m0 = CHUNK * c
-            if held:
-                x = keep.tile([P, CHUNK], F32, name="x_held", tag="z_rows%d" % (c - 2))
-            else:
-                x = keep.tile([P, CHUNK], F32, name="x_last", bufs=4)
-            window = pages[LAST % PAGES][:].indirect(entries(list_tile, m0, CHUNK))
-            nc.vector.tensor_tensor(x[:], window, evs[LAST][:, m0 : m0 + CHUNK], ALU.add)
-            return x
-
         def finish_last(c, x1, x2):
             rows = z_rows[c][:]
-            nc.vector.tensor_tensor(rows[:, LAST - PACK, :], x1[:], x2[:], ALU.min)
+            nc.vector.tensor_tensor(rows[:, LAST - PACK, :], x1, x2, ALU.min)
             z_woven = woven[c // 2][:, CHUNK * (c % 2) : CHUNK * (c % 2 + 1), :]
             nc.scalar.copy(
                 z_woven.rearrange("p (m i) t -> p m t i", i=PACK), rows.rearrange("p t (m i) -> p m t i", i=PACK)
@@ -401,14 +385,24 @@ def tile_list_cousin_matcher_kernel(
         woven = [
             keep.tile([P, HALF, PACK], BF16, name="z_woven", tag=tag, align_bytes=64) for tag in ("z_half_last", "rounded1")
         ]
-        x1 = fetch_last(idx3, 0)
+        def fetch_pair(c):
+            if c == CHUNKS - 1:
+                x = keep.tile([P, 2, CHUNK], F32, name="x_held", tag="z_rows0")
+            else:
+                x = keep.tile([P, 2, CHUNK], F32, name="x_last", bufs=CHUNKS - 1)
+            m0 = CHUNK * c
+            for n, list_tile in enumerate((idx3, idx4)):
+                window = pages[LAST % PAGES][:].indirect(entries(list_tile, m0, CHUNK))
+                nc.vector.tensor_tensor(x[:, n, :], window, evs[LAST][:, m0 : m0 + CHUNK], ALU.add)
+            return x
+
+        pairs = [fetch_pair(0), fetch_pair(1)]
         for c in range(CHUNKS):
-            x2 = fetch_last(idx4, c, held=(c >= 2))
-            x1_next = fetch_last(idx3, c + 1) if c + 1 < CHUNKS else None
-            z_woven = finish_last(c, x1, x2)
+            z_woven = finish_last(c, pairs[c][:, 0, :], pairs[c][:, 1, :])
             if c >= 2:
                 close_scores(c - 2)
             quantise_z(1, z_woven)
-            x1 = x1_next
+            if c == 0:
+                pairs.extend(fetch_pair(n) for n in (2, 3))
         for c in range(2, CHUNKS):
             close_scores(c)

@@ -103,6 +103,13 @@ def tile_list_cousin_matcher_kernel(
         tabs.append(load_table(1))
         wgs_rows = keep.tile([P, S], F32, name="wgs_rows")
         nc.sync.dma_start(wgs_rows[:, 0:HALF], wgs[:, 0:HALF])
+        v_spread = keep.tile([P, S], U8, name="v_spread", align_bytes=64)
+        nc.vector.tensor_copy(v_spread[:], tab_plane[:].indirect(idx[:]))
+        for q in range(P // QUADRANT):
+            nc.sync.dma_start(
+                v_plane[QUADRANT * q : QUADRANT * q + 2 * PACK, :].bitcast(I32),
+                v_spread[PACK * q : P : PACK * PACK, :].bitcast(I32),
+            )
         nc.sync.dma_start(idx2[:], offs2)
         w1_raw.append(load_w1(1))
         nc.sync.dma_start(wgs_rows[:, HALF:], wgs[:, HALF:])
@@ -141,13 +148,6 @@ def tile_list_cousin_matcher_kernel(
                 w2_scales[:, PACK * q : PACK * (q + 1), :].rearrange("a r c -> r a c").bitcast(I32),
             )
 
-        v_spread = keep.tile([P, S], U8, name="v_spread", align_bytes=64)
-        nc.vector.tensor_copy(v_spread[:], tab_plane[:].indirect(idx[:]))
-        for q in range(P // QUADRANT):
-            nc.scalar.dma_start(
-                v_plane[QUADRANT * q : QUADRANT * q + 2 * PACK, :].bitcast(I32),
-                v_spread[PACK * q : P : PACK * PACK, :].bitcast(I32),
-            )
         v_codes = [
             keep.tile([P, S], U32, name="v_codes0", tag="plane_then_words", align_bytes=64),
             keep.tile([P, S], U32, name="v_codes1", align_bytes=64),

@@ -69,6 +69,9 @@ def tile_list_cousin_matcher_kernel(
         for page in pages:
             nc.vector.memset(page[:], 0.0)
 
+        warm = keep.tile([P, 1], F32, name="warm")
+        nc.scalar.activation(warm[:], ident[:, 0:1], ACT.Sigmoid)
+
         idx = lists.tile([P, S // STRIPE], U16, name="idx")
         idx2 = lists.tile([P, S // STRIPE], U16, name="idx2")
         idx3 = lists.tile([P, M // STRIPE], U16, name="idx3")

@@ -51,8 +51,8 @@ def tile_list_cousin_matcher_kernel(
         def work_bank(shape, dtype=F32):
             return psum.tile(shape, dtype, name="work_bank", bufs=BANKS)
 
-        tab_plane = keep.tile([P, T], U8, name="tab_plane", tag="plane_then_words", align_bytes=64)
-        nc.vector.memset(tab_plane[:].bitcast(I32), 0)
+        tab_plane = keep.tile([P, T], U8, name="tab_plane", tag="plane_then_page", align_bytes=64)
+        nc.gpsimd.memset(tab_plane[:].bitcast(I32), 0)
         v_plane = keep.tile([P, S], U8, name="v_plane", align_bytes=64)
         nc.vector.memset(v_plane[:].bitcast(I32), 0)
         gain_rows = keep.tile([P, P], F32, name="gain_rows")
@@ -60,60 +60,68 @@ def tile_list_cousin_matcher_kernel(
         w2_plane = keep.tile([P, 2, N], U8, name="w2_plane", align_bytes=64)
         nc.vector.memset(w2_plane[:].rearrange("p a c -> p (a c)").bitcast(I32), 0)
         minus_one = keep.tile([P, M], F32, name="minus_one")
-        nc.vector.memset(minus_one[:], -1.0)
         ident = keep.tile([P, P], F32, name="ident")
         make_identity(nc, ident[:])
         ident_bf16 = keep.tile([P, P], BF16, name="ident_bf16")
         make_identity(nc, ident_bf16[:])
-        pages = [keep.tile([P, T2], F32, name="page%d" % n) for n in range(PAGES)]
-        for page in pages:
-            nc.vector.memset(page[:], 0.0)
+        pages = [keep.tile([P, T2], F32, name="page0")]
+        nc.gpsimd.memset(pages[0][:], 0.0)
+        nc.gpsimd.memset(minus_one[:], -1.0)
 
         warm = keep.tile([P, 1], F32, name="warm")
-        nc.scalar.activation(warm[:], ident[:, 0:1], ACT.Sigmoid)
+        nc.vector.memset(warm[:], 0.0)
+        nc.scalar.activation(warm[:], warm[:], ACT.Sigmoid)
 
         idx = lists.tile([P, S // STRIPE], U16, name="idx")
         idx2 = lists.tile([P, S // STRIPE], U16, name="idx2")
         idx3 = lists.tile([P, M // STRIPE], U16, name="idx3")
         idx4 = lists.tile([P, M // STRIPE], U16, name="idx4")
 
-        def load_table(a):
-            words = keep.tile([P, T], I32, name="tab", tag="tab%d" % a)
-            nc.sync.dma_start(words[:], tab_words[a].rearrange("p t i -> p (t i)").bitcast(I32))
-            return words
+        def load_table(a, first, last):
+            source = tab_words[a].rearrange("p t i -> p (t i)").bitcast(I32)
+            nc.sync.dma_start(tabs[a][:, first:last], source[:, first:last])
+
+        def move_scale_rows(a):
+            for q in range(P // QUADRANT):
+                first = P // 2 * a + PACK * PACK * q
+                nc.sync.dma_start(
+                    v_plane[QUADRANT * q + PACK * a : QUADRANT * q + PACK * (a + 1), :].bitcast(I32),
+                    v_spread[first : first + PACK * PACK : PACK, :].bitcast(I32),
+                )
+
+        def load_w1_pass(g, a):
+            first, last = W1_GROUPS[g]
+            shape = [P, PACK, P * (last - first)]
+            if (g, a) == (2, 1):
+                raw = shared.tile(shape, F32, name="w1_raw_held", offset=2 * S)
+            else:
+                raw = keep.tile(shape, F32, name="w1_raw", tag="raw%d_%d" % (g, a))
+            rows = w1[K_PASS * a : K_PASS * (a + 1), P * first : P * last]
+            nc.sync.dma_start(raw[:], rows.rearrange("(p i) c -> p i c", i=PACK))
+            return raw
 
         def load_w1(g):
-            first, last = W1_GROUPS[g]
-            raws = []
-            for a in range(2):
-                shape = [P, PACK, P * (last - first)]
-                if (g, a) == (2, 1):
-                    raw = shared.tile(shape, F32, name="w1_raw_held", offset=2 * S)
-                else:
-                    raw = keep.tile(shape, F32, name="w1_raw", tag="raw%d_%d" % (g, a))
-                rows = w1[K_PASS * a : K_PASS * (a + 1), P * first : P * last]
-                nc.sync.dma_start(raw[:], rows.rearrange("(p i) c -> p i c", i=PACK))
-                raws.append(raw)
-            return raws
+            return [load_w1_pass(g, a) for a in range(2)]
 
-        tabs = [load_table(0)]
+        tabs = [keep.tile([P, T], I32, name="tab", tag="tab%d" % a) for a in range(2)]
+        load_table(0, 0, HALF)
         nc.sync.dma_start(idx[:], offs)
-        for a in range(2):
-            rows = tab_plane[P // 2 * a : P // 2 * (a + 1) : PACK, :]
-            nc.sync.dma_start(rows.bitcast(I32), tab_scales[a].rearrange("(q r) t -> r q t", r=PACK).bitcast(I32))
+        nc.sync.dma_start(tab_plane[0:P:PACK, :].bitcast(I32), tab_scales.rearrange("a q t -> (a q) t").bitcast(I32))
+        nc.sync.dma_start(idx2[:], offs2)
+        load_table(0, HALF, T)
         w1_raw = [load_w1(0)]
-        nc.sync.dma_start(gain_rows[0:PACK, :], gain[0:K_PASS].rearrange("(s p) -> s p", p=P))
-        tabs.append(load_table(1))
-        wgs_rows = keep.tile([P, S], F32, name="wgs_rows")
-        nc.sync.dma_start(wgs_rows[:, 0:HALF], wgs[:, 0:HALF])
+        load_table(1, 0, T // 4)
         v_spread = keep.tile([P, S], U8, name="v_spread", align_bytes=64)
         nc.vector.tensor_copy(v_spread[:], tab_plane[:].indirect(idx[:]))
-        for q in range(P // QUADRANT):
-            nc.sync.dma_start(
-                v_plane[QUADRANT * q : QUADRANT * q + 2 * PACK, :].bitcast(I32),
-                v_spread[PACK * q : P : PACK * PACK, :].bitcast(I32),
-            )
-        nc.sync.dma_start(idx2[:], offs2)
+        pages.append(keep.tile([P, T2], F32, name="page1", tag="plane_then_page", align_bytes=64))
+        nc.vector.memset(pages[1][:], 0.0)
+        move_scale_rows(0)
+        load_table(1, T // 4, T - HALF)
+        move_scale_rows(1)
+        load_table(1, T - HALF, T)
+        nc.sync.dma_start(gain_rows[0:PACK, :], gain[0:K_PASS].rearrange("(s p) -> s p", p=P))
+        wgs_rows = keep.tile([P, S], F32, name="wgs_rows")
+        nc.sync.dma_start(wgs_rows[:, 0:HALF], wgs[:, 0:HALF])
         w1_raw.append(load_w1(1))
         nc.sync.dma_start(wgs_rows[:, HALF:], wgs[:, HALF:])
         w1_raw.append(load_w1(2))
@@ -151,11 +159,9 @@ def tile_list_cousin_matcher_kernel(
                 w2_scales[:, PACK * q : PACK * (q + 1), :].rearrange("a r c -> r a c").bitcast(I32),
             )
 
-        v_codes = [
-            keep.tile([P, S], U32, name="v_codes0", tag="plane_then_words", align_bytes=64),
-            keep.tile([P, S], U32, name="v_codes1", align_bytes=64),
-        ]
-        nc.vector.tensor_copy(v_codes[0][:], tabs[0][:].bitcast(U32).indirect(idx[:]))
+        v_first = keep.tile([P, S], U32, name="v_codes0", align_bytes=64)
+        nc.vector.tensor_copy(v_first[:], tabs[0][:].bitcast(U32).indirect(idx[:]))
+        v_codes = {(0, j0): v_first[:, j0 : j0 + HALF] for j0 in range(0, S, HALF)}
         res_rows = keep.tile([P, N // P, M], F32, name="res_rows", tag="tab0")
         nc.sync.dma_start(res_rows[:], res.rearrange("(b p) m -> p b m", p=P))
 
@@ -189,6 +195,23 @@ def tile_list_cousin_matcher_kernel(
                 in_=rounded[:].rearrange("p s a c i -> p (s a c i)"),
             )
 
+        def prepare_first_w1(a):
+            rounded = keep.tile([P, P, PACK], BF16, name="w1_rounded_first", tag="first%d" % a, align_bytes=64)
+            nc.scalar.copy(
+                rounded[:].rearrange("p (c j) i -> p c i j", j=PACK),
+                w1_raw[0][a][:].rearrange("p i (c j) -> p c i j", j=PACK),
+            )
+            nc.vector.quantize_mx(
+                out=w1_codes[:, 0, P * a : P * (a + 1)].bitcast(FP8X4),
+                scales=w1_plane[:, 0, P * a : P * (a + 1)],
+                in_=rounded[:].rearrange("p c i -> p (c i)"),
+            )
+
+        def gather_second_pass(j0, tag):
+            words = keep.tile([P, HALF], U32, name="v_codes1", tag=tag, align_bytes=64)
+            nc.vector.tensor_copy(words[:], tabs[1][:].bitcast(U32).indirect(entries(idx, j0, HALF)))
+            v_codes[1, j0] = words[:]
+
         def sigmoid_of(s):
             if s == 1:
                 sigmoid = shared.tile([P, S], F32, name="sigmoid_first", offset=0)
@@ -204,7 +227,7 @@ def tile_list_cousin_matcher_kernel(
                         out=e_bank[:],
                         lhsT=w1_codes[:, s, P * a : P * (a + 1)].bitcast(FP8X4),
                         lhsT_scale=w1_plane[:, s, P * a : P * (a + 1)],
-                        rhs=v_codes[a][:, cols].bitcast(FP8X4),
+                        rhs=v_codes[a, j0 - j0 % HALF][:, j0 % HALF : j0 % HALF + count].bitcast(FP8X4),
                         rhs_scale=v_plane[PACK * a :, cols],
                         start=(a == 0),
                         stop=(a == 1),
@@ -230,22 +253,23 @@ def tile_list_cousin_matcher_kernel(
             window = pages[s % PAGES][:].indirect(entries(idx2, j0, left.shape[1]))
             nc.vector.tensor_tensor(window, left, right, ALU.mult)
 
-        def first_factor(j0, tag):
-            factor = keep.tile([P, HALF], F32, name="factor", tag=tag)
-            nc.scalar.activation(factor[:], wgs_rows[:, j0 : j0 + HALF], ACT.Copy, scale=gain_plain[:, 0:1])
+        def first_factor(j0, count, tag):
+            factor = keep.tile([P, count], F32, name="factor", tag=tag)
+            nc.scalar.activation(factor[:], wgs_rows[:, j0 : j0 + count], ACT.Copy, scale=gain_plain[:, 0:1])
             return factor[:]
 
         def negate_ev(s):
             nc.scalar.activation(evs[s][:], evs[s][:], ACT.Copy, scale=-1.0)
 
-        prepare_w1(0)
-        for j0 in range(0, S, HALF):
-            window = tabs[1][:].bitcast(U32).indirect(entries(idx, j0, HALF))
-            nc.vector.tensor_copy(v_codes[1][:, j0 : j0 + HALF], window)
+        prepare_first_w1(0)
+        gather_second_pass(0, "v_second")
+        prepare_first_w1(1)
+        gather_second_pass(HALF, "first1")
+        factor = first_factor(0, HALF, "factor")
         sigmoid = sigmoid_of(0)
-        scatter(0, 0, sigmoid[:, 0:HALF], first_factor(0, "factor"))
+        scatter(0, 0, sigmoid[:, 0:HALF], factor)
         prepare_w1(1)
-        scatter(0, HALF, sigmoid[:, HALF:], first_factor(HALF, "raw1_0"))
+        scatter(0, HALF, sigmoid[:, HALF:], first_factor(HALF, HALF, "raw1_0"))
         prepare_w1(2)
         ready = {s: activations(s) for s in (1, 2)}
 

@@ -104,11 +104,11 @@ def tile_list_cousin_matcher_kernel(
             return [load_w1_pass(g, a) for a in range(2)]
 
         tabs = [keep.tile([P, T], I32, name="tab", tag="tab%d" % a) for a in range(2)]
-        load_table(0, 0, HALF)
+        load_table(0, 0, T // 4)
         nc.sync.dma_start(idx[:], offs)
         nc.sync.dma_start(tab_plane[0:P:PACK, :].bitcast(I32), tab_scales.rearrange("a q t -> (a q) t").bitcast(I32))
-        nc.sync.dma_start(idx2[:], offs2)
-        load_table(0, HALF, T)
+        nc.sync.dma_start(gain_rows[0:PACK, :], gain[0:K_PASS].rearrange("(s p) -> s p", p=P))
+        load_table(0, T // 4, T)
         w1_raw = [load_w1(0)]
         load_table(1, 0, T // 4)
         v_spread = keep.tile([P, S], U8, name="v_spread", align_bytes=64)
@@ -119,9 +119,9 @@ def tile_list_cousin_matcher_kernel(
         load_table(1, T // 4, T - HALF)
         move_scale_rows(1)
         load_table(1, T - HALF, T)
-        nc.sync.dma_start(gain_rows[0:PACK, :], gain[0:K_PASS].rearrange("(s p) -> s p", p=P))
         wgs_rows = keep.tile([P, S], F32, name="wgs_rows")
         nc.sync.dma_start(wgs_rows[:, 0:HALF], wgs[:, 0:HALF])
+        nc.sync.dma_start(idx2[:], offs2)
         w1_raw.append(load_w1(1))
         nc.sync.dma_start(wgs_rows[:, HALF:], wgs[:, HALF:])
         w1_raw.append(load_w1(2))

@@ -109,7 +109,7 @@ def tile_list_cousin_matcher_kernel(
         nc.sync.dma_start(tab_plane[0:P:PACK, :].bitcast(I32), tab_scales.rearrange("a q t -> (a q) t").bitcast(I32))
         nc.sync.dma_start(gain_rows[0:PACK, :], gain[0:K_PASS].rearrange("(s p) -> s p", p=P))
         load_table(0, T // 4, T)
-        w1_raw = [load_w1(0)]
+        w1_raw = [[load_w1_pass(0, 0)]]
         load_table(1, 0, T // 4)
         v_spread = keep.tile([P, S], U8, name="v_spread", align_bytes=64)
         nc.vector.tensor_copy(v_spread[:], tab_plane[:].indirect(idx[:]))
@@ -119,6 +119,7 @@ def tile_list_cousin_matcher_kernel(
         load_table(1, T // 4, T - HALF)
         move_scale_rows(1)
         load_table(1, T - HALF, T)
+        w1_raw[0].append(load_w1_pass(0, 1))
         wgs_rows = keep.tile([P, S], F32, name="wgs_rows")
         nc.sync.dma_start(wgs_rows[:, 0:HALF], wgs[:, 0:HALF])
         nc.sync.dma_start(idx2[:], offs2)

@@ -370,17 +370,16 @@ def tile_list_cousin_matcher_kernel(
 
         def multiply(y, a, c, pair):
             codes, plane = z_mx[a][c]
-            parts = [(b, m0) for b in range(2) for m0 in range(0, CHUNK, P)]
-            for b, m0 in parts:
+            for b in range(2):
                 n0 = P * (2 * pair + b)
                 nc.tensor.matmul_mx(
-                    out=y[:, b, m0 : m0 + P],
+                    out=y[:, b, :],
                     lhsT=w2_codes[:, a, 2 * n0 : 2 * (n0 + P)].bitcast(FP4X4),
                     lhsT_scale=w2_plane[:, a, n0 : n0 + P],
-                    rhs=codes[:, m0 : m0 + P].bitcast(FP8X4),
-                    rhs_scale=plane[:, m0 : m0 + P],
-                    start=(a == 0 and (b, m0) == parts[0]),
-                    stop=(a == 1 and (b, m0) == parts[-1]),
+                    rhs=codes.bitcast(FP8X4),
+                    rhs_scale=plane,
+                    start=(a == 0 and b == 0),
+                    stop=(a == 1 and b == 1),
                 )
 
         def open_scores(c):
@@ -394,10 +393,13 @@ def tile_list_cousin_matcher_kernel(
             for pair in range(2):
                 y = score_banks[c][pair]
                 multiply(y, 1, c, pair)
-                result = results[c // 2][:, c % 2, 2 * pair : 2 * pair + 2, :]
-                nc.vector.tensor_tensor(result, y[:], res_rows[:, 2 * pair : 2 * pair + 2, cols], ALU.add)
-                rows = out[2 * P * pair : 2 * P * (pair + 1), cols]
-                nc.sync.dma_start(rows.rearrange("(b p) m -> p b m", p=P), result)
+                step = 1 if (c, pair) == (CHUNKS - 1, 1) else 2
+                for b in range(0, 2, step):
+                    first = 2 * pair + b
+                    result = results[c // 2][:, c % 2, first : first + step, :]
+                    nc.vector.tensor_tensor(result, y[:, b : b + step, :], res_rows[:, first : first + step, cols], ALU.add)
+                    rows = out[P * first : P * (first + step), cols]
+                    nc.sync.dma_start(rows.rearrange("(b p) m -> p b m", p=P), result)
 
         def finish_last(c, x1, x2):
             rows = z_rows[c][:]

@@ -42,6 +42,7 @@ def tile_list_cousin_matcher_kernel(
         lists = ctx.enter_context(tc.tile_pool(name="lists", bufs=1))
         keep = ctx.enter_context(tc.tile_pool(name="keep", bufs=1))
         shared = ctx.enter_context(tc.tile_pool(name="shared", bufs=1))
+        reused = ctx.enter_context(tc.tile_pool(name="reused", bufs=1))
         late = ctx.enter_context(tc.tile_pool(name="late", bufs=1))
         psum = ctx.enter_context(tc.psum_pool(name="psum", bufs=1))
 
@@ -51,7 +52,7 @@ def tile_list_cousin_matcher_kernel(
         def work_bank(shape, dtype=F32):
             return psum.tile(shape, dtype, name="work_bank", bufs=BANKS)
 
-        tab_plane = keep.tile([P, T], U8, name="tab_plane", tag="plane_then_page", align_bytes=64)
+        tab_plane = reused.tile([P, T], U8, name="tab_plane", offset=4 * T2 - T // 2)
         nc.gpsimd.memset(tab_plane[:].bitcast(I32), 0)
         v_plane = keep.tile([P, S], U8, name="v_plane", align_bytes=64)
         nc.vector.memset(v_plane[:].bitcast(I32), 0)
@@ -59,14 +60,12 @@ def tile_list_cousin_matcher_kernel(
         nc.vector.memset(gain_rows[:], 0.0)
         w2_plane = keep.tile([P, 2, N], U8, name="w2_plane", align_bytes=64)
         nc.vector.memset(w2_plane[:].rearrange("p a c -> p (a c)").bitcast(I32), 0)
-        minus_one = keep.tile([P, M], F32, name="minus_one")
         ident = keep.tile([P, P], F32, name="ident")
         make_identity(nc, ident[:])
         ident_bf16 = keep.tile([P, P], BF16, name="ident_bf16")
         make_identity(nc, ident_bf16[:])
         pages = [keep.tile([P, T2], F32, name="page0")]
-        nc.gpsimd.memset(pages[0][:], 0.0)
-        nc.gpsimd.memset(minus_one[:], -1.0)
+        nc.vector.memset(pages[0][:], 0.0)
 
         warm = keep.tile([P, 1], F32, name="warm")
         nc.vector.memset(warm[:], 0.0)
@@ -113,8 +112,10 @@ def tile_list_cousin_matcher_kernel(
         load_table(1, 0, T // 4)
         v_spread = keep.tile([P, S], U8, name="v_spread", align_bytes=64)
         nc.vector.tensor_copy(v_spread[:], tab_plane[:].indirect(idx[:]))
-        pages.append(keep.tile([P, T2], F32, name="page1", tag="plane_then_page", align_bytes=64))
+        pages.append(reused.tile([P, T2], F32, name="page1", offset=0))
         nc.vector.memset(pages[1][:], 0.0)
+        minus_one = reused.tile([P, M], F32, name="minus_one", offset=4 * T2)
+        nc.vector.memset(minus_one[:], -1.0)
         move_scale_rows(0)
         load_table(1, T // 4, T - HALF)
         move_scale_rows(1)

@@ -248,6 +248,9 @@ def tile_list_cousin_matcher_kernel(
                 nc.scalar.copy(column, gain_woven[:, s - PACK : s - PACK + 1])
             h = sigmoid_of(s)
             for j0 in range(0, S, HALF):
+                if (s, j0) == (LAST, HALF):
+                    column = keep.tile([P, 1], F32, name="gain_column_last", tag="held_codes", align_bytes=64)[:]
+                    nc.scalar.copy(column, gain_woven[:, PACK - 1 : PACK])
                 nc.scalar.activation(h[:, j0 : j0 + HALF], h[:, j0 : j0 + HALF], ACT.Copy, scale=column)
             return h[:], weights
 
@@ -279,9 +282,12 @@ def tile_list_cousin_matcher_kernel(
         z_rows = [keep.tile([P, PACK, CHUNK], BF16, name="z_rows%d" % c) for c in range(CHUNKS)]
         z_mx = [[], []]
 
-        def quantise_z(a, rounded):
+        def quantise_z(a, rounded, held=False):
             width = rounded.shape[1]
-            codes = keep.tile([P, width], U32, name="z_codes%d" % a, bufs=2, align_bytes=64)
+            if held:
+                codes = keep.tile([P, width], U32, name="z_codes_held", tag="held_codes", align_bytes=64)
+            else:
+                codes = keep.tile([P, width], U32, name="z_codes%d" % a, bufs=2, align_bytes=64)
             plane = keep.tile([P, width], U8, name="z_plane%d" % a, bufs=M // width, align_bytes=64)
             nc.vector.quantize_mx(
                 out=codes[:].bitcast(FP8X4), scales=plane[:], in_=rounded[:].rearrange("p m t -> p (m t)")
@@ -348,7 +354,7 @@ def tile_list_cousin_matcher_kernel(
                         nc.tensor.transpose(back[:, b, h, :], words[:, 2 * pair + b, h : 2 * P : 2], ident[:])
                 target = z_plain[:, CHUNK * pair : CHUNK * (pair + 1), :].bitcast(F32)
                 nc.scalar.copy(target.rearrange("p (b m) h -> p b m h", b=2), back[:].rearrange("p b h m -> p b m h"))
-            quantise_z(0, z_plain)
+            return z_plain
 
         negate_ev(0)
         for s in range(LAST):
@@ -362,8 +368,12 @@ def tile_list_cousin_matcher_kernel(
                 evs.append(load_ev(s + PACK))
             if s == 0:
                 prepare_w1(3)
-            if s in (PACK - 1, PACK):
-                finish_plain(s - PACK + 1)
+            if s == PACK - 1:
+                quantise_z(0, finish_plain(0))
+            if s == PACK:
+                second_half = finish_plain(1)
+            if s == LAST - 1:
+                quantise_z(0, second_half, held=True)
             if s + 1 < LAST:
                 negate_ev(s + 1)
             if s + 3 < SLICES:

@@ -426,24 +426,30 @@ def tile_list_cousin_matcher_kernel(
         woven = [
             keep.tile([P, HALF, PACK], BF16, name="z_woven", tag=tag, align_bytes=64) for tag in ("z_half_last", "rounded1")
         ]
-        def fetch_pair(c):
-            if c == CHUNKS - 1:
-                x = keep.tile([P, 2, CHUNK], F32, name="x_held", tag="z_rows0")
-            else:
-                x = keep.tile([P, 2, CHUNK], F32, name="x_last", bufs=CHUNKS - 1)
+
+        def fetch_one(list_tile, c, target):
             m0 = CHUNK * c
-            for n, list_tile in enumerate((idx3, idx4)):
-                window = pages[LAST % PAGES][:].indirect(entries(list_tile, m0, CHUNK))
-                nc.vector.tensor_tensor(x[:, n, :], window, evs[LAST][:, m0 : m0 + CHUNK], ALU.add)
-            return x
+            window = pages[LAST % PAGES][:].indirect(entries(list_tile, m0, CHUNK))
+            nc.vector.tensor_tensor(target, window, evs[LAST][:, m0 : m0 + CHUNK], ALU.add)
+            return target
+
+        def fetch_pair(c):
+            x = keep.tile([P, 2, CHUNK], F32, name="x_last", bufs=CHUNKS - 1)
+            return fetch_one(idx3, c, x[:, 0, :]), fetch_one(idx4, c, x[:, 1, :])
 
         pairs = [fetch_pair(0), fetch_pair(1)]
-        for c in range(CHUNKS):
-            z_woven = finish_last(c, pairs[c][:, 0, :], pairs[c][:, 1, :])
-            if c >= 2:
-                close_scores(c - 2)
-            quantise_z(1, z_woven)
-            if c == 0:
-                pairs.extend(fetch_pair(n) for n in (2, 3))
+        z_woven = [finish_last(c, *pairs[c]) for c in range(2)]
+        pairs.append(fetch_pair(2))
+        x_first = keep.tile([P, 2, CHUNK], F32, name="x_last", bufs=CHUNKS - 1)
+        last_first = fetch_one(idx3, CHUNKS - 1, x_first[:, 0, :])
+        quantise_z(1, z_woven[0])
+        x_held = keep.tile([P, CHUNK], F32, name="x_held", tag="z_rows0")
+        pairs.append((last_first, fetch_one(idx4, CHUNKS - 1, x_held[:])))
+        z_woven.append(finish_last(2, *pairs[2]))
+        quantise_z(1, z_woven[1])
+        z_woven.append(finish_last(3, *pairs[3]))
+        for c in range(2, CHUNKS):
+            close_scores(c - 2)
+            quantise_z(1, z_woven[c])
         for c in range(2, CHUNKS):
             close_scores(c)

@@ -30,6 +30,9 @@ LAST = SLICES - 1
 PAGES = 2
 W1_GROUPS = ((0, 1), (1, 2), (2, 4), (4, 8))
 BANKS = 8
+BANK_BYTES = 2048
+ROWS_AT = 4 * CHUNK
+ROW_AT = (ROWS_AT, ROWS_AT + 2 * CHUNK + 32, ROWS_AT + 32, ROWS_AT + 2 * CHUNK + 32)
 FIRST_PIECES = ((0, CHUNK), (CHUNK, CHUNK), (HALF, HALF))
 
 
@@ -44,13 +47,18 @@ def tile_list_cousin_matcher_kernel(
         shared = ctx.enter_context(tc.tile_pool(name="shared", bufs=1))
         reused = ctx.enter_context(tc.tile_pool(name="reused", bufs=1))
         late = ctx.enter_context(tc.tile_pool(name="late", bufs=1))
+        tail = ctx.enter_context(tc.tile_pool(name="tail", bufs=1))
         psum = ctx.enter_context(tc.psum_pool(name="psum", bufs=1))
 
         def entries(list_tile, first, count):
             return list_tile[:, first // STRIPE : (first + count) // STRIPE]
 
-        def work_bank(shape, dtype=F32):
-            return psum.tile(shape, dtype, name="work_bank", bufs=BANKS)
+        taken = []
+
+        def work_bank(shape, dtype=F32, skip=0):
+            bank = (taken[-1] + 1 + skip) % BANKS if taken else 0
+            taken.append(bank)
+            return psum.tile(shape, dtype, name="bank%d" % bank, offset=BANK_BYTES * bank)
 
         tab_plane = reused.tile([P, T], U8, name="tab_plane", offset=4 * T2 - T // 2)
         nc.gpsimd.memset(tab_plane[:].bitcast(I32), 0)
@@ -102,7 +110,7 @@ def tile_list_cousin_matcher_kernel(
         def load_w1(g):
             return [load_w1_pass(g, a) for a in range(2)]
 
-        tabs = [keep.tile([P, T], I32, name="tab", tag="tab%d" % a) for a in range(2)]
+        tabs = [keep.tile([P, T], I32, name="tab", tag="tab%d" % a, align_bytes=64) for a in range(2)]
         load_table(0, 0, T // 4)
         nc.sync.dma_start(idx[:], offs)
         nc.sync.dma_start(tab_plane[0:P:PACK, :].bitcast(I32), tab_scales.rearrange("a q t -> (a q) t").bitcast(I32))
@@ -164,7 +172,7 @@ def tile_list_cousin_matcher_kernel(
         v_first = keep.tile([P, S], U32, name="v_codes0", align_bytes=64)
         nc.vector.tensor_copy(v_first[:], tabs[0][:].bitcast(U32).indirect(idx[:]))
         v_codes = {(0, j0): v_first[:, j0 : j0 + HALF] for j0 in range(0, S, HALF)}
-        res_rows = keep.tile([P, N // P, M], F32, name="res_rows", tag="tab0")
+        res_rows = keep.tile([P, N // P, M], F32, name="res_rows", tag="tab0", align_bytes=64)
         nc.sync.dma_start(res_rows[:], res.rearrange("(b p) m -> p b m", p=P))
 
         gain_bank = work_bank([P, HALF])
@@ -279,7 +287,8 @@ def tile_list_cousin_matcher_kernel(
         ready = {s: activations(s) for s in (1, 2)}
 
         z_turned = [keep.tile([P, PACK, K_PASS], BF16, name="z_turned%d" % half) for half in range(2)]
-        z_rows = [keep.tile([P, PACK, CHUNK], BF16, name="z_rows%d" % c) for c in range(CHUNKS)]
+        z_rows = [keep.tile([P, PACK - 1, CHUNK], BF16, name="z_rows%d" % c) for c in range(CHUNKS - 1)]
+        z_rows.append(tail.tile([P, PACK - 1, CHUNK], BF16, name="z_rows_last", offset=ROWS_AT))
         z_mx = [[], []]
 
         def quantise_z(a, rounded, held=False):
@@ -332,10 +341,7 @@ def tile_list_cousin_matcher_kernel(
                 if s < PACK:
                     nc.scalar.activation(z_turned[half][:, :, P * s : P * (s + 1)], neg_z[:], ACT.Copy, scale=-1.0)
                 else:
-                    if (s, half) == (LAST - 1, 1):
-                        rounded = keep.tile([P, PACK, P], BF16, name="z_half_last", align_bytes=64)
-                    else:
-                        rounded = keep.tile([P, PACK, P], BF16, name="z_half", bufs=2)
+                    rounded = keep.tile([P, PACK, P], BF16, name="z_half", bufs=2)
                     nc.scalar.activation(rounded[:], neg_z[:], ACT.Copy, scale=-1.0)
                     back = work_bank([P, PACK, P], BF16)
                     for b in range(PACK):
@@ -394,7 +400,7 @@ def tile_list_cousin_matcher_kernel(
                 )
 
         def open_scores(c):
-            banks = [work_bank([P, 2, CHUNK]) for pair in range(2)]
+            banks = [work_bank([P, 2, CHUNK], skip=2 if (c, pair) == (2, 0) else 0) for pair in range(2)]
             for pair in range(2):
                 multiply(banks[pair], 0, c, pair)
             return banks
@@ -412,20 +418,24 @@ def tile_list_cousin_matcher_kernel(
                     rows = out[P * first : P * (first + step), cols]
                     nc.sync.dma_start(rows.rearrange("(b p) m -> p b m", p=P), result)
 
-        def finish_last(c, x1, x2):
-            rows = z_rows[c][:]
-            nc.vector.tensor_tensor(rows[:, LAST - PACK, :], x1, x2, ALU.min)
-            z_woven = woven[c // 2][:, CHUNK * (c % 2) : CHUNK * (c % 2 + 1), :]
+        def weave_early(c):
+            target = woven[:, CHUNK * c : CHUNK * (c + 1), 0 : PACK - 1]
             nc.scalar.copy(
-                z_woven.rearrange("p (m i) t -> p m t i", i=PACK), rows.rearrange("p t (m i) -> p m t i", i=PACK)
+                target.rearrange("p (m i) t -> p m t i", i=PACK), z_rows[c][:].rearrange("p t (m i) -> p m t i", i=PACK)
             )
+
+        def finish_last(c, x1, x2):
+            row = tail.tile([P, CHUNK], BF16, name="z_row%d" % c, offset=ROW_AT[c])
+            nc.vector.tensor_tensor(row[:], x1, x2, ALU.min)
+            z_woven = woven[:, CHUNK * c : CHUNK * (c + 1), :]
+            nc.scalar.copy(z_woven[:, :, PACK - 1], row[:])
             return z_woven
 
         results = [keep.tile([P, 2, N // P, CHUNK], F32, name="results", tag="raw3_%d" % n) for n in range(2)]
-        score_banks = [open_scores(c) for c in range(CHUNKS)]
-        woven = [
-            keep.tile([P, HALF, PACK], BF16, name="z_woven", tag=tag, align_bytes=64) for tag in ("z_half_last", "rounded1")
-        ]
+        score_banks = [open_scores(c) for c in range(CHUNKS - 1)]
+        woven = keep.tile([P, M, PACK], BF16, name="z_woven", tag="tab1", align_bytes=64)
+        for c in range(CHUNKS):
+            weave_early(c)
 
         def fetch_one(list_tile, c, target):
             m0 = CHUNK * c
@@ -434,22 +444,24 @@ def tile_list_cousin_matcher_kernel(
             return target
 
         def fetch_pair(c):
-            x = keep.tile([P, 2, CHUNK], F32, name="x_last", bufs=CHUNKS - 1)
+            x = keep.tile([P, 2, CHUNK], F32, name="x_last", bufs=2)
             return fetch_one(idx3, c, x[:, 0, :]), fetch_one(idx4, c, x[:, 1, :])
 
         pairs = [fetch_pair(0), fetch_pair(1)]
         z_woven = [finish_last(c, *pairs[c]) for c in range(2)]
         pairs.append(fetch_pair(2))
-        x_first = keep.tile([P, 2, CHUNK], F32, name="x_last", bufs=CHUNKS - 1)
+        x_first = keep.tile([P, 2, CHUNK], F32, name="x_last", bufs=2)
         last_first = fetch_one(idx3, CHUNKS - 1, x_first[:, 0, :])
         quantise_z(1, z_woven[0])
-        x_held = keep.tile([P, CHUNK], F32, name="x_held", tag="z_rows0")
-        pairs.append((last_first, fetch_one(idx4, CHUNKS - 1, x_held[:])))
         z_woven.append(finish_last(2, *pairs[2]))
+        x_held = tail.tile([P, CHUNK], F32, name="x_held", offset=32)
+        pairs.append((last_first, fetch_one(idx4, CHUNKS - 1, x_held[:])))
         quantise_z(1, z_woven[1])
         z_woven.append(finish_last(3, *pairs[3]))
         for c in range(2, CHUNKS):
             close_scores(c - 2)
+            if c == 2:
+                score_banks.append(open_scores(CHUNKS - 1))
             quantise_z(1, z_woven[c])
         for c in range(2, CHUNKS):
             close_scores(c)

@@ -343,11 +343,16 @@ def tile_list_cousin_matcher_kernel(
                 else:
                     rounded = keep.tile([P, PACK, P], BF16, name="z_half", bufs=2)
                     nc.scalar.activation(rounded[:], neg_z[:], ACT.Copy, scale=-1.0)
-                    back = work_bank([P, PACK, P], BF16)
+                    blocks = 2 if (s, half) == (LAST - 1, 1) else PACK
+                    backs = []
                     for b in range(PACK):
-                        nc.tensor.transpose(back[:, b, :], rounded[:, b, :], ident_bf16[:])
+                        if b % blocks == 0:
+                            back = work_bank([P, blocks, P], BF16)
+                        nc.tensor.transpose(back[:, b % blocks, :], rounded[:, b, :], ident_bf16[:])
+                        if b % 2 == 1:
+                            backs.append(back[:, b % blocks - 1 : b % blocks + 1, :])
                     for pair in range(2):
-                        source = back[:, 2 * pair : 2 * pair + 2, :].rearrange("p b m -> p (b m)")
+                        source = backs[pair].rearrange("p b m -> p (b m)")
                         nc.scalar.copy(z_rows[2 * half + pair][:, s - PACK, :], source)
 
         def finish_plain(half):
@@ -399,10 +404,10 @@ def tile_list_cousin_matcher_kernel(
                     stop=(a == 1 and b == 1),
                 )
 
-        def open_scores(c):
-            banks = [work_bank([P, 2, CHUNK], skip=2 if (c, pair) == (2, 0) else 0) for pair in range(2)]
-            for pair in range(2):
-                multiply(banks[pair], 0, c, pair)
+        def open_scores(c, pairs=(0, 1)):
+            banks = [work_bank([P, 2, CHUNK], skip=1 if (c, pair) == (2, 0) else 0) for pair in pairs]
+            for bank, pair in zip(banks, pairs):
+                multiply(bank, 0, c, pair)
             return banks
 
         def close_scores(c):
@@ -416,7 +421,8 @@ def tile_list_cousin_matcher_kernel(
                     result = results[c // 2][:, c % 2, first : first + step, :]
                     nc.vector.tensor_tensor(result, y[:, b : b + step, :], res_rows[:, first : first + step, cols], ALU.add)
                     rows = out[P * first : P * (first + step), cols]
-                    nc.sync.dma_start(rows.rearrange("(b p) m -> p b m", p=P), result)
+                    queue = nc.scalar if c > 0 and (pair, b) == (1, 0) else nc.sync
+                    queue.dma_start(rows.rearrange("(b p) m -> p b m", p=P), result)
 
         def weave_early(c):
             target = woven[:, CHUNK * c : CHUNK * (c + 1), 0 : PACK - 1]
@@ -432,7 +438,7 @@ def tile_list_cousin_matcher_kernel(
             return z_woven
 
         results = [keep.tile([P, 2, N // P, CHUNK], F32, name="results", tag="raw3_%d" % n) for n in range(2)]
-        score_banks = [open_scores(c) for c in range(CHUNKS - 1)]
+        score_banks = [open_scores(c) for c in range(CHUNKS - 1)] + [open_scores(CHUNKS - 1, (0,))]
         woven = keep.tile([P, M, PACK], BF16, name="z_woven", tag="tab1", align_bytes=64)
         for c in range(CHUNKS):
             weave_early(c)
@@ -461,7 +467,7 @@ def tile_list_cousin_matcher_kernel(
         for c in range(2, CHUNKS):
             close_scores(c - 2)
             if c == 2:
-                score_banks.append(open_scores(CHUNKS - 1))
+                score_banks[-1].extend(open_scores(CHUNKS - 1, (1,)))
             quantise_z(1, z_woven[c])
         for c in range(2, CHUNKS):
             close_scores(c)

@@ -53,12 +53,14 @@ def tile_list_cousin_matcher_kernel(
         def entries(list_tile, first, count):
             return list_tile[:, first // STRIPE : (first + count) // STRIPE]
 
-        taken = []
+        ring = list(range(BANKS))
 
-        def work_bank(shape, dtype=F32, skip=0):
-            bank = (taken[-1] + 1 + skip) % BANKS if taken else 0
-            taken.append(bank)
+        def bank_tile(bank, shape, dtype=F32):
             return psum.tile(shape, dtype, name="bank%d" % bank, offset=BANK_BYTES * bank)
+
+        def work_bank(shape, dtype=F32):
+            ring.append(ring.pop(0))
+            return bank_tile(ring[-1], shape, dtype)
 
         tab_plane = reused.tile([P, T], U8, name="tab_plane", offset=4 * T2 - T // 2)
         nc.gpsimd.memset(tab_plane[:].bitcast(I32), 0)
@@ -287,8 +289,7 @@ def tile_list_cousin_matcher_kernel(
         ready = {s: activations(s) for s in (1, 2)}
 
         z_turned = [keep.tile([P, PACK, K_PASS], BF16, name="z_turned%d" % half) for half in range(2)]
-        z_rows = [keep.tile([P, PACK - 1, CHUNK], BF16, name="z_rows%d" % c) for c in range(CHUNKS - 1)]
-        z_rows.append(tail.tile([P, PACK - 1, CHUNK], BF16, name="z_rows_last", offset=ROWS_AT))
+        z_rows = [keep.tile([P, PACK - 1, CHUNK], BF16, name="z_rows%d" % c) for c in range(CHUNKS)]
         z_mx = [[], []]
 
         def quantise_z(a, rounded, held=False):
@@ -331,17 +332,22 @@ def tile_list_cousin_matcher_kernel(
             for m0 in range(0, M, piece):
                 window = pages[s % PAGES][:].indirect(entries(idx4, m0, piece))
                 nc.vector.tensor_tensor(d[:, m0 : m0 + piece], window, neg_x1[:, m0 : m0 + piece], ALU.add)
-            for half in range(2):
-                cols = slice(HALF * half, HALF * (half + 1))
-                nc.scalar.activation(r[:, cols], d[:, cols], ACT.Relu, scale=-1.0)
-                neg_z = work_bank([P, PACK, P])
+            sums = [work_bank([P, PACK, P]) for half in range(2)]
+            for half, neg_z in enumerate(sums):
                 add_turned(neg_z, evs[s], HALF * half, True, False)
                 add_turned(neg_z, neg_x1, HALF * half, False, False)
+            for half, neg_z in enumerate(sums):
+                cols = slice(HALF * half, HALF * (half + 1))
+                nc.scalar.activation(r[:, cols], d[:, cols], ACT.Relu, scale=-1.0)
                 add_turned(neg_z, r, HALF * half, False, True)
+            for half, neg_z in enumerate(sums):
                 if s < PACK:
                     nc.scalar.activation(z_turned[half][:, :, P * s : P * (s + 1)], neg_z[:], ACT.Copy, scale=-1.0)
                 else:
-                    rounded = keep.tile([P, PACK, P], BF16, name="z_half", bufs=2)
+                    if (s, half) == (LAST - 1, 1):
+                        rounded = tail.tile([P, PACK, P], BF16, name="z_half_last", offset=ROWS_AT)
+                    else:
+                        rounded = keep.tile([P, PACK, P], BF16, name="z_half", bufs=2)
                     nc.scalar.activation(rounded[:], neg_z[:], ACT.Copy, scale=-1.0)
                     blocks = 2 if (s, half) == (LAST - 1, 1) else PACK
                     backs = []
@@ -367,6 +373,26 @@ def tile_list_cousin_matcher_kernel(
                 nc.scalar.copy(target.rearrange("p (b m) h -> p b m h", b=2), back[:].rearrange("p b h m -> p b m h"))
             return z_plain
 
+        def multiply(y, a, c, pair):
+            codes, plane = z_mx[a][c]
+            for b in range(2):
+                n0 = P * (2 * pair + b)
+                nc.tensor.matmul_mx(
+                    out=y[:, b, :],
+                    lhsT=w2_codes[:, a, 2 * n0 : 2 * (n0 + P)].bitcast(FP4X4),
+                    lhsT_scale=w2_plane[:, a, n0 : n0 + P],
+                    rhs=codes.bitcast(FP8X4),
+                    rhs_scale=plane,
+                    start=(a == 0 and b == 0),
+                    stop=(a == 1 and b == 1),
+                )
+
+        def open_scores(bank, c, pair):
+            y = bank_tile(bank, [P, 2, CHUNK])
+            multiply(y, 0, c, pair)
+            score_banks[c, pair] = y
+
+        score_banks = {}
         negate_ev(0)
         for s in range(LAST):
             neg_x1 = fetch_first(s)
@@ -389,31 +415,15 @@ def tile_list_cousin_matcher_kernel(
                 negate_ev(s + 1)
             if s + 3 < SLICES:
                 ready[s + 3] = activations(s + 3)
-
-        def multiply(y, a, c, pair):
-            codes, plane = z_mx[a][c]
-            for b in range(2):
-                n0 = P * (2 * pair + b)
-                nc.tensor.matmul_mx(
-                    out=y[:, b, :],
-                    lhsT=w2_codes[:, a, 2 * n0 : 2 * (n0 + P)].bitcast(FP4X4),
-                    lhsT_scale=w2_plane[:, a, n0 : n0 + P],
-                    rhs=codes.bitcast(FP8X4),
-                    rhs_scale=plane,
-                    start=(a == 0 and b == 0),
-                    stop=(a == 1 and b == 1),
-                )
-
-        def open_scores(c, pairs=(0, 1)):
-            banks = [work_bank([P, 2, CHUNK], skip=1 if (c, pair) == (2, 0) else 0) for pair in pairs]
-            for bank, pair in zip(banks, pairs):
-                multiply(bank, 0, c, pair)
-            return banks
+            if s + 3 == LAST:
+                early_banks = [ring.pop(0) for n in range(PACK)]
+                for n, bank in enumerate(early_banks):
+                    open_scores(bank, n // 2, n % 2)
 
         def close_scores(c):
             cols = slice(CHUNK * c, CHUNK * (c + 1))
             for pair in range(2):
-                y = score_banks[c][pair]
+                y = score_banks[c, pair]
                 multiply(y, 1, c, pair)
                 step = 1 if (c, pair) == (CHUNKS - 1, 1) else 2
                 for b in range(0, 2, step):
@@ -438,7 +448,8 @@ def tile_list_cousin_matcher_kernel(
             return z_woven
 
         results = [keep.tile([P, 2, N // P, CHUNK], F32, name="results", tag="raw3_%d" % n) for n in range(2)]
-        score_banks = [open_scores(c) for c in range(CHUNKS - 1)] + [open_scores(CHUNKS - 1, (0,))]
+        for n, bank in enumerate(ring[0:1] + ring[2:]):
+            open_scores(bank, 2 + n // 2, n % 2)
         woven = keep.tile([P, M, PACK], BF16, name="z_woven", tag="tab1", align_bytes=64)
         for c in range(CHUNKS):
             weave_early(c)
@@ -467,7 +478,7 @@ def tile_list_cousin_matcher_kernel(
         for c in range(2, CHUNKS):
             close_scores(c - 2)
             if c == 2:
-                score_banks[-1].extend(open_scores(CHUNKS - 1, (1,)))
+                open_scores(early_banks[0], CHUNKS - 1, 1)
             quantise_z(1, z_woven[c])
         for c in range(2, CHUNKS):
             close_scores(c)

@@ -31,8 +31,8 @@ PAGES = 2
 W1_GROUPS = ((0, 1), (1, 2), (2, 4), (4, 8))
 BANKS = 8
 BANK_BYTES = 2048
-ROWS_AT = 4 * CHUNK
-ROW_AT = (ROWS_AT, ROWS_AT + 2 * CHUNK + 32, ROWS_AT + 32, ROWS_AT + 2 * CHUNK + 32)
+ROWS_AT = 4 * HALF
+ROW_AT = (ROWS_AT + 2 * CHUNK + 32, ROWS_AT, ROWS_AT + 2 * CHUNK, ROWS_AT)
 FIRST_PIECES = ((0, CHUNK), (CHUNK, CHUNK), (HALF, HALF))
 
 
@@ -345,7 +345,7 @@ def tile_list_cousin_matcher_kernel(
                     nc.scalar.activation(z_turned[half][:, :, P * s : P * (s + 1)], neg_z[:], ACT.Copy, scale=-1.0)
                 else:
                     if (s, half) == (LAST - 1, 1):
-                        rounded = tail.tile([P, PACK, P], BF16, name="z_half_last", offset=ROWS_AT)
+                        rounded = tail.tile([P, PACK, P], BF16, name="z_half_last", offset=ROWS_AT - 32)
                     else:
                         rounded = keep.tile([P, PACK, P], BF16, name="z_half", bufs=2)
                     nc.scalar.activation(rounded[:], neg_z[:], ACT.Copy, scale=-1.0)
@@ -454,27 +454,26 @@ def tile_list_cousin_matcher_kernel(
         for c in range(CHUNKS):
             weave_early(c)
 
-        def fetch_one(list_tile, c, target):
-            m0 = CHUNK * c
-            window = pages[LAST % PAGES][:].indirect(entries(list_tile, m0, CHUNK))
-            nc.vector.tensor_tensor(target, window, evs[LAST][:, m0 : m0 + CHUNK], ALU.add)
+        def fetch_last(list_tile, m0, target):
+            count = target.shape[1]
+            window = pages[LAST % PAGES][:].indirect(entries(list_tile, m0, count))
+            nc.vector.tensor_tensor(target[:], window, evs[LAST][:, m0 : m0 + count], ALU.add)
             return target
 
-        def fetch_pair(c):
-            x = keep.tile([P, 2, CHUNK], F32, name="x_last", bufs=2)
-            return fetch_one(idx3, c, x[:, 0, :]), fetch_one(idx4, c, x[:, 1, :])
-
-        pairs = [fetch_pair(0), fetch_pair(1)]
-        z_woven = [finish_last(c, *pairs[c]) for c in range(2)]
-        pairs.append(fetch_pair(2))
-        x_first = keep.tile([P, 2, CHUNK], F32, name="x_last", bufs=2)
-        last_first = fetch_one(idx3, CHUNKS - 1, x_first[:, 0, :])
+        x1_early = fetch_last(idx3, 0, keep.tile([P, HALF], F32, name="x1_early"))
+        x2_early = fetch_last(idx4, 0, keep.tile([P, HALF], F32, name="x2_early"))
+        x2_third = fetch_last(idx4, HALF, keep.tile([P, CHUNK], F32, name="x2_third"))
+        z_woven = [
+            finish_last(c, x1_early[:, CHUNK * c : CHUNK * (c + 1)], x2_early[:, CHUNK * c : CHUNK * (c + 1)])
+            for c in range(2)
+        ]
+        x1_late = fetch_last(idx3, HALF, tail.tile([P, HALF], F32, name="x1_late", offset=0))
         quantise_z(1, z_woven[0])
-        z_woven.append(finish_last(2, *pairs[2]))
-        x_held = tail.tile([P, CHUNK], F32, name="x_held", offset=32)
-        pairs.append((last_first, fetch_one(idx4, CHUNKS - 1, x_held[:])))
+        x2_held = tail.tile([P, CHUNK], F32, name="x2_held", offset=ROWS_AT + 4 * CHUNK)
+        fetch_last(idx4, M - CHUNK, x2_held)
+        z_woven.append(finish_last(2, x1_late[:, 0:CHUNK], x2_third[:]))
         quantise_z(1, z_woven[1])
-        z_woven.append(finish_last(3, *pairs[3]))
+        z_woven.append(finish_last(3, x1_late[:, CHUNK:], x2_held[:]))
         for c in range(2, CHUNKS):
             close_scores(c - 2)
             if c == 2:

@@ -62,6 +62,10 @@ def tile_list_cousin_matcher_kernel(
             ring.append(ring.pop(0))
             return bank_tile(ring[-1], shape, dtype)
 
+        warm = keep.tile([P, 1], F32, name="warm")
+        nc.vector.memset(warm[:], 0.0)
+        nc.scalar.activation(warm[:], warm[:], ACT.Sigmoid)
+
         tab_plane = reused.tile([P, T], U8, name="tab_plane", offset=4 * T2 - T // 2)
         nc.gpsimd.memset(tab_plane[:].bitcast(I32), 0)
         v_plane = keep.tile([P, S], U8, name="v_plane", align_bytes=64)
@@ -76,10 +80,6 @@ def tile_list_cousin_matcher_kernel(
         make_identity(nc, ident_bf16[:])
         pages = [keep.tile([P, T2], F32, name="page0")]
         nc.vector.memset(pages[0][:], 0.0)
-
-        warm = keep.tile([P, 1], F32, name="warm")
-        nc.vector.memset(warm[:], 0.0)
-        nc.scalar.activation(warm[:], warm[:], ACT.Sigmoid)
 
         idx = lists.tile([P, S // STRIPE], U16, name="idx")
         idx2 = lists.tile([P, S // STRIPE], U16, name="idx2")
@@ -106,7 +106,8 @@ def tile_list_cousin_matcher_kernel(
             else:
                 raw = keep.tile(shape, F32, name="w1_raw", tag="raw%d_%d" % (g, a))
             rows = w1[K_PASS * a : K_PASS * (a + 1), P * first : P * last]
-            nc.sync.dma_start(raw[:], rows.rearrange("(p i) c -> p i c", i=PACK))
+            queue = nc.scalar if (g, a) == (0, 0) else nc.sync
+            queue.dma_start(raw[:], rows.rearrange("(p i) c -> p i c", i=PACK))
             return raw
 
         def load_w1(g):
@@ -119,7 +120,7 @@ def tile_list_cousin_matcher_kernel(
         nc.sync.dma_start(gain_rows[0:PACK, :], gain[0:K_PASS].rearrange("(s p) -> s p", p=P))
         load_table(0, T // 4, T)
         w1_raw = [[load_w1_pass(0, 0)]]
-        load_table(1, 0, T // 4)
+        load_table(1, 0, 3 * T // 8)
         v_spread = keep.tile([P, S], U8, name="v_spread", align_bytes=64)
         nc.vector.tensor_copy(v_spread[:], tab_plane[:].indirect(idx[:]))
         pages.append(reused.tile([P, T2], F32, name="page1", offset=0))
@@ -127,7 +128,7 @@ def tile_list_cousin_matcher_kernel(
         minus_one = reused.tile([P, M], F32, name="minus_one", offset=4 * T2)
         nc.vector.memset(minus_one[:], -1.0)
         move_scale_rows(0)
-        load_table(1, T // 4, T - HALF)
+        load_table(1, 3 * T // 8, T - HALF)
         move_scale_rows(1)
         load_table(1, T - HALF, T)
         w1_raw[0].append(load_w1_pass(0, 1))

@@ -106,8 +106,14 @@ def tile_list_cousin_matcher_kernel(
             else:
                 raw = keep.tile(shape, F32, name="w1_raw", tag="raw%d_%d" % (g, a))
             rows = w1[K_PASS * a : K_PASS * (a + 1), P * first : P * last]
-            queue = nc.scalar if (g, a) == (0, 0) else nc.sync
-            queue.dma_start(raw[:], rows.rearrange("(p i) c -> p i c", i=PACK))
+            dealt = rows.rearrange("(p i) c -> p i c", i=PACK)
+            if (g, a) == (0, 0):
+                nc.scalar.dma_start(raw[:], dealt)
+            elif (g, a) == (0, 1):
+                nc.scalar.dma_start(raw[:, 0:2, :], dealt[:, 0:2, :])
+                nc.sync.dma_start(raw[:, 2:, :], dealt[:, 2:, :])
+            else:
+                nc.sync.dma_start(raw[:], dealt)
             return raw
 
         def load_w1(g):

@@ -31,8 +31,11 @@ PAGES = 2
 W1_GROUPS = ((0, 1), (1, 2), (2, 4), (4, 8))
 BANKS = 8
 BANK_BYTES = 2048
-ROWS_AT = 4 * HALF
-ROW_AT = (ROWS_AT + 2 * CHUNK + 32, ROWS_AT, ROWS_AT + 2 * CHUNK, ROWS_AT)
+ROW_BYTES = 2 * CHUNK
+ROW_AT = (992, 1536, 1856, 1056)
+PLANE_AT = 1600
+ROUNDED_AT = 1472
+LATE_AT = 2464
 FIRST_PIECES = ((0, CHUNK), (CHUNK, CHUNK), (HALF, HALF))
 
 
@@ -216,10 +219,12 @@ def tile_list_cousin_matcher_kernel(
 
         def prepare_first_w1(a):
             rounded = keep.tile([P, P, PACK], BF16, name="w1_rounded_first", tag="first%d" % a, align_bytes=64)
-            nc.scalar.copy(
-                rounded[:].rearrange("p (c j) i -> p c i j", j=PACK),
-                w1_raw[0][a][:].rearrange("p i (c j) -> p c i j", j=PACK),
-            )
+            step = PACK if a == 0 else 2
+            for i in range(0, PACK, step):
+                nc.scalar.copy(
+                    rounded[:, :, i : i + step].rearrange("p (c j) i -> p c i j", j=PACK),
+                    w1_raw[0][a][:, i : i + step, :].rearrange("p i (c j) -> p c i j", j=PACK),
+                )
             nc.vector.quantize_mx(
                 out=w1_codes[:, 0, P * a : P * (a + 1)].bitcast(FP8X4),
                 scales=w1_plane[:, 0, P * a : P * (a + 1)],
@@ -297,19 +302,16 @@ def tile_list_cousin_matcher_kernel(
 
         z_turned = [keep.tile([P, PACK, K_PASS], BF16, name="z_turned%d" % half) for half in range(2)]
         z_rows = [keep.tile([P, PACK - 1, CHUNK], BF16, name="z_rows%d" % c) for c in range(CHUNKS)]
-        z_mx = [[], []]
+        z_mx = {}
 
-        def quantise_z(a, rounded, held=False):
-            width = rounded.shape[1]
-            if held:
-                codes = keep.tile([P, width], U32, name="z_codes_held", tag="held_codes", align_bytes=64)
-            else:
-                codes = keep.tile([P, width], U32, name="z_codes%d" % a, bufs=2, align_bytes=64)
-            plane = keep.tile([P, width], U8, name="z_plane%d" % a, bufs=M // width, align_bytes=64)
-            nc.vector.quantize_mx(
-                out=codes[:].bitcast(FP8X4), scales=plane[:], in_=rounded[:].rearrange("p m t -> p (m t)")
-            )
-            z_mx[a].extend((codes[:, c0 : c0 + CHUNK], plane[:, c0 : c0 + CHUNK]) for c0 in range(0, width, CHUNK))
+        def mx_tiles(name, width):
+            codes = keep.tile([P, width], U32, name="z_codes_" + name, align_bytes=64)
+            plane = keep.tile([P, width], U8, name="z_plane_" + name, align_bytes=64)
+            return codes[:], plane[:]
+
+        def quantise_z(a, m0, rounded, codes, plane):
+            nc.vector.quantize_mx(out=codes.bitcast(FP8X4), scales=plane, in_=rounded.rearrange("p m t -> p (m t)"))
+            z_mx[a, m0] = (codes, plane)
 
         def add_turned(target, term, first, start, stop):
             for b in range(PACK):
@@ -352,7 +354,7 @@ def tile_list_cousin_matcher_kernel(
                     nc.scalar.activation(z_turned[half][:, :, P * s : P * (s + 1)], neg_z[:], ACT.Copy, scale=-1.0)
                 else:
                     if (s, half) == (LAST - 1, 1):
-                        rounded = tail.tile([P, PACK, P], BF16, name="z_half_last", offset=ROWS_AT - 32)
+                        rounded = tail.tile([P, PACK, P], BF16, name="z_half_last", offset=ROUNDED_AT)
                     else:
                         rounded = keep.tile([P, PACK, P], BF16, name="z_half", bufs=2)
                     nc.scalar.activation(rounded[:], neg_z[:], ACT.Copy, scale=-1.0)
@@ -380,24 +382,22 @@ def tile_list_cousin_matcher_kernel(
                 nc.scalar.copy(target.rearrange("p (b m) h -> p b m h", b=2), back[:].rearrange("p b h m -> p b m h"))
             return z_plain
 
-        def multiply(y, a, c, pair):
-            codes, plane = z_mx[a][c]
-            for b in range(2):
-                n0 = P * (2 * pair + b)
-                nc.tensor.matmul_mx(
-                    out=y[:, b, :],
-                    lhsT=w2_codes[:, a, 2 * n0 : 2 * (n0 + P)].bitcast(FP4X4),
-                    lhsT_scale=w2_plane[:, a, n0 : n0 + P],
-                    rhs=codes.bitcast(FP8X4),
-                    rhs_scale=plane,
-                    start=(a == 0 and b == 0),
-                    stop=(a == 1 and b == 1),
-                )
+        def multiply(a, m0, b, start, stop):
+            codes, plane = z_mx[a, m0]
+            first = m0 % HALF
+            nc.tensor.matmul_mx(
+                out=score_banks[m0 // HALF, b][:, first : first + codes.shape[1]],
+                lhsT=w2_codes[:, a, 2 * P * b : 2 * P * (b + 1)].bitcast(FP4X4),
+                lhsT_scale=w2_plane[:, a, P * b : P * (b + 1)],
+                rhs=codes.bitcast(FP8X4),
+                rhs_scale=plane,
+                start=start,
+                stop=stop,
+            )
 
-        def open_scores(bank, c, pair):
-            y = bank_tile(bank, [P, 2, CHUNK])
-            multiply(y, 0, c, pair)
-            score_banks[c, pair] = y
+        def open_scores(bank, half, b):
+            score_banks[half, b] = bank_tile(bank, [P, HALF])
+            multiply(0, HALF * half, b, True, False)
 
         score_banks = {}
         negate_ev(0)
@@ -413,33 +413,33 @@ def tile_list_cousin_matcher_kernel(
             if s == 0:
                 prepare_w1(3)
             if s == PACK - 1:
-                quantise_z(0, finish_plain(0))
+                quantise_z(0, 0, finish_plain(0)[:], *mx_tiles("early", HALF))
             if s == PACK:
                 second_half = finish_plain(1)
             if s == LAST - 1:
-                quantise_z(0, second_half, held=True)
+                codes = keep.tile([P, CHUNK], U32, name="z_codes_held", tag="held_codes", align_bytes=64)
+                plane = keep.tile([P, CHUNK], U8, name="z_plane_held", align_bytes=64)
+                quantise_z(0, HALF, second_half[:, 0:CHUNK, :], codes[:], plane[:])
             if s + 1 < LAST:
                 negate_ev(s + 1)
             if s + 3 < SLICES:
                 ready[s + 3] = activations(s + 3)
             if s + 3 == LAST:
                 early_banks = [ring.pop(0) for n in range(PACK)]
-                for n, bank in enumerate(early_banks):
-                    open_scores(bank, n // 2, n % 2)
+                for b, bank in enumerate(early_banks):
+                    open_scores(bank, 0, b)
 
-        def close_scores(c):
-            cols = slice(CHUNK * c, CHUNK * (c + 1))
-            for pair in range(2):
-                y = score_banks[c, pair]
-                multiply(y, 1, c, pair)
-                step = 1 if (c, pair) == (CHUNKS - 1, 1) else 2
-                for b in range(0, 2, step):
-                    first = 2 * pair + b
-                    result = results[c // 2][:, c % 2, first : first + step, :]
-                    nc.vector.tensor_tensor(result, y[:, b : b + step, :], res_rows[:, first : first + step, cols], ALU.add)
-                    rows = out[P * first : P * (first + step), cols]
-                    queue = nc.scalar if c > 0 and (pair, b) == (1, 0) else nc.sync
-                    queue.dma_start(rows.rearrange("(b p) m -> p b m", p=P), result)
+        def store_scores(half, b):
+            cols = slice(HALF * half, HALF * (half + 1))
+            result = results[half][:, b, :]
+            nc.vector.tensor_tensor(result, score_banks[half, b][:], res_rows[:, b, cols], ALU.add)
+            queue = nc.scalar if b % 2 == 1 else nc.sync
+            queue.dma_start(out[P * b : P * (b + 1), cols], result)
+
+        def last_pass_early(c):
+            quantise_z(1, CHUNK * c, z_woven[c], *mx_tiles("chunk%d" % c, CHUNK))
+            for b in range(N // P):
+                multiply(1, CHUNK * c, b, False, c == 1)
 
         def weave_early(c):
             target = woven[:, CHUNK * c : CHUNK * (c + 1), 0 : PACK - 1]
@@ -448,15 +448,15 @@ def tile_list_cousin_matcher_kernel(
             )
 
         def finish_last(c, x1, x2):
-            row = tail.tile([P, CHUNK], BF16, name="z_row%d" % c, offset=ROW_AT[c])
-            nc.vector.tensor_tensor(row[:], x1, x2, ALU.min)
+            row = tail.tile([P, CHUNK], BF16, name="z_row%d" % c, offset=ROW_AT[c])[:]
+            nc.vector.tensor_tensor(row, x1, x2, ALU.min)
             z_woven = woven[:, CHUNK * c : CHUNK * (c + 1), :]
-            nc.scalar.copy(z_woven[:, :, PACK - 1], row[:])
+            nc.scalar.copy(z_woven[:, :, PACK - 1], row)
             return z_woven
 
-        results = [keep.tile([P, 2, N // P, CHUNK], F32, name="results", tag="raw3_%d" % n) for n in range(2)]
-        for n, bank in enumerate(ring[0:1] + ring[2:]):
-            open_scores(bank, 2 + n // 2, n % 2)
+        results = [keep.tile([P, N // P, HALF], F32, name="results", tag="raw3_%d" % n) for n in range(2)]
+        for b, bank in enumerate(ring[0:1] + ring[2:]):
+            open_scores(bank, 1, b)
         woven = keep.tile([P, M, PACK], BF16, name="z_woven", tag="tab1", align_bytes=64)
         for c in range(CHUNKS):
             weave_early(c)
@@ -474,17 +474,30 @@ def tile_list_cousin_matcher_kernel(
             finish_last(c, x1_early[:, CHUNK * c : CHUNK * (c + 1)], x2_early[:, CHUNK * c : CHUNK * (c + 1)])
             for c in range(2)
         ]
-        x1_late = fetch_last(idx3, HALF, tail.tile([P, HALF], F32, name="x1_late", offset=0))
-        quantise_z(1, z_woven[0])
-        x2_held = tail.tile([P, CHUNK], F32, name="x2_held", offset=ROWS_AT + 4 * CHUNK)
+        x1_late = fetch_last(idx3, HALF, tail.tile([P, HALF], F32, name="x1_late", offset=LATE_AT))
+        last_pass_early(0)
+        x2_held = tail.tile([P, CHUNK], F32, name="x2_held", offset=0)
         fetch_last(idx4, M - CHUNK, x2_held)
+        last_pass_early(1)
         z_woven.append(finish_last(2, x1_late[:, 0:CHUNK], x2_third[:]))
-        quantise_z(1, z_woven[1])
         z_woven.append(finish_last(3, x1_late[:, CHUNK:], x2_held[:]))
-        for c in range(2, CHUNKS):
-            close_scores(c - 2)
-            if c == 2:
-                open_scores(early_banks[0], CHUNKS - 1, 1)
-            quantise_z(1, z_woven[c])
-        for c in range(2, CHUNKS):
-            close_scores(c)
+        codes = keep.tile([P, CHUNK], U32, name="z_codes_filler", align_bytes=64)
+        plane = tail.tile([P, CHUNK], U8, name="z_plane_filler", offset=PLANE_AT, align_bytes=64)
+        quantise_z(0, M - CHUNK, second_half[:, CHUNK:, :], codes[:], plane[:])
+        for b in range(N // P - 1):
+            multiply(0, M - CHUNK, b, False, False)
+        store_scores(0, 0)
+        open_scores(early_banks[0], 1, N // P - 1)
+        multiply(0, M - CHUNK, N // P - 1, False, False)
+        store_scores(0, 1)
+        codes, plane = mx_tiles("late", HALF)
+        for c in range(2):
+            cols = slice(CHUNK * c, CHUNK * (c + 1))
+            quantise_z(1, HALF, z_woven[2 + c], codes[:, cols], plane[:, cols])
+        z_mx[1, HALF] = (codes, plane)
+        for b in range(N // P):
+            multiply(1, HALF, b, False, True)
+        store_scores(0, 2)
+        store_scores(0, 3)
+        for b in range(N // P):
+            store_scores(1, b)

@@ -242,7 +242,7 @@ def tile_list_cousin_matcher_kernel(
             elif s == 3:
                 sigmoid = keep.tile([P, S], F32, name="sigmoid_held", tag="raw3_1")
             else:
-                sigmoid = keep.tile([P, S], F32, name="sigmoid", bufs=2)
+                sigmoid = keep.tile([P, S], F32, name="sigmoid", bufs=2, align_bytes=64)
             for j0, count in FIRST_PIECES if s == 0 else ((0, HALF), (HALF, HALF)):
                 cols = slice(j0, j0 + count)
                 e_bank = work_bank([P, count])
@@ -323,12 +323,11 @@ def tile_list_cousin_matcher_kernel(
         def fetch_first(s):
             if s == 0:
                 neg_x1 = shared.tile([P, M], F32, name="neg_x1_first", offset=4 * S)
+            elif s == LAST - 1:
+                neg_x1 = keep.tile([P, M], F32, name="neg_x1_last")
             else:
                 neg_x1 = keep.tile([P, M], F32, name="neg_x1", bufs=2)
-            piece = HALF if s == LAST - 1 else M
-            for m0 in range(0, M, piece):
-                window = pages[s % PAGES][:].indirect(entries(idx3, m0, piece))
-                nc.vector.tensor_tensor(neg_x1[:, m0 : m0 + piece], window, minus_one[:, 0:piece], ALU.mult)
+            nc.vector.tensor_tensor(neg_x1[:], pages[s % PAGES][:].indirect(idx3[:]), minus_one[:], ALU.mult)
             return neg_x1
 
         def fetch_second(s, neg_x1):
@@ -337,10 +336,7 @@ def tile_list_cousin_matcher_kernel(
             else:
                 d = keep.tile([P, M], F32, name="difference_early")
             r = late.tile([P, M], F32, name="excess%d" % s, offset=4 * M)
-            piece = HALF if s == LAST - 1 else M
-            for m0 in range(0, M, piece):
-                window = pages[s % PAGES][:].indirect(entries(idx4, m0, piece))
-                nc.vector.tensor_tensor(d[:, m0 : m0 + piece], window, neg_x1[:, m0 : m0 + piece], ALU.add)
+            nc.vector.tensor_tensor(d[:], pages[s % PAGES][:].indirect(idx4[:]), neg_x1[:], ALU.add)
             sums = [work_bank([P, PACK, P]) for half in range(2)]
             for half, neg_z in enumerate(sums):
                 add_turned(neg_z, evs[s], HALF * half, True, False)
@@ -404,6 +400,11 @@ def tile_list_cousin_matcher_kernel(
         for s in range(LAST):
             neg_x1 = fetch_first(s)
             if s == LAST - 1:
+                codes = keep.tile([P, HALF], U32, name="z_codes_early", tag="sigmoid", bufs=2, align_bytes=64)
+                plane = keep.tile([P, HALF], U8, name="z_plane_early", align_bytes=64)
+                quantise_z(0, 0, first_half[:], codes[:], plane[:])
+                for b, bank in enumerate(early_banks):
+                    open_scores(bank, 0, b)
                 fetch_second(s, neg_x1)
             scatter(s + 1, 0, *ready[s + 1])
             if s < LAST - 1:
@@ -413,7 +414,7 @@ def tile_list_cousin_matcher_kernel(
             if s == 0:
                 prepare_w1(3)
             if s == PACK - 1:
-                quantise_z(0, 0, finish_plain(0)[:], *mx_tiles("early", HALF))
+                first_half = finish_plain(0)
             if s == PACK:
                 second_half = finish_plain(1)
             if s == LAST - 1:
@@ -426,8 +427,6 @@ def tile_list_cousin_matcher_kernel(
                 ready[s + 3] = activations(s + 3)
             if s + 3 == LAST:
                 early_banks = [ring.pop(0) for n in range(PACK)]
-                for b, bank in enumerate(early_banks):
-                    open_scores(bank, 0, b)
 
         def store_scores(half, b):
             cols = slice(HALF * half, HALF * (half + 1))

from contextlib import ExitStack

import concourse.mybir as mybir
from concourse.masks import make_identity

K, T, S, H, T2, M, N = 1024, 4096, 1024, 1024, 2048, 1024, 512
FLOPS = 2 * K * H * S + 2 * H * N * M

F32 = mybir.dt.float32
BF16 = mybir.dt.bfloat16
I32 = mybir.dt.int32
U32 = mybir.dt.uint32
U16 = mybir.dt.uint16
U8 = mybir.dt.uint8
FP8X4 = mybir.dt.float8_e4m3fn_x4
FP4X4 = mybir.dt.float4_e2m1fn_x4
ALU = mybir.AluOpType
ACT = mybir.ActivationFunctionType

P = 128
QUADRANT = 32
PACK = 4
K_PASS = P * PACK
HALF = 512
CHUNK = 256
STRIPE = 16
SLICES = H // P
CHUNKS = M // CHUNK
LAST = SLICES - 1
PAGES = 2
W1_GROUPS = ((0, 1), (1, 2), (2, 4), (4, 8))
BANKS = 8
BANK_BYTES = 2048
ROW_BYTES = 2 * CHUNK
ROW_AT = (992, 1536, 1856, 1056)
PLANE_AT = 1600
ROUNDED_AT = 1472
LATE_AT = 2464
FIRST_PIECES = ((0, CHUNK), (CHUNK, CHUNK), (HALF, HALF))


def tile_list_cousin_matcher_kernel(
    tc, tab_words, tab_scales, offs, w1, gain, wgs, offs2, offs3, offs4, ev, w2_words, w2_scales, res, out
):
    nc = tc.nc

    with ExitStack() as ctx:
        lists = ctx.enter_context(tc.tile_pool(name="lists", bufs=1))
        keep = ctx.enter_context(tc.tile_pool(name="keep", bufs=1))
        shared = ctx.enter_context(tc.tile_pool(name="shared", bufs=1))
        reused = ctx.enter_context(tc.tile_pool(name="reused", bufs=1))
        late = ctx.enter_context(tc.tile_pool(name="late", bufs=1))
        tail = ctx.enter_context(tc.tile_pool(name="tail", bufs=1))
        psum = ctx.enter_context(tc.psum_pool(name="psum", bufs=1))

        def entries(list_tile, first, count):
            return list_tile[:, first // STRIPE : (first + count) // STRIPE]

        ring = list(range(BANKS))

        def bank_tile(bank, shape, dtype=F32):
            return psum.tile(shape, dtype, name="bank%d" % bank, offset=BANK_BYTES * bank)

        def work_bank(shape, dtype=F32):
            ring.append(ring.pop(0))
            return bank_tile(ring[-1], shape, dtype)

        warm = keep.tile([P, 1], F32, name="warm")
        nc.vector.memset(warm[:], 0.0)
        nc.scalar.activation(warm[:], warm[:], ACT.Sigmoid)

        tab_plane = reused.tile([P, T], U8, name="tab_plane", offset=4 * T2 - T // 2)
        nc.gpsimd.memset(tab_plane[:].bitcast(I32), 0)
        v_plane = keep.tile([P, S], U8, name="v_plane", align_bytes=64)
        nc.vector.memset(v_plane[:].bitcast(I32), 0)
        gain_rows = keep.tile([P, P], F32, name="gain_rows")
        nc.vector.memset(gain_rows[:], 0.0)
        w2_plane = keep.tile([P, 2, N], U8, name="w2_plane", align_bytes=64)
        nc.vector.memset(w2_plane[:].rearrange("p a c -> p (a c)").bitcast(I32), 0)
        ident = keep.tile([P, P], F32, name="ident")
        make_identity(nc, ident[:])
        ident_bf16 = keep.tile([P, P], BF16, name="ident_bf16")
        make_identity(nc, ident_bf16[:])
        pages = [keep.tile([P, T2], F32, name="page0")]
        nc.vector.memset(pages[0][:], 0.0)

        idx = lists.tile([P, S // STRIPE], U16, name="idx")
        idx2 = lists.tile([P, S // STRIPE], U16, name="idx2")
        idx3 = lists.tile([P, M // STRIPE], U16, name="idx3")
        idx4 = lists.tile([P, M // STRIPE], U16, name="idx4")

        def load_table(a, first, last):
            source = tab_words[a].rearrange("p t i -> p (t i)").bitcast(I32)
            nc.sync.dma_start(tabs[a][:, first:last], source[:, first:last])

        def move_scale_rows(a):
            for q in range(P // QUADRANT):
                first = P // 2 * a + PACK * PACK * q
                nc.sync.dma_start(
                    v_plane[QUADRANT * q + PACK * a : QUADRANT * q + PACK * (a + 1), :].bitcast(I32),
                    v_spread[first : first + PACK * PACK : PACK, :].bitcast(I32),
                )

        def load_w1_pass(g, a):
            first, last = W1_GROUPS[g]
            shape = [P, PACK, P * (last - first)]
            if (g, a) == (2, 1):
                raw = shared.tile(shape, F32, name="w1_raw_held", offset=2 * S)
            else:
                raw = keep.tile(shape, F32, name="w1_raw", tag="raw%d_%d" % (g, a))
            rows = w1[K_PASS * a : K_PASS * (a + 1), P * first : P * last]
            dealt = rows.rearrange("(p i) c -> p i c", i=PACK)
            if (g, a) == (0, 0):
                nc.scalar.dma_start(raw[:], dealt)
            elif (g, a) == (0, 1):
                nc.scalar.dma_start(raw[:, 0:2, :], dealt[:, 0:2, :])
                nc.sync.dma_start(raw[:, 2:, :], dealt[:, 2:, :])
            else:
                nc.sync.dma_start(raw[:], dealt)
            return raw

        def load_w1(g):
            return [load_w1_pass(g, a) for a in range(2)]

        tabs = [keep.tile([P, T], I32, name="tab", tag="tab%d" % a, align_bytes=64) for a in range(2)]
        load_table(0, 0, T // 4)
        nc.sync.dma_start(idx[:], offs)
        nc.sync.dma_start(tab_plane[0:P:PACK, :].bitcast(I32), tab_scales.rearrange("a q t -> (a q) t").bitcast(I32))
        nc.sync.dma_start(gain_rows[0:PACK, :], gain[0:K_PASS].rearrange("(s p) -> s p", p=P))
        load_table(0, T // 4, T)
        w1_raw = [[load_w1_pass(0, 0)]]
        load_table(1, 0, 3 * T // 8)
        v_spread = keep.tile([P, S], U8, name="v_spread", align_bytes=64)
        nc.vector.tensor_copy(v_spread[:], tab_plane[:].indirect(idx[:]))
        pages.append(reused.tile([P, T2], F32, name="page1", offset=0))
        nc.vector.memset(pages[1][:], 0.0)
        minus_one = reused.tile([P, M], F32, name="minus_one", offset=4 * T2)
        nc.vector.memset(minus_one[:], -1.0)
        move_scale_rows(0)
        load_table(1, 3 * T // 8, T - HALF)
        move_scale_rows(1)
        load_table(1, T - HALF, T)
        w1_raw[0].append(load_w1_pass(0, 1))
        wgs_rows = keep.tile([P, S], F32, name="wgs_rows")
        nc.sync.dma_start(wgs_rows[:, 0:HALF], wgs[:, 0:HALF])
        nc.sync.dma_start(idx2[:], offs2)
        w1_raw.append(load_w1(1))
        nc.sync.dma_start(wgs_rows[:, HALF:], wgs[:, HALF:])
        w1_raw.append(load_w1(2))
        nc.sync.dma_start(idx3[:], offs3)
        nc.sync.dma_start(idx4[:], offs4)

        def load_ev(s):
            rows = keep.tile([P, M], F32, name="ev_rows", bufs=PACK)
            if s < PACK:
                nc.sync.dma_start(rows[:], ev[P * s : P * (s + 1), :])
            else:
                nc.sync.dma_start(rows[:], ev[K_PASS:, :].rearrange("(p t) m -> p t m", t=PACK)[:, s - PACK, :])
            return rows

        def load_wgs_woven(pair):
            rows = keep.tile([P, 2, S], F32, name="wgs_woven%d" % pair)
            source = wgs.rearrange("(p t) j -> p t j", t=PACK)[:, 2 * pair : 2 * pair + 2, :]
            for q in range(P // QUADRANT):
                nc.sync.dma_start(rows[QUADRANT * q : QUADRANT * (q + 1), :, :], source)
            return [rows[:, 0, :], rows[:, 1, :]]

        w1_raw.append(load_w1(3))
        evs = [load_ev(0)]
        gain_woven = keep.tile([P, PACK], F32, name="gain_woven")
        nc.sync.dma_start(gain_woven[:], gain[K_PASS:].rearrange("(p t) -> p t", t=PACK))
        evs.append(load_ev(1))
        wgs_woven = load_wgs_woven(0)
        evs.extend(load_ev(s) for s in range(2, PACK))
        wgs_woven.extend(load_wgs_woven(1))
        w2_codes = keep.tile([P, 2, 2 * N], U8, name="w2_codes", align_bytes=64)
        nc.sync.dma_start(w2_codes[:].bitcast(I32), w2_words.rearrange("a p c -> p a c").bitcast(I32))
        for q in range(P // QUADRANT):
            nc.sync.dma_start(
                w2_plane[QUADRANT * q : QUADRANT * q + PACK, :, :].bitcast(I32),
                w2_scales[:, PACK * q : PACK * (q + 1), :].rearrange("a r c -> r a c").bitcast(I32),
            )

        v_first = keep.tile([P, S], U32, name="v_codes0", align_bytes=64)
        nc.vector.tensor_copy(v_first[:], tabs[0][:].bitcast(U32).indirect(idx[:]))
        v_codes = {(0, j0): v_first[:, j0 : j0 + HALF] for j0 in range(0, S, HALF)}
        res_rows = keep.tile([P, N // P, M], F32, name="res_rows", tag="tab0", align_bytes=64)
        nc.sync.dma_start(res_rows[:], res.rearrange("(b p) m -> p b m", p=P))

        gain_bank = work_bank([P, HALF])
        nc.tensor.transpose(gain_bank[:, 0:P], gain_rows[:], ident[:])
        gain_plain = keep.tile([P, PACK], F32, name="gain_plain")
        nc.scalar.copy(gain_plain[:], gain_bank[:, 0:PACK])

        w1_codes = keep.tile([P, SLICES, 2 * P], U32, name="w1_codes", align_bytes=64)
        w1_plane = keep.tile([P, SLICES, 2 * P], U8, name="w1_plane", align_bytes=64)

        def prepare_w1(g):
            first, last = W1_GROUPS[g]
            rounded = keep.tile(
                [P, last - first, 2, P, PACK], BF16, name="w1_rounded", tag="rounded%d" % (g % 2), align_bytes=64
            )
            for a in range(2):
                if first < PACK:
                    nc.scalar.copy(
                        rounded[:, :, a, :, :].rearrange("p s (c j) i -> p s c i j", j=PACK),
                        w1_raw[g][a][:].rearrange("p i (s c j) -> p s c i j", s=last - first, j=PACK),
                    )
                else:
                    nc.scalar.copy(
                        rounded[:, :, a, :, :].rearrange("p t c i -> p c t i"),
                        w1_raw[g][a][:].rearrange("p i (c t) -> p c t i", t=PACK),
                    )
            nc.vector.quantize_mx(
                out=w1_codes[:, first:last, :].rearrange("p s c -> p (s c)").bitcast(FP8X4),
                scales=w1_plane[:, first:last, :].rearrange("p s c -> p (s c)"),
                in_=rounded[:].rearrange("p s a c i -> p (s a c i)"),
            )

        def prepare_first_w1(a):
            rounded = keep.tile([P, P, PACK], BF16, name="w1_rounded_first", tag="first%d" % a, align_bytes=64)
            step = PACK if a == 0 else 2
            for i in range(0, PACK, step):
                nc.scalar.copy(
                    rounded[:, :, i : i + step].rearrange("p (c j) i -> p c i j", j=PACK),
                    w1_raw[0][a][:, i : i + step, :].rearrange("p i (c j) -> p c i j", j=PACK),
                )
            nc.vector.quantize_mx(
                out=w1_codes[:, 0, P * a : P * (a + 1)].bitcast(FP8X4),
                scales=w1_plane[:, 0, P * a : P * (a + 1)],
                in_=rounded[:].rearrange("p c i -> p (c i)"),
            )

        def gather_second_pass(j0, tag):
            words = keep.tile([P, HALF], U32, name="v_codes1", tag=tag, align_bytes=64)
            nc.vector.tensor_copy(words[:], tabs[1][:].bitcast(U32).indirect(entries(idx, j0, HALF)))
            v_codes[1, j0] = words[:]

        def sigmoid_of(s):
            if s == 1:
                sigmoid = shared.tile([P, S], F32, name="sigmoid_first", offset=0)
            elif s == 3:
                sigmoid = keep.tile([P, S], F32, name="sigmoid_held", tag="raw3_1")
            else:
                sigmoid = keep.tile([P, S], F32, name="sigmoid", bufs=2, align_bytes=64)
            for j0, count in FIRST_PIECES if s == 0 else ((0, HALF), (HALF, HALF)):
                cols = slice(j0, j0 + count)
                e_bank = work_bank([P, count])
                for a in range(2):
                    nc.tensor.matmul_mx(
                        out=e_bank[:],
                        lhsT=w1_codes[:, s, P * a : P * (a + 1)].bitcast(FP8X4),
                        lhsT_scale=w1_plane[:, s, P * a : P * (a + 1)],
                        rhs=v_codes[a, j0 - j0 % HALF][:, j0 % HALF : j0 % HALF + count].bitcast(FP8X4),
                        rhs_scale=v_plane[PACK * a :, cols],
                        start=(a == 0),
                        stop=(a == 1),
                    )
                nc.scalar.activation(sigmoid[:, cols], e_bank[:], ACT.Sigmoid)
            return sigmoid

        def activations(s):
            edge = 4 * M * (1 + (s - 1) % 2)
            column = late.tile([P, 16], F32, name="gain_column%d" % s, offset=edge - 32)[:, 0:1]
            if s < PACK:
                weights = wgs_rows[:]
                nc.scalar.copy(column, gain_plain[:, s : s + 1])
            else:
                weights = wgs_woven[s - PACK]
                nc.scalar.copy(column, gain_woven[:, s - PACK : s - PACK + 1])
            h = sigmoid_of(s)
            for j0 in range(0, S, HALF):
                if (s, j0) == (LAST, HALF):
                    column = keep.tile([P, 1], F32, name="gain_column_last", tag="held_codes", align_bytes=64)[:]
                    nc.scalar.copy(column, gain_woven[:, PACK - 1 : PACK])
                nc.scalar.activation(h[:, j0 : j0 + HALF], h[:, j0 : j0 + HALF], ACT.Copy, scale=column)
            return h[:], weights

        def scatter(s, j0, left, right):
            window = pages[s % PAGES][:].indirect(entries(idx2, j0, left.shape[1]))
            nc.vector.tensor_tensor(window, left, right, ALU.mult)

        def first_factor(j0, count, tag):
            factor = keep.tile([P, count], F32, name="factor", tag=tag)
            nc.scalar.activation(factor[:], wgs_rows[:, j0 : j0 + count], ACT.Copy, scale=gain_plain[:, 0:1])
            return factor[:]

        def negate_ev(s):
            nc.scalar.activation(evs[s][:], evs[s][:], ACT.Copy, scale=-1.0)

        prepare_first_w1(0)
        gather_second_pass(0, "v_second")
        prepare_first_w1(1)
        gather_second_pass(HALF, "first1")
        factor = first_factor(0, HALF, "factor")
        sigmoid = sigmoid_of(0)
        scatter(0, 0, sigmoid[:, 0:HALF], factor)
        prepare_w1(1)
        scatter(0, HALF, sigmoid[:, HALF:], first_factor(HALF, HALF, "raw1_0"))
        prepare_w1(2)
        ready = {s: activations(s) for s in (1, 2)}

        z_turned = [keep.tile([P, PACK, K_PASS], BF16, name="z_turned%d" % half) for half in range(2)]
        z_rows = [keep.tile([P, PACK - 1, CHUNK], BF16, name="z_rows%d" % c) for c in range(CHUNKS)]
        z_mx = {}

        def mx_tiles(name, width):
            codes = keep.tile([P, width], U32, name="z_codes_" + name, align_bytes=64)
            plane = keep.tile([P, width], U8, name="z_plane_" + name, align_bytes=64)
            return codes[:], plane[:]

        def quantise_z(a, m0, rounded, codes, plane):
            nc.vector.quantize_mx(out=codes.bitcast(FP8X4), scales=plane, in_=rounded.rearrange("p m t -> p (m t)"))
            z_mx[a, m0] = (codes, plane)

        def add_turned(target, term, first, start, stop):
            for b in range(PACK):
                nc.tensor.matmul(
                    target[:, b, :], term[:, first + P * b : first + P * (b + 1)], ident[:],
                    start=(start and b == 0), stop=(stop and b == PACK - 1), is_transpose=True,
                )

        def fetch_first(s):
            if s == 0:
                neg_x1 = shared.tile([P, M], F32, name="neg_x1_first", offset=4 * S)
            elif s == LAST - 1:
                neg_x1 = keep.tile([P, M], F32, name="neg_x1_last")
            else:
                neg_x1 = keep.tile([P, M], F32, name="neg_x1", bufs=2)
            nc.vector.tensor_tensor(neg_x1[:], pages[s % PAGES][:].indirect(idx3[:]), minus_one[:], ALU.mult)
            return neg_x1

        def fetch_second(s, neg_x1):
            if s < LAST - 1:
                d = late.tile([P, M], F32, name="difference%d" % s, offset=8 * M * (s % 2))
            else:
                d = keep.tile([P, M], F32, name="difference_early")
            r = late.tile([P, M], F32, name="excess%d" % s, offset=4 * M)
            nc.vector.tensor_tensor(d[:], pages[s % PAGES][:].indirect(idx4[:]), neg_x1[:], ALU.add)
            sums = [work_bank([P, PACK, P]) for half in range(2)]
            for half, neg_z in enumerate(sums):
                add_turned(neg_z, evs[s], HALF * half, True, False)
                add_turned(neg_z, neg_x1, HALF * half, False, False)
            for half, neg_z in enumerate(sums):
                cols = slice(HALF * half, HALF * (half + 1))
                nc.scalar.activation(r[:, cols], d[:, cols], ACT.Relu, scale=-1.0)
                add_turned(neg_z, r, HALF * half, False, True)
            for half, neg_z in enumerate(sums):
                if s < PACK:
                    nc.scalar.activation(z_turned[half][:, :, P * s : P * (s + 1)], neg_z[:], ACT.Copy, scale=-1.0)
                else:
                    if (s, half) == (LAST - 1, 1):
                        rounded = tail.tile([P, PACK, P], BF16, name="z_half_last", offset=ROUNDED_AT)
                    else:
                        rounded = keep.tile([P, PACK, P], BF16, name="z_half", bufs=2)
                    nc.scalar.activation(rounded[:], neg_z[:], ACT.Copy, scale=-1.0)
                    blocks = 2 if (s, half) == (LAST - 1, 1) else PACK
                    backs = []
                    for b in range(PACK):
                        if b % blocks == 0:
                            back = work_bank([P, blocks, P], BF16)
                        nc.tensor.transpose(back[:, b % blocks, :], rounded[:, b, :], ident_bf16[:])
                        if b % 2 == 1:
                            backs.append(back[:, b % blocks - 1 : b % blocks + 1, :])
                    for pair in range(2):
                        source = backs[pair].rearrange("p b m -> p (b m)")
                        nc.scalar.copy(z_rows[2 * half + pair][:, s - PACK, :], source)

        def finish_plain(half):
            z_plain = keep.tile([P, HALF, PACK], BF16, name="z_plain", tag="rounded%d" % half, align_bytes=64)
            words = z_turned[half][:].bitcast(F32)
            for pair in range(2):
                back = work_bank([P, 2, 2, P])
                for b in range(2):
                    for h in range(2):
                        nc.tensor.transpose(back[:, b, h, :], words[:, 2 * pair + b, h : 2 * P : 2], ident[:])
                target = z_plain[:, CHUNK * pair : CHUNK * (pair + 1), :].bitcast(F32)
                nc.scalar.copy(target.rearrange("p (b m) h -> p b m h", b=2), back[:].rearrange("p b h m -> p b m h"))
            return z_plain

        def multiply(a, m0, b, start, stop):
            codes, plane = z_mx[a, m0]
            first = m0 % HALF
            nc.tensor.matmul_mx(
                out=score_banks[m0 // HALF, b][:, first : first + codes.shape[1]],
                lhsT=w2_codes[:, a, 2 * P * b : 2 * P * (b + 1)].bitcast(FP4X4),
                lhsT_scale=w2_plane[:, a, P * b : P * (b + 1)],
                rhs=codes.bitcast(FP8X4),
                rhs_scale=plane,
                start=start,
                stop=stop,
            )

        def open_scores(bank, half, b):
            score_banks[half, b] = bank_tile(bank, [P, HALF])
            multiply(0, HALF * half, b, True, False)

        score_banks = {}
        negate_ev(0)
        for s in range(LAST):
            neg_x1 = fetch_first(s)
            if s == LAST - 1:
                codes = keep.tile([P, HALF], U32, name="z_codes_early", tag="sigmoid", bufs=2, align_bytes=64)
                plane = keep.tile([P, HALF], U8, name="z_plane_early", align_bytes=64)
                quantise_z(0, 0, first_half[:], codes[:], plane[:])
                for b, bank in enumerate(early_banks):
                    open_scores(bank, 0, b)
                fetch_second(s, neg_x1)
            scatter(s + 1, 0, *ready[s + 1])
            if s < LAST - 1:
                fetch_second(s, neg_x1)
            if s + PACK < SLICES:
                evs.append(load_ev(s + PACK))
            if s == 0:
                prepare_w1(3)
            if s == PACK - 1:
                first_half = finish_plain(0)
            if s == PACK:
                second_half = finish_plain(1)
            if s == LAST - 1:
                codes = keep.tile([P, CHUNK], U32, name="z_codes_held", tag="held_codes", align_bytes=64)
                plane = keep.tile([P, CHUNK], U8, name="z_plane_held", align_bytes=64)
                quantise_z(0, HALF, second_half[:, 0:CHUNK, :], codes[:], plane[:])
            if s + 1 < LAST:
                negate_ev(s + 1)
            if s + 3 < SLICES:
                ready[s + 3] = activations(s + 3)
            if s + 3 == LAST:
                early_banks = [ring.pop(0) for n in range(PACK)]

        def store_scores(half, b):
            cols = slice(HALF * half, HALF * (half + 1))
            result = results[half][:, b, :]
            nc.vector.tensor_tensor(result, score_banks[half, b][:], res_rows[:, b, cols], ALU.add)
            queue = nc.scalar if b % 2 == 1 else nc.sync
            queue.dma_start(out[P * b : P * (b + 1), cols], result)

        def last_pass_early(c):
            quantise_z(1, CHUNK * c, z_woven[c], *mx_tiles("chunk%d" % c, CHUNK))
            for b in range(N // P):
                multiply(1, CHUNK * c, b, False, c == 1)

        def weave_early(c):
            target = woven[:, CHUNK * c : CHUNK * (c + 1), 0 : PACK - 1]
            nc.scalar.copy(
                target.rearrange("p (m i) t -> p m t i", i=PACK), z_rows[c][:].rearrange("p t (m i) -> p m t i", i=PACK)
            )

        def finish_last(c, x1, x2):
            row = tail.tile([P, CHUNK], BF16, name="z_row%d" % c, offset=ROW_AT[c])[:]
            nc.vector.tensor_tensor(row, x1, x2, ALU.min)
            z_woven = woven[:, CHUNK * c : CHUNK * (c + 1), :]
            nc.scalar.copy(z_woven[:, :, PACK - 1], row)
            return z_woven

        results = [keep.tile([P, N // P, HALF], F32, name="results", tag="raw3_%d" % n) for n in range(2)]
        for b, bank in enumerate(ring[0:1] + ring[2:]):
            open_scores(bank, 1, b)
        woven = keep.tile([P, M, PACK], BF16, name="z_woven", tag="tab1", align_bytes=64)
        for c in range(CHUNKS):
            weave_early(c)

        def fetch_last(list_tile, m0, target):
            count = target.shape[1]
            window = pages[LAST % PAGES][:].indirect(entries(list_tile, m0, count))
            nc.vector.tensor_tensor(target[:], window, evs[LAST][:, m0 : m0 + count], ALU.add)
            return target

        x1_early = fetch_last(idx3, 0, keep.tile([P, HALF], F32, name="x1_early"))
        x2_early = fetch_last(idx4, 0, keep.tile([P, HALF], F32, name="x2_early"))
        x2_third = fetch_last(idx4, HALF, keep.tile([P, CHUNK], F32, name="x2_third"))
        z_woven = [
            finish_last(c, x1_early[:, CHUNK * c : CHUNK * (c + 1)], x2_early[:, CHUNK * c : CHUNK * (c + 1)])
            for c in range(2)
        ]
        x1_late = fetch_last(idx3, HALF, tail.tile([P, HALF], F32, name="x1_late", offset=LATE_AT))
        last_pass_early(0)
        x2_held = tail.tile([P, CHUNK], F32, name="x2_held", offset=0)
        fetch_last(idx4, M - CHUNK, x2_held)
        last_pass_early(1)
        z_woven.append(finish_last(2, x1_late[:, 0:CHUNK], x2_third[:]))
        z_woven.append(finish_last(3, x1_late[:, CHUNK:], x2_held[:]))
        codes = keep.tile([P, CHUNK], U32, name="z_codes_filler", align_bytes=64)
        plane = tail.tile([P, CHUNK], U8, name="z_plane_filler", offset=PLANE_AT, align_bytes=64)
        quantise_z(0, M - CHUNK, second_half[:, CHUNK:, :], codes[:], plane[:])
        for b in range(N // P - 1):
            multiply(0, M - CHUNK, b, False, False)
        store_scores(0, 0)
        open_scores(early_banks[0], 1, N // P - 1)
        multiply(0, M - CHUNK, N // P - 1, False, False)
        store_scores(0, 1)
        codes, plane = mx_tiles("late", HALF)
        for c in range(2):
            cols = slice(CHUNK * c, CHUNK * (c + 1))
            quantise_z(1, HALF, z_woven[2 + c], codes[:, cols], plane[:, cols])
        z_mx[1, HALF] = (codes, plane)
        for b in range(N // P):
            multiply(1, HALF, b, False, True)
        store_scores(0, 2)
        store_scores(0, 3)
        for b in range(N // P):
            store_scores(1, b)
